import numpy as np
import ml_dtypes


def mxq(x, axis, fmt="e4m3"):
    dtype, down = {"e4m3": (ml_dtypes.float8_e4m3fn, 7), "e5m2": (ml_dtypes.float8_e5m2, 14)}[fmt]
    v = np.moveaxis(np.asarray(x, np.float32).astype(ml_dtypes.bfloat16).astype(np.float64), axis, -1)
    blocks = v.reshape(v.shape[:-1] + (-1, 32))
    amax = np.abs(blocks).max(-1, keepdims=True)
    byte = np.maximum(np.where(amax > 0, np.frexp(amax)[1] - 1 + 127, 0) - down, 1)
    scale = np.exp2(byte - 127.0)
    codes = (blocks / scale).astype(np.float32).astype(dtype).astype(np.float64)
    return np.moveaxis((codes * scale).reshape(v.shape), -1, axis)


WIDE = False


def mx_kscale(k):
    if not WIDE:
        return np.ones(k)
    levels = np.array([10, -10, 5, -5, 0])
    if k % 512:
        return np.exp2(np.random.permutation(np.resize(levels, k // 32))).repeat(32)
    a = np.empty((k // 512, 16))
    for p in range(k // 512):
        a[p, :8] = np.random.permutation(np.resize(levels, 8))
        for g in range(8):
            far = levels[np.abs(levels - a[p, g]) >= 10]
            a[p, g + 8] = far[np.random.randint(len(far))]
    return np.exp2(a.ravel()).repeat(32)


BF16 = ml_dtypes.bfloat16


def bf(x):
    return np.asarray(x, np.float32).astype(BF16)


def f64(x):
    return np.asarray(x).astype(np.float64)


E2M1 = np.array([0.0, 0.5, 1.0, 1.5, 2.0, 3.0, 4.0, 6.0, -0.0, -0.5, -1.0, -1.5, -2.0, -3.0, -4.0, -6.0])


def pack_weight(w, fmt):
    k, n = w.shape
    w = f64(bf(w)).reshape(k // 32, 32, n)
    amax = np.abs(w).max(1)
    if fmt == "e4m3":
        byte = np.frexp(amax)[1] - 1 + 127 - 7
    else:
        mant, ex = np.frexp(amax / 6.0)
        byte = np.where(mant > 0.5, ex, ex - 1) + 127
    byte = np.clip(np.where(amax > 0, byte, 1), 1, 254)
    scaled = (w * np.exp2(127.0 - byte)[:, None, :]).reshape(k, n).astype(np.float32)
    by_word = np.ascontiguousarray(scaled.reshape(k // 512, 128, 4, n).transpose(0, 1, 3, 2))
    if fmt == "e4m3":
        words = by_word.astype(ml_dtypes.float8_e4m3fn).view(np.uint8)
    else:
        c = by_word.astype(ml_dtypes.float4_e2m1fn).view(np.uint8) & 0xF
        words = c[..., 0::2] | (c[..., 1::2] << 4)
    return np.ascontiguousarray(words), np.ascontiguousarray(byte.astype(np.uint8).reshape(k // 512, 16, n))


def unpack_weight(words, scales, fmt):
    g, p, n, _ = words.shape
    if fmt == "e4m3":
        vals = np.ascontiguousarray(words).view(ml_dtypes.float8_e4m3fn).astype(np.float64)
    else:
        nib = np.empty((g, p, n, 4), np.uint8)
        nib[..., 0::2] = words & 0xF
        nib[..., 1::2] = words >> 4
        vals = E2M1[nib]
    vals = vals * np.repeat(np.exp2(scales.astype(np.float64) - 127.0), 8, axis=1)[..., None]
    return vals.transpose(0, 1, 3, 2).reshape(g * 512, n)
def pack4(w):
    words, scales = pack_weight(w, "e2m1")
    return words.reshape(words.shape[0], 128, -1), scales


def unpack4(words, scales):
    return unpack_weight(words.reshape(words.shape[0], 128, -1, 2), scales, "e2m1")


P, K, Q, F = 2048, 1024, 512, 1024
DELTA_LO, DELTA_HI = 0.05, 0.45
IPW_LO, IPW_HI = 0.5, 2.0


def draw0():
    s = mx_kscale(K)
    t = mx_kscale(P)
    d = bf(np.random.standard_normal((P, K)) * s)
    v = bf(np.random.standard_normal((K, Q)) / np.sqrt(K) / s[:, None])
    delta = bf(np.random.uniform(DELTA_LO, DELTA_HI, (P, Q)) * t[:, None])
    ipw = bf(np.random.uniform(IPW_LO, IPW_HI, P) / t)
    e_words, e_scales = pack4(np.random.standard_normal((K, F)) / np.sqrt(K) / s[:, None])
    return {"d": d, "v": v, "delta": delta, "ipw": ipw,
            "e_words": e_words, "e_scales": e_scales}


def core(d, v, delta, ipw, e_words, e_scales):
    dq = mxq(f64(d), 1, "e4m3")
    diff = dq @ mxq(f64(v), 0, "e4m3")
    lam = f64(delta) / (1.0 + np.exp(diff))
    h = (dq @ unpack4(e_words, e_scales)) * f64(ipw)[:, None]
    return mxq(lam, 0, "e4m3").T @ mxq(h, 0, "e4m3")


def e4m3fn_bytes(y):
    return np.clip(np.asarray(y, np.float64), -448.0, 448.0).astype(np.float32).astype(ml_dtypes.float8_e4m3fn).view(np.uint8)


def e4m3fn_values(b):
    return np.asarray(b, np.uint8).view(ml_dtypes.float8_e4m3fn).astype(np.float64)


def setup_inputs():
    d = draw0()
    x0 = np.asarray(d['d']).astype(np.float64)
    s = (np.max(np.abs(x0), axis=(0,), keepdims=True) / 448.0).astype(np.float32)
    out = {}
    for k, v in d.items():
        if k == 'd':
            out['d_bytes'] = e4m3fn_bytes(x0 / s.astype(np.float64))
            out['d_scale'] = s
        else:
            out[k] = v
    return out


def reference(d_bytes, d_scale, v, delta, ipw, e_words, e_scales):
    return core(e4m3fn_values(d_bytes) * d_scale.astype(np.float64), v, delta, ipw, e_words, e_scales)

@@ -1,0 +1,287 @@
+from contextlib import ExitStack
+
+import concourse.mybir as mybir
+from concourse.masks import make_identity
+
+F32 = mybir.dt.float32
+BF16 = mybir.dt.bfloat16
+I32 = mybir.dt.int32
+U32 = mybir.dt.uint32
+U8 = mybir.dt.uint8
+FP8 = mybir.dt.float8_e4m3fn
+E4M3X4 = mybir.dt.float8_e4m3fn_x4
+E2M1X4 = mybir.dt.float4_e2m1fn_x4
+MULT = mybir.AluOpType.mult
+COPY = mybir.ActivationFunctionType.Copy
+SIGMOID = mybir.ActivationFunctionType.Sigmoid
+
+PAIRS, RAW, RANKERS, FEATS = 2048, 1024, 512, 1024
+P = 128
+PACK = 4
+GROUP = P * PACK
+GROUPS = PAIRS // GROUP
+PASSES = RAW // GROUP
+HALVES = FEATS // 512
+TILES = PAIRS // P
+QTILES = RANKERS // P
+
+PROGRAM = """c0 T0 C1 C2 C3 v T1 p0 v x d T2 e p1 p2 d T3 p3 w q w d e w v v t e w q e d e t d w e w t s s e s w t e d d e s i00 w t d h00 l00 d t w e e s d e w i01 l01 t t w s e s h01 L0 w s s e e e e e d t d d t i10 i11 u001 e e l10 s e h10 s l11 d e s t t u000 e e u003 e L1 i20 e d h20 s u100 u103 l20 s d e u101 s l21 e s e h11 e e i21 L2 e u113 u203 h21 u110 I31 u012 l30 i30 L30 u213 l32 u202 u013 u201 h30 u211 L32 u212 u200 l31 u102 u210 h31 u002 L31 l33 u300 u302 u010 u011 o00 u310 o02 u111 u311 u312 o10 u301 L33 u313 O11 O01 u112 o13 O12 u303 O03"""
+
+FLOPS = 2 * PAIRS * RAW * RANKERS + 2 * PAIRS * RAW * FEATS + 2 * RANKERS * PAIRS * FEATS
+
+
+def tile_lambdarank_head_gradient_s11_kernel(tc, d_bytes, d_scale, v, delta, ipw, e_words, e_scales, out):
+    nc = tc.nc
+    with ExitStack() as ctx:
+        keep = ctx.enter_context(tc.tile_pool(name="keep", bufs=1))
+        work = ctx.enter_context(tc.tile_pool(name="work", bufs=3))
+        psum = ctx.enter_context(tc.psum_pool(name="psum", bufs=1))
+
+        ident = keep.tile([P, P], F32, name="ident")
+        make_identity(nc, ident[:])
+
+        ctx.enter_context(tc.manual_schedule())
+
+        scale_kp = keep.tile([P, PASSES, PACK], F32, name="scale_kp")
+        scale_bc = keep.tile([P, RAW], F32, name="scale_bc", align_bytes=64)
+        raw = [keep.tile([P, PACK, RAW], U8, name=f"raw{s}", align_bytes=64) for s in range(GROUPS)]
+        dlt = [keep.tile([P, PACK, RANKERS], BF16, name=f"dlt{s}", align_bytes=64) for s in range(GROUPS)]
+        v_raw = [keep.tile([P, PACK, RANKERS], BF16, name=f"v_raw{g}", align_bytes=64) for g in range(PASSES)]
+        e_w = [keep.tile([P, 2 * FEATS], U8, name=f"e_w{g}", align_bytes=64) for g in range(PASSES)]
+        e_s = keep.tile([P, PASSES, FEATS], U8, name="e_s", align_bytes=64)
+        ipw_bf = keep.tile([P, GROUPS, PACK], BF16, name="ipw_bf")
+        ipw_f = keep.tile([P, GROUPS, PACK], F32, name="ipw_f")
+
+        warm = keep.tile([P, 1], F32, name="warm")
+        nc.vector.memset(warm[:], 0.0)
+        warm_out = keep.tile([P, 1], F32, name="warm_out")
+        nc.scalar.activation(out=warm_out[:], in_=warm[:], func=SIGMOID, scale=-1.0)
+        nc.vector.memset(e_s[:].bitcast(I32), 0)
+
+        d_view = d_bytes.rearrange("(s m t) k -> s m t k", m=P, t=PACK)
+        dlt_view = delta.rearrange("(s m t) q -> s m t q", m=P, t=PACK)
+        v_view = v.rearrange("(g p t) n -> g p t n", p=P, t=PACK)
+        s_view = e_scales.rearrange("g r n -> r g n")
+
+        nc.scalar.dma_start(out=scale_kp[:], in_=d_scale.rearrange("o (g p t) -> p (o g) t", p=P, t=PACK))
+        nc.scalar.dma_start(out=ipw_bf[:], in_=ipw.rearrange("(s m t) -> m s t", m=P, t=PACK))
+        nc.sync.dma_start(out=raw[0][:, 0:1, :], in_=d_view[0][:, 0:1, :])
+        nc.sync.dma_start(out=raw[0][:, 1:4, :], in_=d_view[0][:, 1:4, :])
+        for g in range(PASSES):
+            nc.sync.dma_start(out=e_w[g][:], in_=e_words[g])
+        for quad in range(4):
+            nc.sync.dma_start(out=e_s[32 * quad : 32 * quad + 4].bitcast(I32), in_=s_view[4 * quad : 4 * quad + 4].bitcast(I32))
+        nc.sync.dma_start(out=v_raw[0][:], in_=v_view[0])
+        nc.sync.dma_start(out=scale_bc[:], in_=d_scale.rearrange("o k -> (o k)").partition_broadcast(P))
+        nc.sync.dma_start(out=raw[1][:], in_=d_view[1])
+        nc.sync.dma_start(out=v_raw[1][:], in_=v_view[1])
+        nc.sync.dma_start(out=raw[2][:], in_=d_view[2])
+        nc.sync.dma_start(out=dlt[0][:], in_=dlt_view[0])
+        nc.sync.dma_start(out=raw[3][:], in_=d_view[3])
+        for s in range(1, GROUPS):
+            nc.sync.dma_start(out=dlt[s][:], in_=dlt_view[s])
+
+        v_codes = [keep.tile([P, RANKERS], U32, name=f"v_codes{g}", align_bytes=64) for g in range(PASSES)]
+        v_planes = [keep.tile([P, RANKERS], U8, name=f"v_planes{g}", align_bytes=64) for g in range(PASSES)]
+        v_grp = [keep.tile([P, RANKERS, PACK], BF16, name=f"v_grp{g}", align_bytes=64) for g in range(PASSES)]
+
+        def v_interleave(g, part, parts, copy):
+            cols = slice(RANKERS // parts * part, RANKERS // parts * (part + 1))
+            copy(
+                out=v_grp[g][:, cols, :].rearrange("p (c i) t -> p c t i", i=4),
+                in_=v_raw[g][:, :, cols].rearrange("p t (c i) -> p c t i", i=4),
+            )
+
+        def v_quantize(g):
+            nc.vector.quantize_mx(
+                out=v_codes[g][:].bitcast(E4M3X4), scales=v_planes[g][:], in_=v_grp[g][:].rearrange("p n t -> p (n t)")
+            )
+
+        d_codes = [keep.tile([P, PASSES * P], U32, name=f"d_codes{j}", align_bytes=64) for j in range(TILES)]
+        d_planes = [keep.tile([P, PASSES * P], U8, name=f"d_planes{j}", align_bytes=64) for j in range(TILES)]
+        scaled, turned, grouped = {}, {}, {}
+
+        def widen(j):
+            scaled[j] = work.tile([P, RAW], BF16, name="scaled", bufs=9, align_bytes=64)
+            nc.vector.tensor_tensor(
+                out=scaled[j][:], in0=raw[j // PACK][:, j % PACK, :].bitcast(FP8), in1=scale_bc[:], op=MULT
+            )
+
+        def widen_only(j, copy):
+            scaled[j] = work.tile([P, RAW], BF16, name="scaled", bufs=9, align_bytes=64)
+            copy(out=scaled[j][:], in_=raw[j // PACK][:, j % PACK, :].bitcast(FP8))
+
+        def scale_turned(j):
+            grouped[j] = work.tile([P, PASSES * P * PACK], BF16, name="grouped", align_bytes=64)
+            for g in range(PASSES):
+                nc.vector.tensor_tensor(
+                    out=grouped[j][:, 512 * g : 512 * (g + 1)].rearrange("p (r u e) -> p r u e", u=2, e=2),
+                    in0=turned[j][:, g].bitcast(BF16).rearrange("p u (r e) -> p r u e", e=2),
+                    in1=scale_kp[:, g : g + 1, :].rearrange("p o (u e) -> p o u e", e=2).to_broadcast([P, P, 2, 2]),
+                    op=MULT,
+                )
+
+        def turn(j):
+            turned[j] = psum.tile([P, PASSES, 2, P], F32, name=f"tp{j % 2}")
+            words = scaled[j][:].bitcast(F32)
+            for g in range(PASSES):
+                for u in range(2):
+                    nc.tensor.transpose(turned[j][:, g, u, :], words[:, 256 * g + u : 256 * (g + 1) : 2], ident[:])
+
+        def gather(j):
+            grouped[j] = work.tile([P, PASSES * P * PACK], BF16, name="grouped", align_bytes=64)
+            nc.scalar.copy(
+                out=grouped[j][:].bitcast(F32).rearrange("p (g r u) -> p g r u", g=PASSES, u=2),
+                in_=turned[j][:].rearrange("p g u r -> p g r u"),
+            )
+
+        def d_quantize(j):
+            nc.vector.quantize_mx(out=d_codes[j][:].bitcast(E4M3X4), scales=d_planes[j][:], in_=grouped[j][:])
+
+        diff, encoded = {}, {}
+        sig, h_raw = {}, {}
+
+        def score(j):
+            diff[j] = psum.tile([P, RANKERS], F32, name="mm", bufs=4)
+            for g in range(PASSES):
+                cols = slice(g * P, (g + 1) * P)
+                nc.tensor.matmul_mx(
+                    out=diff[j][:], lhsT=d_codes[j][:, cols].bitcast(E4M3X4), lhsT_scale=d_planes[j][:, cols],
+                    rhs=v_codes[g][:].bitcast(E4M3X4), rhs_scale=v_planes[g][:], start=(g == 0), stop=(g == PASSES - 1),
+                )
+
+        def sigmoid(j):
+            s, t = divmod(j, PACK)
+            if t == 0:
+                sig[s] = work.tile([P, PACK, RANKERS], F32, name="sig", bufs=3, align_bytes=64)
+            nc.scalar.activation(out=sig[s][:, t, :], in_=diff[j][:], func=SIGMOID, scale=-1.0)
+
+        def encode(j, half):
+            encoded[j, half] = psum.tile([P, 512], F32, name="mm", bufs=4)
+            for g in range(PASSES):
+                cols = slice(g * P, (g + 1) * P)
+                nc.tensor.matmul_mx(
+                    out=encoded[j, half][:], lhsT=d_codes[j][:, cols].bitcast(E4M3X4), lhsT_scale=d_planes[j][:, cols],
+                    rhs=e_w[g][:, 1024 * half : 1024 * (half + 1)].bitcast(E2M1X4), rhs_scale=e_s[:, g, 512 * half : 512 * (half + 1)],
+                    start=(g == 0), stop=(g == PASSES - 1),
+                )
+
+        def weigh(j, half):
+            s, t = divmod(j, PACK)
+            if t == 0:
+                h_raw[s, half] = work.tile([P, PACK, 512], BF16, name=f"h_raw{half}", bufs=2, align_bytes=64)
+            nc.scalar.activation(out=h_raw[s, half][:, t, :], in_=encoded[j, half][:], func=COPY, scale=ipw_f[:, s, t : t + 1])
+
+        lam_codes = [keep.tile([P, RANKERS], U32, name=f"lam_codes{s}", align_bytes=64) for s in range(GROUPS)]
+        lam_planes = [keep.tile([P, RANKERS], U8, name=f"lam_planes{s}", align_bytes=64) for s in range(GROUPS)]
+        h_codes = {(s, h): keep.tile([P, 512], U32, name=f"h_codes{s}_{h}", align_bytes=64) for s in range(GROUPS) for h in range(HALVES)}
+        h_planes = {(s, h): keep.tile([P, 512], U8, name=f"h_planes{s}_{h}", align_bytes=64) for s in range(GROUPS) for h in range(HALVES)}
+        lam, h_grp = {}, {}
+
+        def lam_mult(s, part, parts):
+            if part == 0:
+                lam[s] = work.tile([P, RANKERS, PACK], BF16, name="lam", bufs=2, align_bytes=64)
+            cols = slice(RANKERS // parts * part, RANKERS // parts * (part + 1))
+            nc.vector.tensor_tensor(
+                out=lam[s][:, cols, :].rearrange("p (c i) t -> p c t i", i=4),
+                in0=sig[s][:, :, cols].rearrange("p t (c i) -> p c t i", i=4),
+                in1=dlt[s][:, :, cols].rearrange("p t (c i) -> p c t i", i=4),
+                op=MULT,
+            )
+
+        def lam_quantize(s, part, parts):
+            cols = slice(RANKERS // parts * part, RANKERS // parts * (part + 1))
+            nc.vector.quantize_mx(
+                out=lam_codes[s][:, cols].bitcast(E4M3X4), scales=lam_planes[s][:, cols],
+                in_=lam[s][:, cols, :].rearrange("p n t -> p (n t)"),
+            )
+
+        def h_interleave(s, half, copy=nc.vector.tensor_copy):
+            h_grp[s, half] = work.tile([P, 512, PACK], BF16, name="h_grp", bufs=4, align_bytes=64)
+            copy(
+                out=h_grp[s, half][:].rearrange("p (c i) t -> p c t i", i=4),
+                in_=h_raw[s, half][:].rearrange("p t (c i) -> p c t i", i=4),
+            )
+
+        def h_quantize(s, half):
+            nc.vector.quantize_mx(
+                out=h_codes[s, half][:].bitcast(E4M3X4), scales=h_planes[s, half][:],
+                in_=h_grp[s, half][:].rearrange("p n t -> p (n t)"),
+            )
+
+        acc, summed = {}, {}
+        banks = {(0, 0): "acc0", (0, 1): "acc1", (0, 2): "tp0", (0, 3): "tp1", (1, 0): "mm", (1, 1): "mm", (1, 2): "mm", (1, 3): "mm"}
+
+        def update(s, half, m):
+            summed[half, m] = summed.get((half, m), 0) + 1
+            if summed[half, m] == 1:
+                acc[half, m] = psum.tile([P, 512], F32, name=banks[half, m], bufs=4 if half == 1 else 1)
+            cols = slice(m * P, (m + 1) * P)
+            nc.tensor.matmul_mx(
+                out=acc[half, m][:], lhsT=lam_codes[s][:, cols].bitcast(E4M3X4), lhsT_scale=lam_planes[s][:, cols],
+                rhs=h_codes[s, half][:].bitcast(E4M3X4), rhs_scale=h_planes[s, half][:], start=(summed[half, m] == 1), stop=(summed[half, m] == GROUPS),
+            )
+
+        def store(half, m, engine):
+            assert summed[half, m] == GROUPS
+            res = work.tile([P, 512], F32, name="res", bufs=8)
+            if engine == "scalar":
+                nc.scalar.copy(out=res[:], in_=acc[half, m][:])
+            else:
+                nc.vector.tensor_copy(out=res[:], in_=acc[half, m][:])
+            nc.sync.dma_start(out=out[m * P : (m + 1) * P, 512 * half : 512 * (half + 1)], in_=res[:])
+
+        last = GROUPS - 1
+        order = dict(w=list(range(PACK, TILES)), t=list(range(PACK, TILES)), d=list(range(TILES)), s=list(range(TILES)),
+                     e=[(j, h) for j in range(TILES) for h in range(HALVES)], v=[(g, part) for g in range(PASSES) for part in range(2)],
+                     q=list(range(PASSES)))
+
+        def step(token):
+            kind, arg = token[0], [int(x) for x in token[1:]]
+            nxt = order[kind].pop(0) if kind in order else None
+            if kind == "w":
+                widen(nxt)
+            elif kind == "t":
+                turn(nxt)
+                gather(nxt)
+            elif kind == "d":
+                d_quantize(nxt)
+            elif kind == "s":
+                score(nxt)
+                sigmoid(nxt)
+            elif kind == "e":
+                encode(*nxt)
+                weigh(*nxt)
+            elif kind == "v":
+                v_interleave(*nxt, 2, nc.scalar.copy)
+            elif kind == "q":
+                v_quantize(nxt)
+            elif kind == "c":
+                widen_only(arg[0], nc.vector.tensor_copy)
+            elif kind == "C":
+                widen_only(arg[0], nc.scalar.copy)
+            elif kind == "T":
+                turn(arg[0])
+            elif kind == "p":
+                scale_turned(arg[0])
+            elif kind == "l":
+                lam_mult(arg[0], arg[1], 4 if arg[0] == last else 2)
+            elif kind == "L":
+                lam_quantize(arg[0], arg[1] if arg[0] == last else 0, 4 if arg[0] == last else 1)
+            elif kind == "i":
+                h_interleave(*arg)
+            elif kind == "I":
+                h_interleave(*arg, nc.scalar.copy)
+            elif kind == "h":
+                h_quantize(*arg)
+            elif kind == "u":
+                update(*arg)
+            elif kind == "x":
+                nc.vector.tensor_copy(out=ipw_f[:], in_=ipw_bf[:])
+            elif kind == "o":
+                store(arg[0], arg[1], "scalar")
+            elif kind == "O":
+                store(arg[0], arg[1], "vector")
+
+        for token in PROGRAM.split():
+            step(token)

@@ -24,8 +24,16 @@ PASSES = RAW // GROUP
 HALVES = FEATS // 512
 TILES = PAIRS // P
 QTILES = RANKERS // P
+STEPS = TILES // 2
+BANKS = 8
 
-PROGRAM = """c0 T0 C1 C2 C3 v T1 p0 v x d T2 e p1 p2 d T3 p3 w q w d e w v v t e w q e d e t d w e w t s s e s w t e d d e s i00 w t d h00 l00 d t w e e s d e w i01 l01 t t w s e s h01 L0 w s s e e e e e d t d d t i10 i11 u001 e e l10 s e h10 s l11 d e s t t u000 e e u003 e L1 i20 e d h20 s u100 u103 l20 s d e u101 s l21 e s e h11 e e i21 L2 e u113 u203 h21 u110 I31 u012 l30 i30 L30 u213 l32 u202 u013 u201 h30 u211 L32 u212 u200 l31 u102 u210 h31 u002 L31 l33 u300 u302 u010 u011 o00 u310 o02 u111 u311 u312 o10 u301 L33 u313 O11 O01 u112 o13 O12 u303 O03"""
+EARLY = 2
+SCORE_LAG = 1
+WARM = 0
+ROOM = 5
+ON_SCALAR = 2
+EARLY_SUMS = 1
+CATCH = False
 
 FLOPS = 2 * PAIRS * RAW * RANKERS + 2 * PAIRS * RAW * FEATS + 2 * RANKERS * PAIRS * FEATS
 
@@ -35,7 +43,7 @@ def tile_lambdarank_head_gradient_s11_kernel(tc, d_bytes, d_scale, v, delta, ipw
     with ExitStack() as ctx:
         keep = ctx.enter_context(tc.tile_pool(name="keep", bufs=1))
         work = ctx.enter_context(tc.tile_pool(name="work", bufs=3))
-        psum = ctx.enter_context(tc.psum_pool(name="psum", bufs=1))
+        psum = ctx.enter_context(tc.psum_pool(name="psum", bufs=BANKS - EARLY_SUMS))
 
         ident = keep.tile([P, P], F32, name="ident")
         make_identity(nc, ident[:])
@@ -47,39 +55,51 @@ def tile_lambdarank_head_gradient_s11_kernel(tc, d_bytes, d_scale, v, delta, ipw
         raw = [keep.tile([P, PACK, RAW], U8, name=f"raw{s}", align_bytes=64) for s in range(GROUPS)]
         dlt = [keep.tile([P, PACK, RANKERS], BF16, name=f"dlt{s}", align_bytes=64) for s in range(GROUPS)]
         v_raw = [keep.tile([P, PACK, RANKERS], BF16, name=f"v_raw{g}", align_bytes=64) for g in range(PASSES)]
-        e_w = [keep.tile([P, 2 * FEATS], U8, name=f"e_w{g}", align_bytes=64) for g in range(PASSES)]
+        e_w = keep.tile([P, PASSES, 2 * FEATS], U8, name="e_w", align_bytes=64)
         e_s = keep.tile([P, PASSES, FEATS], U8, name="e_s", align_bytes=64)
         ipw_bf = keep.tile([P, GROUPS, PACK], BF16, name="ipw_bf")
         ipw_f = keep.tile([P, GROUPS, PACK], F32, name="ipw_f")
-
-        warm = keep.tile([P, 1], F32, name="warm")
-        nc.vector.memset(warm[:], 0.0)
-        warm_out = keep.tile([P, 1], F32, name="warm_out")
-        nc.scalar.activation(out=warm_out[:], in_=warm[:], func=SIGMOID, scale=-1.0)
-        nc.vector.memset(e_s[:].bitcast(I32), 0)
 
         d_view = d_bytes.rearrange("(s m t) k -> s m t k", m=P, t=PACK)
         dlt_view = delta.rearrange("(s m t) q -> s m t q", m=P, t=PACK)
         v_view = v.rearrange("(g p t) n -> g p t n", p=P, t=PACK)
         s_view = e_scales.rearrange("g r n -> r g n")
 
+        nc.vector.memset(e_s[:].bitcast(I32), 0)
+        warm = keep.tile([P, 1], F32, name="warm")
+        nc.vector.memset(warm[:], 0.0)
+        nc.sync.dma_start(out=raw[0][:, 0:2, :], in_=d_view[0][:, 0:2, :])
         nc.scalar.dma_start(out=scale_kp[:], in_=d_scale.rearrange("o (g p t) -> p (o g) t", p=P, t=PACK))
-        nc.scalar.dma_start(out=ipw_bf[:], in_=ipw.rearrange("(s m t) -> m s t", m=P, t=PACK))
-        nc.sync.dma_start(out=raw[0][:, 0:1, :], in_=d_view[0][:, 0:1, :])
-        nc.sync.dma_start(out=raw[0][:, 1:4, :], in_=d_view[0][:, 1:4, :])
-        for g in range(PASSES):
-            nc.sync.dma_start(out=e_w[g][:], in_=e_words[g])
+        warm_out = keep.tile([P, 1], F32, name="warm_out")
+        nc.scalar.activation(out=warm_out[:], in_=warm[:], func=SIGMOID, scale=-1.0)
+        nc.sync.dma_start(out=v_raw[0][:], in_=v_view[0])
         for quad in range(4):
             nc.sync.dma_start(out=e_s[32 * quad : 32 * quad + 4].bitcast(I32), in_=s_view[4 * quad : 4 * quad + 4].bitcast(I32))
-        nc.sync.dma_start(out=v_raw[0][:], in_=v_view[0])
-        nc.sync.dma_start(out=scale_bc[:], in_=d_scale.rearrange("o k -> (o k)").partition_broadcast(P))
+        nc.sync.dma_start(out=e_w[:], in_=e_words.rearrange("g p n -> p g n"))
+        nc.sync.dma_start(out=raw[0][:, 2:4, :], in_=d_view[0][:, 2:4, :])
+        nc.sync.dma_start(out=ipw_bf[:], in_=ipw.rearrange("(s m t) -> m s t", m=P, t=PACK))
         nc.sync.dma_start(out=raw[1][:], in_=d_view[1])
         nc.sync.dma_start(out=v_raw[1][:], in_=v_view[1])
         nc.sync.dma_start(out=raw[2][:], in_=d_view[2])
-        nc.sync.dma_start(out=dlt[0][:], in_=dlt_view[0])
         nc.sync.dma_start(out=raw[3][:], in_=d_view[3])
-        for s in range(1, GROUPS):
+        for s in range(GROUPS):
             nc.sync.dma_start(out=dlt[s][:], in_=dlt_view[s])
+
+        def spread_scales():
+            banks = []
+            for g in range(PASSES):
+                bank = psum.tile([P, PACK, P], F32, name="bank")
+                for t in range(PACK):
+                    nc.tensor.transpose(bank[:, t, :], scale_kp[:, g, t : t + 1].to_broadcast([P, P]), ident[:])
+                banks.append(bank)
+            return banks
+
+        def spread_out(banks):
+            for g in range(PASSES):
+                nc.scalar.copy(
+                    out=scale_bc[:, GROUP * g : GROUP * (g + 1)].rearrange("p (q t) -> p q t", t=PACK),
+                    in_=banks[g][:].rearrange("p t q -> p q t"),
+                )
 
         v_codes = [keep.tile([P, RANKERS], U32, name=f"v_codes{g}", align_bytes=64) for g in range(PASSES)]
         v_planes = [keep.tile([P, RANKERS], U8, name=f"v_planes{g}", align_bytes=64) for g in range(PASSES)]
@@ -102,17 +122,17 @@ def tile_lambdarank_head_gradient_s11_kernel(tc, d_bytes, d_scale, v, delta, ipw
         scaled, turned, grouped = {}, {}, {}
 
         def widen(j):
-            scaled[j] = work.tile([P, RAW], BF16, name="scaled", bufs=9, align_bytes=64)
+            scaled[j] = work.tile([P, RAW], BF16, name="scaled", bufs=8, align_bytes=64)
             nc.vector.tensor_tensor(
                 out=scaled[j][:], in0=raw[j // PACK][:, j % PACK, :].bitcast(FP8), in1=scale_bc[:], op=MULT
             )
 
         def widen_only(j, copy):
-            scaled[j] = work.tile([P, RAW], BF16, name="scaled", bufs=9, align_bytes=64)
+            scaled[j] = work.tile([P, RAW], BF16, name="scaled", bufs=8, align_bytes=64)
             copy(out=scaled[j][:], in_=raw[j // PACK][:, j % PACK, :].bitcast(FP8))
 
         def scale_turned(j):
-            grouped[j] = work.tile([P, PASSES * P * PACK], BF16, name="grouped", align_bytes=64)
+            grouped[j] = work.tile([P, PASSES * P * PACK], BF16, name="grouped", bufs=4, align_bytes=64)
             for g in range(PASSES):
                 nc.vector.tensor_tensor(
                     out=grouped[j][:, 512 * g : 512 * (g + 1)].rearrange("p (r u e) -> p r u e", u=2, e=2),
@@ -122,14 +142,14 @@ def tile_lambdarank_head_gradient_s11_kernel(tc, d_bytes, d_scale, v, delta, ipw
                 )
 
         def turn(j):
-            turned[j] = psum.tile([P, PASSES, 2, P], F32, name=f"tp{j % 2}")
+            turned[j] = psum.tile([P, PASSES, 2, P], F32, name="bank")
             words = scaled[j][:].bitcast(F32)
             for g in range(PASSES):
                 for u in range(2):
                     nc.tensor.transpose(turned[j][:, g, u, :], words[:, 256 * g + u : 256 * (g + 1) : 2], ident[:])
 
         def gather(j):
-            grouped[j] = work.tile([P, PASSES * P * PACK], BF16, name="grouped", align_bytes=64)
+            grouped[j] = work.tile([P, PASSES * P * PACK], BF16, name="grouped", bufs=4, align_bytes=64)
             nc.scalar.copy(
                 out=grouped[j][:].bitcast(F32).rearrange("p (g r u) -> p g r u", g=PASSES, u=2),
                 in_=turned[j][:].rearrange("p g u r -> p g r u"),
@@ -142,7 +162,7 @@ def tile_lambdarank_head_gradient_s11_kernel(tc, d_bytes, d_scale, v, delta, ipw
         sig, h_raw = {}, {}
 
         def score(j):
-            diff[j] = psum.tile([P, RANKERS], F32, name="mm", bufs=4)
+            diff[j] = psum.tile([P, RANKERS], F32, name="bank")
             for g in range(PASSES):
                 cols = slice(g * P, (g + 1) * P)
                 nc.tensor.matmul_mx(
@@ -157,19 +177,19 @@ def tile_lambdarank_head_gradient_s11_kernel(tc, d_bytes, d_scale, v, delta, ipw
             nc.scalar.activation(out=sig[s][:, t, :], in_=diff[j][:], func=SIGMOID, scale=-1.0)
 
         def encode(j, half):
-            encoded[j, half] = psum.tile([P, 512], F32, name="mm", bufs=4)
+            encoded[j, half] = psum.tile([P, 512], F32, name="bank")
             for g in range(PASSES):
                 cols = slice(g * P, (g + 1) * P)
                 nc.tensor.matmul_mx(
                     out=encoded[j, half][:], lhsT=d_codes[j][:, cols].bitcast(E4M3X4), lhsT_scale=d_planes[j][:, cols],
-                    rhs=e_w[g][:, 1024 * half : 1024 * (half + 1)].bitcast(E2M1X4), rhs_scale=e_s[:, g, 512 * half : 512 * (half + 1)],
+                    rhs=e_w[:, g, 1024 * half : 1024 * (half + 1)].bitcast(E2M1X4), rhs_scale=e_s[:, g, 512 * half : 512 * (half + 1)],
                     start=(g == 0), stop=(g == PASSES - 1),
                 )
 
         def weigh(j, half):
             s, t = divmod(j, PACK)
             if t == 0:
-                h_raw[s, half] = work.tile([P, PACK, 512], BF16, name=f"h_raw{half}", bufs=2, align_bytes=64)
+                h_raw[s, half] = work.tile([P, PACK, 512], BF16, name=f"h_raw{half}", bufs=3, align_bytes=64)
             nc.scalar.activation(out=h_raw[s, half][:, t, :], in_=encoded[j, half][:], func=COPY, scale=ipw_f[:, s, t : t + 1])
 
         lam_codes = [keep.tile([P, RANKERS], U32, name=f"lam_codes{s}", align_bytes=64) for s in range(GROUPS)]
@@ -210,12 +230,14 @@ def tile_lambdarank_head_gradient_s11_kernel(tc, d_bytes, d_scale, v, delta, ipw
             )
 
         acc, summed = {}, {}
-        banks = {(0, 0): "acc0", (0, 1): "acc1", (0, 2): "tp0", (0, 3): "tp1", (1, 0): "mm", (1, 1): "mm", (1, 2): "mm", (1, 3): "mm"}
 
         def update(s, half, m):
             summed[half, m] = summed.get((half, m), 0) + 1
             if summed[half, m] == 1:
-                acc[half, m] = psum.tile([P, 512], F32, name=banks[half, m], bufs=4 if half == 1 else 1)
+                if half == 0 and m < EARLY_SUMS:
+                    acc[half, m] = psum.tile([P, 512], F32, name=f"sum{m}", bufs=1)
+                else:
+                    acc[half, m] = psum.tile([P, 512], F32, name="bank")
             cols = slice(m * P, (m + 1) * P)
             nc.tensor.matmul_mx(
                 out=acc[half, m][:], lhsT=lam_codes[s][:, cols].bitcast(E4M3X4), lhsT_scale=lam_planes[s][:, cols],
@@ -232,56 +254,132 @@ def tile_lambdarank_head_gradient_s11_kernel(tc, d_bytes, d_scale, v, delta, ipw
             nc.sync.dma_start(out=out[m * P : (m + 1) * P, 512 * half : 512 * (half + 1)], in_=res[:])
 
         last = GROUPS - 1
-        order = dict(w=list(range(PACK, TILES)), t=list(range(PACK, TILES)), d=list(range(TILES)), s=list(range(TILES)),
-                     e=[(j, h) for j in range(TILES) for h in range(HALVES)], v=[(g, part) for g in range(PASSES) for part in range(2)],
-                     q=list(range(PASSES)))
 
-        def step(token):
-            kind, arg = token[0], [int(x) for x in token[1:]]
-            nxt = order[kind].pop(0) if kind in order else None
-            if kind == "w":
-                widen(nxt)
-            elif kind == "t":
-                turn(nxt)
-                gather(nxt)
-            elif kind == "d":
-                d_quantize(nxt)
-            elif kind == "s":
-                score(nxt)
-                sigmoid(nxt)
-            elif kind == "e":
-                encode(*nxt)
-                weigh(*nxt)
-            elif kind == "v":
-                v_interleave(*nxt, 2, nc.scalar.copy)
-            elif kind == "q":
-                v_quantize(nxt)
-            elif kind == "c":
-                widen_only(arg[0], nc.vector.tensor_copy)
-            elif kind == "C":
-                widen_only(arg[0], nc.scalar.copy)
-            elif kind == "T":
-                turn(arg[0])
-            elif kind == "p":
-                scale_turned(arg[0])
-            elif kind == "l":
-                lam_mult(arg[0], arg[1], 4 if arg[0] == last else 2)
-            elif kind == "L":
-                lam_quantize(arg[0], arg[1] if arg[0] == last else 0, 4 if arg[0] == last else 1)
-            elif kind == "i":
-                h_interleave(*arg)
-            elif kind == "I":
-                h_interleave(*arg, nc.scalar.copy)
-            elif kind == "h":
-                h_quantize(*arg)
-            elif kind == "u":
-                update(*arg)
-            elif kind == "x":
-                nc.vector.tensor_copy(out=ipw_f[:], in_=ipw_bf[:])
-            elif kind == "o":
-                store(arg[0], arg[1], "scalar")
-            elif kind == "O":
-                store(arg[0], arg[1], "vector")
+        def encode_tile(j):
+            for half in range(HALVES):
+                encode(j, half)
+                weigh(j, half)
 
-        for token in PROGRAM.split():
-            step(token)
+        def score_tile(j):
+            score(j)
+            sigmoid(j)
+
+        def turn_tile(j):
+            turn(j)
+            gather(j)
+
+        def early_updates(s):
+            for m in range(EARLY_SUMS):
+                update(s, 0, m)
+
+        def group_work(s):
+            ready = 2 * s + 2
+            items = [(ready, h_interleave, (s, 0)), (ready + SCORE_LAG, lam_mult, (s, 0, 2)), (ready, h_quantize, (s, 0)), (ready + SCORE_LAG, lam_mult, (s, 1, 2))]
+            if s > 0:
+                items += [(ready, h_quantize, (s - 1, 1))]
+            items += [(ready + SCORE_LAG, lam_quantize, (s, 0, 1))]
+            if s < ON_SCALAR:
+                items += [(ready, h_interleave, (s, 1))]
+            return items
+
+        widen_only(0, nc.vector.tensor_copy)
+        widen_only(1, nc.vector.tensor_copy)
+        turn(0)
+        v_interleave(0, 0, 2, nc.scalar.copy)
+        spread_out(spread_scales())
+        v_interleave(0, 1, 2, nc.scalar.copy)
+        turn(1)
+        scale_turned(0)
+        d_quantize(0)
+        scale_turned(1)
+        nc.gpsimd.tensor_copy(out=ipw_f[:], in_=ipw_bf[:])
+        widen(2)
+        d_quantize(1)
+        widen(3)
+        encode_tile(0)
+        turn_tile(2)
+        v_interleave(1, 0, 2, nc.scalar.copy)
+        widen(4)
+        d_quantize(2)
+        for half in range(HALVES):
+            encode(1, half)
+        turn_tile(3)
+        for half in range(HALVES):
+            weigh(1, half)
+        widen(5)
+        d_quantize(3)
+        v_interleave(1, 1, 2, nc.vector.tensor_copy)
+        v_quantize(0)
+
+        waiting = [(1, v_quantize, (1,))]
+        for s in range(last):
+            waiting += group_work(s)
+        scored = 0
+        done = []
+        for p in range(1, STEPS):
+            if p == 1:
+                for j in (2, 3):
+                    for half in range(HALVES):
+                        encode(j, half)
+                    turn_tile(j + 2)
+                    for half in range(HALVES):
+                        weigh(j, half)
+            else:
+                if p + 1 < STEPS:
+                    turn(2 * p + 2)
+                    turn(2 * p + 3)
+                    gather(2 * p + 2)
+                    gather(2 * p + 3)
+                for j in (2 * p, 2 * p + 1):
+                    encode_tile(j)
+                    for n in range(2 if scored + 2 * SCORE_LAG <= j - 1 or p + 1 == STEPS and CATCH else 1):
+                        if scored <= j:
+                            score_tile(scored)
+                            scored += 1
+            for s in range(last):
+                if (lam_quantize, (s, 0, 1)) in done and summed.get((0, 0), 0) == s:
+                    early_updates(s)
+            room = ROOM
+            if p + 2 < STEPS:
+                widen(2 * p + 4)
+                widen(2 * p + 5)
+                room -= 2
+            if p + 1 < STEPS:
+                d_quantize(2 * p + 2)
+                d_quantize(2 * p + 3)
+            while room > 0 and waiting and waiting[0][0] <= p and (waiting[0][1] is not lam_mult or scored >= PACK * waiting[0][2][0] + PACK):
+                ready, fn, args = waiting.pop(0)
+                if fn is not None:
+                    fn(*args)
+                    done.append((fn, args))
+                    room -= 1
+        for j in range(scored, TILES):
+            score_tile(j)
+        for s in range(ON_SCALAR, GROUPS):
+            h_interleave(s, 1, nc.scalar.copy)
+        for ready, fn, args in waiting:
+            fn(*args)
+        h_interleave(last, 0)
+        lam_mult(last, 0, QTILES)
+        h_quantize(last, 0)
+        for s in range(last):
+            for m in range(QTILES):
+                if summed.get((0, m), 0) == s:
+                    update(s, 0, m)
+        for s in range(last - 1):
+            for m in range(QTILES):
+                update(s, 1, m)
+        for m in range(QTILES):
+            if m + 1 < QTILES:
+                lam_mult(last, m + 1, QTILES)
+            else:
+                h_quantize(last - 1, 1)
+            lam_quantize(last, m, QTILES)
+            update(last, 0, m)
+            store(0, m, "scalar")
+        h_quantize(last, 1)
+        for m in range(QTILES):
+            update(last - 1, 1, m)
+        for m in range(QTILES):
+            update(last, 1, m)
+            store(1, m, "vector" if m % 2 == 0 else "scalar")

@@ -31,9 +31,15 @@ EARLY = 2
 SCORE_LAG = 1
 WARM = 0
 ROOM = 5
-ON_SCALAR = 2
-EARLY_SUMS = 1
+ON_SCALAR = 1
+EARLY_SUMS = 0
 CATCH = False
+HEAD_SCORES = 2
+V_ON_SCALAR = 4
+PIECES = ((0, 0, 512), (1, 0, 256), (1, 256, 512))
+BEFORE = 1
+LAST_ON_V = False
+Q3_ON_SCALAR = 0
 
 FLOPS = 2 * PAIRS * RAW * RANKERS + 2 * PAIRS * RAW * FEATS + 2 * RANKERS * PAIRS * FEATS
 
@@ -72,14 +78,14 @@ def tile_lambdarank_head_gradient_s11_kernel(tc, d_bytes, d_scale, v, delta, ipw
         nc.scalar.dma_start(out=scale_kp[:], in_=d_scale.rearrange("o (g p t) -> p (o g) t", p=P, t=PACK))
         warm_out = keep.tile([P, 1], F32, name="warm_out")
         nc.scalar.activation(out=warm_out[:], in_=warm[:], func=SIGMOID, scale=-1.0)
+        nc.sync.dma_start(out=raw[0][:, 2:4, :], in_=d_view[0][:, 2:4, :])
         nc.sync.dma_start(out=v_raw[0][:], in_=v_view[0])
         for quad in range(4):
             nc.sync.dma_start(out=e_s[32 * quad : 32 * quad + 4].bitcast(I32), in_=s_view[4 * quad : 4 * quad + 4].bitcast(I32))
         nc.sync.dma_start(out=e_w[:], in_=e_words.rearrange("g p n -> p g n"))
-        nc.sync.dma_start(out=raw[0][:, 2:4, :], in_=d_view[0][:, 2:4, :])
+        nc.sync.dma_start(out=v_raw[1][:], in_=v_view[1])
         nc.sync.dma_start(out=ipw_bf[:], in_=ipw.rearrange("(s m t) -> m s t", m=P, t=PACK))
         nc.sync.dma_start(out=raw[1][:], in_=d_view[1])
-        nc.sync.dma_start(out=v_raw[1][:], in_=v_view[1])
         nc.sync.dma_start(out=raw[2][:], in_=d_view[2])
         nc.sync.dma_start(out=raw[3][:], in_=d_view[3])
         for s in range(GROUPS):
@@ -131,9 +137,10 @@ def tile_lambdarank_head_gradient_s11_kernel(tc, d_bytes, d_scale, v, delta, ipw
             scaled[j] = work.tile([P, RAW], BF16, name="scaled", bufs=8, align_bytes=64)
             copy(out=scaled[j][:], in_=raw[j // PACK][:, j % PACK, :].bitcast(FP8))
 
-        def scale_turned(j):
-            grouped[j] = work.tile([P, PASSES * P * PACK], BF16, name="grouped", bufs=4, align_bytes=64)
-            for g in range(PASSES):
+        def scale_turned(j, g):
+            if g == 0:
+                grouped[j] = work.tile([P, PASSES * P * PACK], BF16, name="grouped", bufs=4, align_bytes=64)
+            if True:
                 nc.vector.tensor_tensor(
                     out=grouped[j][:, 512 * g : 512 * (g + 1)].rearrange("p (r u e) -> p r u e", u=2, e=2),
                     in0=turned[j][:, g].bitcast(BF16).rearrange("p u (r e) -> p r u e", e=2),
@@ -189,7 +196,7 @@ def tile_lambdarank_head_gradient_s11_kernel(tc, d_bytes, d_scale, v, delta, ipw
         def weigh(j, half):
             s, t = divmod(j, PACK)
             if t == 0:
-                h_raw[s, half] = work.tile([P, PACK, 512], BF16, name=f"h_raw{half}", bufs=3, align_bytes=64)
+                h_raw[s, half] = work.tile([P, PACK, 512], BF16, name=f"h_raw{half}", bufs=2 + half, align_bytes=64)
             nc.scalar.activation(out=h_raw[s, half][:, t, :], in_=encoded[j, half][:], func=COPY, scale=ipw_f[:, s, t : t + 1])
 
         lam_codes = [keep.tile([P, RANKERS], U32, name=f"lam_codes{s}", align_bytes=64) for s in range(GROUPS)]
@@ -216,42 +223,45 @@ def tile_lambdarank_head_gradient_s11_kernel(tc, d_bytes, d_scale, v, delta, ipw
                 in_=lam[s][:, cols, :].rearrange("p n t -> p (n t)"),
             )
 
-        def h_interleave(s, half, copy=nc.vector.tensor_copy):
-            h_grp[s, half] = work.tile([P, 512, PACK], BF16, name="h_grp", bufs=4, align_bytes=64)
+        def h_interleave(s, half, copy=nc.vector.tensor_copy, part=0, parts=1):
+            if part == 0:
+                h_grp[s, half] = work.tile([P, 512, PACK], BF16, name="h_grp", bufs=5, align_bytes=64)
+            cols = slice(512 // parts * part, 512 // parts * (part + 1))
             copy(
-                out=h_grp[s, half][:].rearrange("p (c i) t -> p c t i", i=4),
-                in_=h_raw[s, half][:].rearrange("p t (c i) -> p c t i", i=4),
+                out=h_grp[s, half][:, cols, :].rearrange("p (c i) t -> p c t i", i=4),
+                in_=h_raw[s, half][:, :, cols].rearrange("p t (c i) -> p c t i", i=4),
             )
 
-        def h_quantize(s, half):
+        def h_quantize(s, half, part=0, parts=1):
+            cols = slice(512 // parts * part, 512 // parts * (part + 1))
             nc.vector.quantize_mx(
-                out=h_codes[s, half][:].bitcast(E4M3X4), scales=h_planes[s, half][:],
-                in_=h_grp[s, half][:].rearrange("p n t -> p (n t)"),
+                out=h_codes[s, half][:, cols].bitcast(E4M3X4), scales=h_planes[s, half][:, cols],
+                in_=h_grp[s, half][:, cols, :].rearrange("p n t -> p (n t)"),
             )
 
         acc, summed = {}, {}
 
-        def update(s, half, m):
-            summed[half, m] = summed.get((half, m), 0) + 1
-            if summed[half, m] == 1:
-                if half == 0 and m < EARLY_SUMS:
-                    acc[half, m] = psum.tile([P, 512], F32, name=f"sum{m}", bufs=1)
-                else:
-                    acc[half, m] = psum.tile([P, 512], F32, name="bank")
-            cols = slice(m * P, (m + 1) * P)
+        def update(s, piece, m):
+            half, cols = PIECES[piece][0], slice(*PIECES[piece][1:])
+            summed[piece, m] = summed.get((piece, m), 0) + 1
+            if summed[piece, m] == 1:
+                acc[piece, m] = psum.tile([P, 512], F32, name="bank")
+            rows = slice(m * P, (m + 1) * P)
             nc.tensor.matmul_mx(
-                out=acc[half, m][:], lhsT=lam_codes[s][:, cols].bitcast(E4M3X4), lhsT_scale=lam_planes[s][:, cols],
-                rhs=h_codes[s, half][:].bitcast(E4M3X4), rhs_scale=h_planes[s, half][:], start=(summed[half, m] == 1), stop=(summed[half, m] == GROUPS),
+                out=acc[piece, m][:, : cols.stop - cols.start], lhsT=lam_codes[s][:, rows].bitcast(E4M3X4), lhsT_scale=lam_planes[s][:, rows],
+                rhs=h_codes[s, half][:, cols].bitcast(E4M3X4), rhs_scale=h_planes[s, half][:, cols],
+                start=(summed[piece, m] == 1), stop=(summed[piece, m] == GROUPS),
             )
 
-        def store(half, m, engine):
-            assert summed[half, m] == GROUPS
-            res = work.tile([P, 512], F32, name="res", bufs=8)
+        def store(piece, m, engine):
+            half, first, stop = PIECES[piece]
+            width = stop - first
+            res = work.tile([P, width], F32, name=f"res{piece}", bufs=QTILES)
             if engine == "scalar":
-                nc.scalar.copy(out=res[:], in_=acc[half, m][:])
+                nc.scalar.copy(out=res[:, :width], in_=acc[piece, m][:, :width])
             else:
-                nc.vector.tensor_copy(out=res[:], in_=acc[half, m][:])
-            nc.sync.dma_start(out=out[m * P : (m + 1) * P, 512 * half : 512 * (half + 1)], in_=res[:])
+                nc.vector.tensor_copy(out=res[:, :width], in_=acc[piece, m][:, :width])
+            nc.sync.dma_start(out=out[m * P : (m + 1) * P, 512 * half + first : 512 * half + stop], in_=res[:, :width])
 
         last = GROUPS - 1
 
@@ -268,95 +278,94 @@ def tile_lambdarank_head_gradient_s11_kernel(tc, d_bytes, d_scale, v, delta, ipw
             turn(j)
             gather(j)
 
-        def early_updates(s):
-            for m in range(EARLY_SUMS):
-                update(s, 0, m)
-
         def group_work(s):
             ready = 2 * s + 2
             items = [(ready, h_interleave, (s, 0)), (ready + SCORE_LAG, lam_mult, (s, 0, 2)), (ready, h_quantize, (s, 0)), (ready + SCORE_LAG, lam_mult, (s, 1, 2))]
-            if s > 0:
+            if 0 < s <= ON_SCALAR:
                 items += [(ready, h_quantize, (s - 1, 1))]
             items += [(ready + SCORE_LAG, lam_quantize, (s, 0, 1))]
             if s < ON_SCALAR:
                 items += [(ready, h_interleave, (s, 1))]
             return items
 
-        widen_only(0, nc.vector.tensor_copy)
-        widen_only(1, nc.vector.tensor_copy)
+        for j in range(PACK):
+            widen_only(j, nc.scalar.copy if j % 2 else nc.vector.tensor_copy)
         turn(0)
+        turn(1)
         v_interleave(0, 0, 2, nc.scalar.copy)
         spread_out(spread_scales())
-        v_interleave(0, 1, 2, nc.scalar.copy)
-        turn(1)
-        scale_turned(0)
-        d_quantize(0)
-        scale_turned(1)
+        turn(2)
+        turn(3)
         nc.gpsimd.tensor_copy(out=ipw_f[:], in_=ipw_bf[:])
-        widen(2)
-        d_quantize(1)
-        widen(3)
-        encode_tile(0)
-        turn_tile(2)
-        v_interleave(1, 0, 2, nc.scalar.copy)
+        for part in range(1, 4):
+            v_interleave(part // 2, part % 2, 2, nc.scalar.copy)
+        for j in range(PACK):
+            scale_turned(j, 0)
+            if j > 0:
+                d_quantize(j - 1)
+            scale_turned(j, 1)
         widen(4)
-        d_quantize(2)
-        for half in range(HALVES):
-            encode(1, half)
-        turn_tile(3)
-        for half in range(HALVES):
-            weigh(1, half)
-        widen(5)
         d_quantize(3)
-        v_interleave(1, 1, 2, nc.vector.tensor_copy)
+        widen(5)
         v_quantize(0)
+        encode_tile(0)
+        for j in (1, 2):
+            for half in range(HALVES):
+                encode(j, half)
+        turn(4)
+        weigh(1, 0)
+        gather(4)
+        weigh(1, 1)
+        for half in range(HALVES):
+            encode(3, half)
+        turn_tile(5)
+        for j in (2, 3):
+            for half in range(HALVES):
+                weigh(j, half)
+        d_quantize(4)
+        v_quantize(1)
+        widen(6)
+        d_quantize(5)
+        widen(7)
+        for j in range(HEAD_SCORES):
+            score_tile(j)
 
-        waiting = [(1, v_quantize, (1,))]
+        waiting = []
         for s in range(last):
             waiting += group_work(s)
-        scored = 0
+        scored = HEAD_SCORES
         done = []
-        for p in range(1, STEPS):
-            if p == 1:
-                for j in (2, 3):
-                    for half in range(HALVES):
-                        encode(j, half)
-                    turn_tile(j + 2)
-                    for half in range(HALVES):
-                        weigh(j, half)
-            else:
+        for p in range(2, STEPS):
+            if True:
                 if p + 1 < STEPS:
                     turn(2 * p + 2)
                     turn(2 * p + 3)
                     gather(2 * p + 2)
                     gather(2 * p + 3)
                 for j in (2 * p, 2 * p + 1):
-                    encode_tile(j)
-                    for n in range(2 if scored + 2 * SCORE_LAG <= j - 1 or p + 1 == STEPS and CATCH else 1):
-                        if scored <= j:
-                            score_tile(scored)
-                            scored += 1
-            for s in range(last):
-                if (lam_quantize, (s, 0, 1)) in done and summed.get((0, 0), 0) == s:
-                    early_updates(s)
+                    encode(j, 0)
+                    weigh(j, 0)
+                    score_tile(scored)
+                    scored += 1
+                    encode(j, 1)
+                    weigh(j, 1)
             room = ROOM
             if p + 2 < STEPS:
                 widen(2 * p + 4)
                 widen(2 * p + 5)
                 room -= 2
+            todo = []
+            while len(todo) < room and waiting and waiting[0][0] <= p and (waiting[0][1] is not lam_mult or scored >= PACK * waiting[0][2][0] + PACK):
+                todo.append(waiting.pop(0))
             if p + 1 < STEPS:
-                d_quantize(2 * p + 2)
-                d_quantize(2 * p + 3)
-            while room > 0 and waiting and waiting[0][0] <= p and (waiting[0][1] is not lam_mult or scored >= PACK * waiting[0][2][0] + PACK):
-                ready, fn, args = waiting.pop(0)
-                if fn is not None:
-                    fn(*args)
-                    done.append((fn, args))
-                    room -= 1
+                todo[BEFORE:BEFORE] = [(p, d_quantize, (2 * p + 2,)), (p, d_quantize, (2 * p + 3,))]
+            for ready, fn, args in todo:
+                fn(*args)
         for j in range(scored, TILES):
             score_tile(j)
-        for s in range(ON_SCALAR, GROUPS):
-            h_interleave(s, 1, nc.scalar.copy)
+        late = list(range(ON_SCALAR, GROUPS))
+        for s in late:
+            h_interleave(s, 1, nc.scalar.copy, 0, 2)
         for ready, fn, args in waiting:
             fn(*args)
         h_interleave(last, 0)
@@ -364,22 +373,33 @@ def tile_lambdarank_head_gradient_s11_kernel(tc, d_bytes, d_scale, v, delta, ipw
         h_quantize(last, 0)
         for s in range(last):
             for m in range(QTILES):
-                if summed.get((0, m), 0) == s:
-                    update(s, 0, m)
-        for s in range(last - 1):
+                update(s, 0, m)
+        for s in range(ON_SCALAR):
             for m in range(QTILES):
                 update(s, 1, m)
         for m in range(QTILES):
             if m + 1 < QTILES:
                 lam_mult(last, m + 1, QTILES)
-            else:
-                h_quantize(last - 1, 1)
+            if m < len(late):
+                h_quantize(late[m], 1, 0, 2)
             lam_quantize(last, m, QTILES)
+            if m < len(late) - 1:
+                for n in range(QTILES):
+                    update(late[m], 1, n)
             update(last, 0, m)
             store(0, m, "scalar")
-        h_quantize(last, 1)
-        for m in range(QTILES):
-            update(last - 1, 1, m)
         for m in range(QTILES):
             update(last, 1, m)
-            store(1, m, "vector" if m % 2 == 0 else "scalar")
+        for s in late[:Q3_ON_SCALAR]:
+            h_interleave(s, 1, nc.scalar.copy, 1, 2)
+        for s in late[Q3_ON_SCALAR:]:
+            h_interleave(s, 1, nc.vector.tensor_copy, 1, 2)
+        for s in late:
+            h_quantize(s, 1, 1, 2)
+        for m in range(QTILES):
+            store(1, m, "scalar")
+        for s in range(GROUPS):
+            for m in range(QTILES):
+                update(s, 2, m)
+        for m in range(QTILES):
+            store(2, m, "vector" if m % 2 == 0 else "scalar")

@@ -40,6 +40,12 @@ PIECES = ((0, 0, 512), (1, 0, 256), (1, 256, 512))
 BEFORE = 1
 LAST_ON_V = False
 Q3_ON_SCALAR = 0
+DEFER = 4
+FIRST = 2
+AFTER = (0,)
+SHARE = 5
+WROOM = 2
+BEFORE_LAST = 2
 
 FLOPS = 2 * PAIRS * RAW * RANKERS + 2 * PAIRS * RAW * FEATS + 2 * RANKERS * PAIRS * FEATS
 
@@ -84,8 +90,9 @@ def tile_lambdarank_head_gradient_s11_kernel(tc, d_bytes, d_scale, v, delta, ipw
             nc.sync.dma_start(out=e_s[32 * quad : 32 * quad + 4].bitcast(I32), in_=s_view[4 * quad : 4 * quad + 4].bitcast(I32))
         nc.sync.dma_start(out=e_w[:], in_=e_words.rearrange("g p n -> p g n"))
         nc.sync.dma_start(out=v_raw[1][:], in_=v_view[1])
+        nc.sync.dma_start(out=raw[1][:, 0:2, :], in_=d_view[1][:, 0:2, :])
         nc.sync.dma_start(out=ipw_bf[:], in_=ipw.rearrange("(s m t) -> m s t", m=P, t=PACK))
-        nc.sync.dma_start(out=raw[1][:], in_=d_view[1])
+        nc.sync.dma_start(out=raw[1][:, 2:4, :], in_=d_view[1][:, 2:4, :])
         nc.sync.dma_start(out=raw[2][:], in_=d_view[2])
         nc.sync.dma_start(out=raw[3][:], in_=d_view[3])
         for s in range(GROUPS):
@@ -128,13 +135,13 @@ def tile_lambdarank_head_gradient_s11_kernel(tc, d_bytes, d_scale, v, delta, ipw
         scaled, turned, grouped = {}, {}, {}
 
         def widen(j):
-            scaled[j] = work.tile([P, RAW], BF16, name="scaled", bufs=8, align_bytes=64)
+            scaled[j] = work.tile([P, RAW], BF16, name="scaled", bufs=5, align_bytes=64)
             nc.vector.tensor_tensor(
                 out=scaled[j][:], in0=raw[j // PACK][:, j % PACK, :].bitcast(FP8), in1=scale_bc[:], op=MULT
             )
 
         def widen_only(j, copy):
-            scaled[j] = work.tile([P, RAW], BF16, name="scaled", bufs=8, align_bytes=64)
+            scaled[j] = work.tile([P, RAW], BF16, name="scaled", bufs=5, align_bytes=64)
             copy(out=scaled[j][:], in_=raw[j // PACK][:, j % PACK, :].bitcast(FP8))
 
         def scale_turned(j, g):
@@ -196,7 +203,7 @@ def tile_lambdarank_head_gradient_s11_kernel(tc, d_bytes, d_scale, v, delta, ipw
         def weigh(j, half):
             s, t = divmod(j, PACK)
             if t == 0:
-                h_raw[s, half] = work.tile([P, PACK, 512], BF16, name=f"h_raw{half}", bufs=2 + half, align_bytes=64)
+                h_raw[s, half] = work.tile([P, PACK, 512], BF16, name=f"h_raw{half}", bufs=2 + 2 * half, align_bytes=64)
             nc.scalar.activation(out=h_raw[s, half][:, t, :], in_=encoded[j, half][:], func=COPY, scale=ipw_f[:, s, t : t + 1])
 
         lam_codes = [keep.tile([P, RANKERS], U32, name=f"lam_codes{s}", align_bytes=64) for s in range(GROUPS)]
@@ -210,9 +217,9 @@ def tile_lambdarank_head_gradient_s11_kernel(tc, d_bytes, d_scale, v, delta, ipw
                 lam[s] = work.tile([P, RANKERS, PACK], BF16, name="lam", bufs=2, align_bytes=64)
             cols = slice(RANKERS // parts * part, RANKERS // parts * (part + 1))
             nc.vector.tensor_tensor(
-                out=lam[s][:, cols, :].rearrange("p (c i) t -> p c t i", i=4),
-                in0=sig[s][:, :, cols].rearrange("p t (c i) -> p c t i", i=4),
-                in1=dlt[s][:, :, cols].rearrange("p t (c i) -> p c t i", i=4),
+                out=lam[s][:, cols, :].rearrange("p (c i) t -> p c t i", i=2),
+                in0=sig[s][:, :, cols].rearrange("p t (c i) -> p c t i", i=2),
+                in1=dlt[s][:, :, cols].rearrange("p t (c i) -> p c t i", i=2),
                 op=MULT,
             )
 
@@ -223,17 +230,17 @@ def tile_lambdarank_head_gradient_s11_kernel(tc, d_bytes, d_scale, v, delta, ipw
                 in_=lam[s][:, cols, :].rearrange("p n t -> p (n t)"),
             )
 
-        def h_interleave(s, half, copy=nc.vector.tensor_copy, part=0, parts=1):
-            if part == 0:
-                h_grp[s, half] = work.tile([P, 512, PACK], BF16, name="h_grp", bufs=5, align_bytes=64)
-            cols = slice(512 // parts * part, 512 // parts * (part + 1))
+        def h_interleave(s, piece, copy=nc.vector.tensor_copy):
+            half, cols = PIECES[piece][0], slice(*PIECES[piece][1:])
+            if cols.start == 0:
+                h_grp[s, half] = work.tile([P, 512, PACK], BF16, name=f"h_grp{half}", bufs=2 + 2 * half, align_bytes=64)
             copy(
                 out=h_grp[s, half][:, cols, :].rearrange("p (c i) t -> p c t i", i=4),
                 in_=h_raw[s, half][:, :, cols].rearrange("p t (c i) -> p c t i", i=4),
             )
 
-        def h_quantize(s, half, part=0, parts=1):
-            cols = slice(512 // parts * part, 512 // parts * (part + 1))
+        def h_quantize(s, piece):
+            half, cols = PIECES[piece][0], slice(*PIECES[piece][1:])
             nc.vector.quantize_mx(
                 out=h_codes[s, half][:, cols].bitcast(E4M3X4), scales=h_planes[s, half][:, cols],
                 in_=h_grp[s, half][:, cols, :].rearrange("p n t -> p (n t)"),
@@ -241,11 +248,13 @@ def tile_lambdarank_head_gradient_s11_kernel(tc, d_bytes, d_scale, v, delta, ipw
 
         acc, summed = {}, {}
 
+        def open_sums(piece):
+            for m in range(QTILES):
+                acc[piece, m] = psum.tile([P, 512], F32, name="bank")
+
         def update(s, piece, m):
             half, cols = PIECES[piece][0], slice(*PIECES[piece][1:])
             summed[piece, m] = summed.get((piece, m), 0) + 1
-            if summed[piece, m] == 1:
-                acc[piece, m] = psum.tile([P, 512], F32, name="bank")
             rows = slice(m * P, (m + 1) * P)
             nc.tensor.matmul_mx(
                 out=acc[piece, m][:, : cols.stop - cols.start], lhsT=lam_codes[s][:, rows].bitcast(E4M3X4), lhsT_scale=lam_planes[s][:, rows],
@@ -279,14 +288,8 @@ def tile_lambdarank_head_gradient_s11_kernel(tc, d_bytes, d_scale, v, delta, ipw
             gather(j)
 
         def group_work(s):
-            ready = 2 * s + 2
-            items = [(ready, h_interleave, (s, 0)), (ready + SCORE_LAG, lam_mult, (s, 0, 2)), (ready, h_quantize, (s, 0)), (ready + SCORE_LAG, lam_mult, (s, 1, 2))]
-            if 0 < s <= ON_SCALAR:
-                items += [(ready, h_quantize, (s - 1, 1))]
-            items += [(ready + SCORE_LAG, lam_quantize, (s, 0, 1))]
-            if s < ON_SCALAR:
-                items += [(ready, h_interleave, (s, 1))]
-            return items
+            ready = 2 * s + 4
+            return [(ready, lam_mult, (s, 0, 2)), (ready, lam_mult, (s, 1, 2)), (ready, h_interleave, (s + 1, 0)), (ready, lam_quantize, (s, 0, 1)), (ready, h_quantize, (s + 1, 0))]
 
         for j in range(PACK):
             widen_only(j, nc.scalar.copy if j % 2 else nc.vector.tensor_copy)
@@ -296,9 +299,10 @@ def tile_lambdarank_head_gradient_s11_kernel(tc, d_bytes, d_scale, v, delta, ipw
         spread_out(spread_scales())
         turn(2)
         turn(3)
-        nc.gpsimd.tensor_copy(out=ipw_f[:], in_=ipw_bf[:])
-        for part in range(1, 4):
+        for part in range(1, 3):
             v_interleave(part // 2, part % 2, 2, nc.scalar.copy)
+        nc.scalar.copy(out=ipw_f[:], in_=ipw_bf[:])
+        v_interleave(1, 1, 2, nc.scalar.copy)
         for j in range(PACK):
             scale_turned(j, 0)
             if j > 0:
@@ -307,7 +311,7 @@ def tile_lambdarank_head_gradient_s11_kernel(tc, d_bytes, d_scale, v, delta, ipw
         widen(4)
         d_quantize(3)
         widen(5)
-        v_quantize(0)
+        widen(6)
         encode_tile(0)
         for j in (1, 2):
             for half in range(HALVES):
@@ -323,19 +327,31 @@ def tile_lambdarank_head_gradient_s11_kernel(tc, d_bytes, d_scale, v, delta, ipw
             for half in range(HALVES):
                 weigh(j, half)
         d_quantize(4)
-        v_quantize(1)
-        widen(6)
-        d_quantize(5)
         widen(7)
-        for j in range(HEAD_SCORES):
-            score_tile(j)
+        d_quantize(5)
+        v_quantize(0)
+        v_quantize(1)
+        encode_tile(4)
+        turn(6)
+        turn(7)
+        gather(6)
+        gather(7)
+        encode_tile(5)
+        score_tile(0)
+        score_tile(1)
+        widen(8)
+        widen(9)
+        d_quantize(6)
+        d_quantize(7)
 
         waiting = []
-        for s in range(last):
+        for s in range(last - 1):
             waiting += group_work(s)
+        waiting += [(STEPS - 1, h_interleave, (last, 0))]
+        waiting = [(3, h_interleave, (0, 0)), (3, h_quantize, (0, 0))] + waiting
         scored = HEAD_SCORES
         done = []
-        for p in range(2, STEPS):
+        for p in range(3, STEPS):
             if True:
                 if p + 1 < STEPS:
                     turn(2 * p + 2)
@@ -347,58 +363,66 @@ def tile_lambdarank_head_gradient_s11_kernel(tc, d_bytes, d_scale, v, delta, ipw
                     weigh(j, 0)
                     score_tile(scored)
                     scored += 1
-                    encode(j, 1)
-                    weigh(j, 1)
+                    if j < TILES - DEFER:
+                        encode(j, 1)
+                        weigh(j, 1)
             room = ROOM
             if p + 2 < STEPS:
                 widen(2 * p + 4)
                 widen(2 * p + 5)
-                room -= 2
+                room = WROOM
             todo = []
             while len(todo) < room and waiting and waiting[0][0] <= p and (waiting[0][1] is not lam_mult or scored >= PACK * waiting[0][2][0] + PACK):
                 todo.append(waiting.pop(0))
             if p + 1 < STEPS:
-                todo[BEFORE:BEFORE] = [(p, d_quantize, (2 * p + 2,)), (p, d_quantize, (2 * p + 3,))]
+                first = BEFORE if p + 2 < STEPS else BEFORE_LAST
+                todo[first:first] = [(p, d_quantize, (2 * p + 2,)), (p, d_quantize, (2 * p + 3,))]
             for ready, fn, args in todo:
                 fn(*args)
         for j in range(scored, TILES):
             score_tile(j)
-        late = list(range(ON_SCALAR, GROUPS))
-        for s in late:
-            h_interleave(s, 1, nc.scalar.copy, 0, 2)
+        for j in range(TILES - DEFER, TILES):
+            encode(j, 1)
+            weigh(j, 1)
+        late = (last - 1, last)
+        open_sums(0)
+        open_sums(1)
+        for s in range(FIRST):
+            h_interleave(s, 1, nc.scalar.copy)
         for ready, fn, args in waiting:
             fn(*args)
-        h_interleave(last, 0)
-        lam_mult(last, 0, QTILES)
+        lam_mult(late[0], 0, QTILES)
         h_quantize(last, 0)
-        for s in range(last):
-            for m in range(QTILES):
+        for m in range(QTILES):
+            lam_mult(late[1], m, QTILES)
+            lam_quantize(late[0], m, QTILES)
+            if m + 1 < QTILES:
+                lam_mult(late[0], m + 1, QTILES)
+            else:
+                h_quantize(last - 1, 1)
+            lam_quantize(late[1], m, QTILES)
+            for s in range(GROUPS):
                 update(s, 0, m)
-        for s in range(ON_SCALAR):
+            store(0, m, "scalar")
+            if FIRST + m < GROUPS:
+                h_interleave(FIRST + m, 1, nc.scalar.copy)
+            if 1 <= m < last:
+                h_quantize(m - 1, 1)
+                for n in range(QTILES):
+                    update(m - 1, 1, n)
+        open_sums(2)
+        h_interleave(0, 2)
+        h_interleave(1, 2)
+        h_quantize(last, 1)
+        for s in late:
             for m in range(QTILES):
                 update(s, 1, m)
         for m in range(QTILES):
-            if m + 1 < QTILES:
-                lam_mult(last, m + 1, QTILES)
-            if m < len(late):
-                h_quantize(late[m], 1, 0, 2)
-            lam_quantize(last, m, QTILES)
-            if m < len(late) - 1:
-                for n in range(QTILES):
-                    update(late[m], 1, n)
-            update(last, 0, m)
-            store(0, m, "scalar")
-        for m in range(QTILES):
-            update(last, 1, m)
-        for s in late[:Q3_ON_SCALAR]:
-            h_interleave(s, 1, nc.scalar.copy, 1, 2)
-        for s in late[Q3_ON_SCALAR:]:
-            h_interleave(s, 1, nc.vector.tensor_copy, 1, 2)
-        for s in late:
-            h_quantize(s, 1, 1, 2)
-        for m in range(QTILES):
             store(1, m, "scalar")
         for s in range(GROUPS):
+            h_quantize(s, 2)
+            if s + 2 < GROUPS:
+                h_interleave(s + 2, 2)
             for m in range(QTILES):
                 update(s, 2, m)
         for m in range(QTILES):

@@ -21,31 +21,16 @@ PACK = 4
 GROUP = P * PACK
 GROUPS = PAIRS // GROUP
 PASSES = RAW // GROUP
-HALVES = FEATS // 512
+BANK = 512
+HALVES = FEATS // BANK
 TILES = PAIRS // P
-QTILES = RANKERS // P
 STEPS = TILES // 2
+QTILES = RANKERS // P
 BANKS = 8
-
-EARLY = 2
-SCORE_LAG = 1
-WARM = 0
-ROOM = 5
-ON_SCALAR = 1
-EARLY_SUMS = 0
-CATCH = False
-HEAD_SCORES = 2
-V_ON_SCALAR = 4
-PIECES = ((0, 0, 512), (1, 0, 256), (1, 256, 512))
-BEFORE = 1
-LAST_ON_V = False
-Q3_ON_SCALAR = 0
-DEFER = 4
-FIRST = 2
-AFTER = (0,)
-SHARE = 5
-WROOM = 2
-BEFORE_LAST = 2
+PIECES = ((0, 512), (512, 768), (768, 1024))
+SCORE_LAG = 4
+FIRST = 3
+PLACE = 2
 
 FLOPS = 2 * PAIRS * RAW * RANKERS + 2 * PAIRS * RAW * FEATS + 2 * RANKERS * PAIRS * FEATS
 
@@ -54,8 +39,8 @@ def tile_lambdarank_head_gradient_s11_kernel(tc, d_bytes, d_scale, v, delta, ipw
     nc = tc.nc
     with ExitStack() as ctx:
         keep = ctx.enter_context(tc.tile_pool(name="keep", bufs=1))
-        work = ctx.enter_context(tc.tile_pool(name="work", bufs=3))
-        psum = ctx.enter_context(tc.psum_pool(name="psum", bufs=BANKS - EARLY_SUMS))
+        work = ctx.enter_context(tc.tile_pool(name="work", bufs=1))
+        psum = ctx.enter_context(tc.psum_pool(name="psum", bufs=BANKS))
 
         ident = keep.tile([P, P], F32, name="ident")
         make_identity(nc, ident[:])
@@ -63,7 +48,7 @@ def tile_lambdarank_head_gradient_s11_kernel(tc, d_bytes, d_scale, v, delta, ipw
         ctx.enter_context(tc.manual_schedule())
 
         scale_kp = keep.tile([P, PASSES, PACK], F32, name="scale_kp")
-        scale_bc = keep.tile([P, RAW], F32, name="scale_bc", align_bytes=64)
+        scale_row = keep.tile([P, RAW], F32, name="scale_row", align_bytes=64)
         raw = [keep.tile([P, PACK, RAW], U8, name=f"raw{s}", align_bytes=64) for s in range(GROUPS)]
         dlt = [keep.tile([P, PACK, RANKERS], BF16, name=f"dlt{s}", align_bytes=64) for s in range(GROUPS)]
         v_raw = [keep.tile([P, PACK, RANKERS], BF16, name=f"v_raw{g}", align_bytes=64) for g in range(PASSES)]
@@ -78,241 +63,209 @@ def tile_lambdarank_head_gradient_s11_kernel(tc, d_bytes, d_scale, v, delta, ipw
         s_view = e_scales.rearrange("g r n -> r g n")
 
         nc.vector.memset(e_s[:].bitcast(I32), 0)
-        warm = keep.tile([P, 1], F32, name="warm")
-        nc.vector.memset(warm[:], 0.0)
+        table_in = keep.tile([P, 1], F32, name="table_in")
+        table_out = keep.tile([P, 1], F32, name="table_out")
+        nc.vector.memset(table_in[:], 0.0)
+
         nc.sync.dma_start(out=raw[0][:, 0:2, :], in_=d_view[0][:, 0:2, :])
         nc.scalar.dma_start(out=scale_kp[:], in_=d_scale.rearrange("o (g p t) -> p (o g) t", p=P, t=PACK))
-        warm_out = keep.tile([P, 1], F32, name="warm_out")
-        nc.scalar.activation(out=warm_out[:], in_=warm[:], func=SIGMOID, scale=-1.0)
+        nc.scalar.activation(out=table_out[:], in_=table_in[:], func=SIGMOID, scale=-1.0)
         nc.sync.dma_start(out=raw[0][:, 2:4, :], in_=d_view[0][:, 2:4, :])
         nc.sync.dma_start(out=v_raw[0][:], in_=v_view[0])
         for quad in range(4):
             nc.sync.dma_start(out=e_s[32 * quad : 32 * quad + 4].bitcast(I32), in_=s_view[4 * quad : 4 * quad + 4].bitcast(I32))
         nc.sync.dma_start(out=e_w[:], in_=e_words.rearrange("g p n -> p g n"))
-        nc.sync.dma_start(out=v_raw[1][:], in_=v_view[1])
-        nc.sync.dma_start(out=raw[1][:, 0:2, :], in_=d_view[1][:, 0:2, :])
         nc.sync.dma_start(out=ipw_bf[:], in_=ipw.rearrange("(s m t) -> m s t", m=P, t=PACK))
+        nc.sync.dma_start(out=raw[1][:, 0:2, :], in_=d_view[1][:, 0:2, :])
+        nc.sync.dma_start(out=v_raw[1][:], in_=v_view[1])
         nc.sync.dma_start(out=raw[1][:, 2:4, :], in_=d_view[1][:, 2:4, :])
-        nc.sync.dma_start(out=raw[2][:], in_=d_view[2])
-        nc.sync.dma_start(out=raw[3][:], in_=d_view[3])
+        for s in range(2, GROUPS):
+            nc.sync.dma_start(out=raw[s][:], in_=d_view[s])
         for s in range(GROUPS):
             nc.sync.dma_start(out=dlt[s][:], in_=dlt_view[s])
 
         def spread_scales():
-            banks = []
             for g in range(PASSES):
                 bank = psum.tile([P, PACK, P], F32, name="bank")
                 for t in range(PACK):
                     nc.tensor.transpose(bank[:, t, :], scale_kp[:, g, t : t + 1].to_broadcast([P, P]), ident[:])
-                banks.append(bank)
-            return banks
-
-        def spread_out(banks):
-            for g in range(PASSES):
                 nc.scalar.copy(
-                    out=scale_bc[:, GROUP * g : GROUP * (g + 1)].rearrange("p (q t) -> p q t", t=PACK),
-                    in_=banks[g][:].rearrange("p t q -> p q t"),
+                    out=scale_row[:, GROUP * g : GROUP * (g + 1)].rearrange("p (q t) -> p q t", t=PACK),
+                    in_=bank[:].rearrange("p t q -> p q t"),
                 )
 
-        v_codes = [keep.tile([P, RANKERS], U32, name=f"v_codes{g}", align_bytes=64) for g in range(PASSES)]
-        v_planes = [keep.tile([P, RANKERS], U8, name=f"v_planes{g}", align_bytes=64) for g in range(PASSES)]
-        v_grp = [keep.tile([P, RANKERS, PACK], BF16, name=f"v_grp{g}", align_bytes=64) for g in range(PASSES)]
+        def interleave(copy, planes, grouped):
+            copy(out=grouped.rearrange("p (c i) t -> p c t i", i=4), in_=planes.rearrange("p t (c i) -> p c t i", i=4))
 
-        def v_interleave(g, part, parts, copy):
-            cols = slice(RANKERS // parts * part, RANKERS // parts * (part + 1))
-            copy(
-                out=v_grp[g][:, cols, :].rearrange("p (c i) t -> p c t i", i=4),
-                in_=v_raw[g][:, :, cols].rearrange("p t (c i) -> p c t i", i=4),
-            )
+        def quantize(codes, planes, grouped):
+            nc.vector.quantize_mx(out=codes.bitcast(E4M3X4), scales=planes, in_=grouped)
 
-        def v_quantize(g):
-            nc.vector.quantize_mx(
-                out=v_codes[g][:].bitcast(E4M3X4), scales=v_planes[g][:], in_=v_grp[g][:].rearrange("p n t -> p (n t)")
-            )
+        v_codes = keep.tile([P, PASSES * RANKERS], U32, name="v_codes", align_bytes=64)
+        v_planes = keep.tile([P, PASSES * RANKERS], U8, name="v_planes", align_bytes=64)
+        v_grp = keep.tile([P, PASSES * RANKERS, PACK], BF16, name="v_grp", align_bytes=64)
 
-        d_codes = [keep.tile([P, PASSES * P], U32, name=f"d_codes{j}", align_bytes=64) for j in range(TILES)]
-        d_planes = [keep.tile([P, PASSES * P], U8, name=f"d_planes{j}", align_bytes=64) for j in range(TILES)]
-        scaled, turned, grouped = {}, {}, {}
+        def v_interleave(g, first, stop):
+            interleave(nc.scalar.copy, v_raw[g][:, :, first:stop], v_grp[:, g * RANKERS + first : g * RANKERS + stop, :])
 
-        def widen(j):
-            scaled[j] = work.tile([P, RAW], BF16, name="scaled", bufs=5, align_bytes=64)
-            nc.vector.tensor_tensor(
-                out=scaled[j][:], in0=raw[j // PACK][:, j % PACK, :].bitcast(FP8), in1=scale_bc[:], op=MULT
-            )
+        def v_quantize():
+            quantize(v_codes[:], v_planes[:], v_grp[:].rearrange("p n t -> p (n t)"))
 
-        def widen_only(j, copy):
-            scaled[j] = work.tile([P, RAW], BF16, name="scaled", bufs=5, align_bytes=64)
-            copy(out=scaled[j][:], in_=raw[j // PACK][:, j % PACK, :].bitcast(FP8))
+        WORDS = PASSES * P
+        d_codes = [keep.tile([P, 2 * WORDS], U32, name=f"d_codes{p}", align_bytes=64) for p in range(STEPS)]
+        d_planes = [keep.tile([P, 2 * WORDS], U8, name=f"d_planes{p}", align_bytes=64) for p in range(STEPS)]
+        wide, turned, d_grp = {}, {}, {}
 
-        def scale_turned(j, g):
-            if g == 0:
-                grouped[j] = work.tile([P, PASSES * P * PACK], BF16, name="grouped", bufs=4, align_bytes=64)
-            if True:
-                nc.vector.tensor_tensor(
-                    out=grouped[j][:, 512 * g : 512 * (g + 1)].rearrange("p (r u e) -> p r u e", u=2, e=2),
-                    in0=turned[j][:, g].bitcast(BF16).rearrange("p u (r e) -> p r u e", e=2),
-                    in1=scale_kp[:, g : g + 1, :].rearrange("p o (u e) -> p o u e", e=2).to_broadcast([P, P, 2, 2]),
-                    op=MULT,
-                )
+        def d_bytes_of(j):
+            return raw[j // PACK][:, j % PACK, :].bitcast(FP8)
+
+        def d_grouped(j):
+            if j // 2 not in d_grp:
+                d_grp[j // 2] = work.tile([P, 2 * RAW], BF16, name="d_grp", bufs=2, align_bytes=64)
+            return d_grp[j // 2][:, RAW * (j % 2) : RAW * (j % 2 + 1)]
+
+        def widen_scaled(j):
+            wide[j] = work.tile([P, RAW], BF16, name="wide", bufs=5, align_bytes=64)
+            nc.vector.tensor_tensor(out=wide[j][:], in0=d_bytes_of(j), in1=scale_row[:], op=MULT)
+
+        def widen_plain(j, copy):
+            wide[j] = work.tile([P, RAW], BF16, name="wide", bufs=5, align_bytes=64)
+            copy(out=wide[j][:], in_=d_bytes_of(j))
 
         def turn(j):
             turned[j] = psum.tile([P, PASSES, 2, P], F32, name="bank")
-            words = scaled[j][:].bitcast(F32)
+            words = wide[j][:].bitcast(F32)
             for g in range(PASSES):
                 for u in range(2):
                     nc.tensor.transpose(turned[j][:, g, u, :], words[:, 256 * g + u : 256 * (g + 1) : 2], ident[:])
 
         def gather(j):
-            grouped[j] = work.tile([P, PASSES * P * PACK], BF16, name="grouped", bufs=4, align_bytes=64)
             nc.scalar.copy(
-                out=grouped[j][:].bitcast(F32).rearrange("p (g r u) -> p g r u", g=PASSES, u=2),
+                out=d_grouped(j).bitcast(F32).rearrange("p (g r u) -> p g r u", g=PASSES, u=2),
                 in_=turned[j][:].rearrange("p g u r -> p g r u"),
             )
 
-        def d_quantize(j):
-            nc.vector.quantize_mx(out=d_codes[j][:].bitcast(E4M3X4), scales=d_planes[j][:], in_=grouped[j][:])
+        def gather_scaled(j, g):
+            nc.vector.tensor_tensor(
+                out=d_grouped(j)[:, GROUP * g : GROUP * (g + 1)].rearrange("p (r u e) -> p r u e", u=2, e=2),
+                in0=turned[j][:, g].bitcast(BF16).rearrange("p u (r e) -> p r u e", e=2),
+                in1=scale_kp[:, g : g + 1, :].rearrange("p o (u e) -> p o u e", e=2).to_broadcast([P, P, 2, 2]),
+                op=MULT,
+            )
 
-        diff, encoded = {}, {}
-        sig, h_raw = {}, {}
+        def d_quantize_tile(j):
+            cols = slice(WORDS * (j % 2), WORDS * (j % 2 + 1))
+            quantize(d_codes[j // 2][:, cols], d_planes[j // 2][:, cols], d_grouped(j))
+
+        def d_quantize_step(p):
+            quantize(d_codes[p][:], d_planes[p][:], d_grp[p][:])
+
+        def times_d(j, bank, moving):
+            for g in range(PASSES):
+                cols = slice(WORDS * (j % 2) + g * P, WORDS * (j % 2) + (g + 1) * P)
+                codes, planes = moving(g)
+                nc.tensor.matmul_mx(
+                    out=bank[:], lhsT=d_codes[j // 2][:, cols].bitcast(E4M3X4), lhsT_scale=d_planes[j // 2][:, cols],
+                    rhs=codes, rhs_scale=planes, start=(g == 0), stop=(g == PASSES - 1),
+                )
+
+        encoded, sig, h_raw = {}, {}, {}
 
         def score(j):
-            diff[j] = psum.tile([P, RANKERS], F32, name="bank")
-            for g in range(PASSES):
-                cols = slice(g * P, (g + 1) * P)
-                nc.tensor.matmul_mx(
-                    out=diff[j][:], lhsT=d_codes[j][:, cols].bitcast(E4M3X4), lhsT_scale=d_planes[j][:, cols],
-                    rhs=v_codes[g][:].bitcast(E4M3X4), rhs_scale=v_planes[g][:], start=(g == 0), stop=(g == PASSES - 1),
-                )
-
-        def sigmoid(j):
             s, t = divmod(j, PACK)
+            diff = psum.tile([P, RANKERS], F32, name="bank")
+            times_d(j, diff, lambda g: (v_codes[:, g * RANKERS : (g + 1) * RANKERS].bitcast(E4M3X4), v_planes[:, g * RANKERS : (g + 1) * RANKERS]))
             if t == 0:
                 sig[s] = work.tile([P, PACK, RANKERS], F32, name="sig", bufs=3, align_bytes=64)
-            nc.scalar.activation(out=sig[s][:, t, :], in_=diff[j][:], func=SIGMOID, scale=-1.0)
+            nc.scalar.activation(out=sig[s][:, t, :], in_=diff[:], func=SIGMOID, scale=-1.0)
 
         def encode(j, half):
-            encoded[j, half] = psum.tile([P, 512], F32, name="bank")
-            for g in range(PASSES):
-                cols = slice(g * P, (g + 1) * P)
-                nc.tensor.matmul_mx(
-                    out=encoded[j, half][:], lhsT=d_codes[j][:, cols].bitcast(E4M3X4), lhsT_scale=d_planes[j][:, cols],
-                    rhs=e_w[:, g, 1024 * half : 1024 * (half + 1)].bitcast(E2M1X4), rhs_scale=e_s[:, g, 512 * half : 512 * (half + 1)],
-                    start=(g == 0), stop=(g == PASSES - 1),
-                )
+            encoded[j, half] = psum.tile([P, BANK], F32, name="bank")
+            times_d(j, encoded[j, half], lambda g: (e_w[:, g, 2 * BANK * half : 2 * BANK * (half + 1)].bitcast(E2M1X4), e_s[:, g, BANK * half : BANK * (half + 1)]))
 
         def weigh(j, half):
             s, t = divmod(j, PACK)
             if t == 0:
-                h_raw[s, half] = work.tile([P, PACK, 512], BF16, name=f"h_raw{half}", bufs=2 + 2 * half, align_bytes=64)
+                h_raw[s, half] = work.tile([P, PACK, BANK], BF16, name=f"h_raw{half}", bufs=(2, GROUPS)[half], align_bytes=64)
             nc.scalar.activation(out=h_raw[s, half][:, t, :], in_=encoded[j, half][:], func=COPY, scale=ipw_f[:, s, t : t + 1])
+
+        def encode_and_weigh(j, half):
+            encode(j, half)
+            weigh(j, half)
 
         lam_codes = [keep.tile([P, RANKERS], U32, name=f"lam_codes{s}", align_bytes=64) for s in range(GROUPS)]
         lam_planes = [keep.tile([P, RANKERS], U8, name=f"lam_planes{s}", align_bytes=64) for s in range(GROUPS)]
-        h_codes = {(s, h): keep.tile([P, 512], U32, name=f"h_codes{s}_{h}", align_bytes=64) for s in range(GROUPS) for h in range(HALVES)}
-        h_planes = {(s, h): keep.tile([P, 512], U8, name=f"h_planes{s}_{h}", align_bytes=64) for s in range(GROUPS) for h in range(HALVES)}
+        h_codes = [keep.tile([P, FEATS], U32, name=f"h_codes{s}", align_bytes=64) for s in range(GROUPS)]
+        h_planes = [keep.tile([P, FEATS], U8, name=f"h_planes{s}", align_bytes=64) for s in range(GROUPS)]
         lam, h_grp = {}, {}
 
-        def lam_mult(s, part, parts):
-            if part == 0:
+        def lam_multiply(s, first, stop):
+            if first == 0:
                 lam[s] = work.tile([P, RANKERS, PACK], BF16, name="lam", bufs=2, align_bytes=64)
-            cols = slice(RANKERS // parts * part, RANKERS // parts * (part + 1))
             nc.vector.tensor_tensor(
-                out=lam[s][:, cols, :].rearrange("p (c i) t -> p c t i", i=2),
-                in0=sig[s][:, :, cols].rearrange("p t (c i) -> p c t i", i=2),
-                in1=dlt[s][:, :, cols].rearrange("p t (c i) -> p c t i", i=2),
+                out=lam[s][:, first:stop, :].rearrange("p (c i) t -> p c t i", i=2),
+                in0=sig[s][:, :, first:stop].rearrange("p t (c i) -> p c t i", i=2),
+                in1=dlt[s][:, :, first:stop].rearrange("p t (c i) -> p c t i", i=2),
                 op=MULT,
             )
 
-        def lam_quantize(s, part, parts):
-            cols = slice(RANKERS // parts * part, RANKERS // parts * (part + 1))
-            nc.vector.quantize_mx(
-                out=lam_codes[s][:, cols].bitcast(E4M3X4), scales=lam_planes[s][:, cols],
-                in_=lam[s][:, cols, :].rearrange("p n t -> p (n t)"),
-            )
+        def lam_quantize(s, first, stop):
+            quantize(lam_codes[s][:, first:stop], lam_planes[s][:, first:stop], lam[s][:, first:stop, :].rearrange("p n t -> p (n t)"))
 
-        def h_interleave(s, piece, copy=nc.vector.tensor_copy):
-            half, cols = PIECES[piece][0], slice(*PIECES[piece][1:])
-            if cols.start == 0:
-                h_grp[s, half] = work.tile([P, 512, PACK], BF16, name=f"h_grp{half}", bufs=2 + 2 * half, align_bytes=64)
-            copy(
-                out=h_grp[s, half][:, cols, :].rearrange("p (c i) t -> p c t i", i=4),
-                in_=h_raw[s, half][:, :, cols].rearrange("p t (c i) -> p c t i", i=4),
-            )
+        def h_interleave(s, piece, copy):
+            first, stop = PIECES[piece]
+            half = first // BANK
+            h_grp[s, piece] = work.tile([P, stop - first, PACK], BF16, name=f"h_grp{piece}", bufs=(2, GROUPS, GROUPS)[piece], align_bytes=64)
+            interleave(copy, h_raw[s, half][:, :, first - BANK * half : stop - BANK * half], h_grp[s, piece][:])
 
         def h_quantize(s, piece):
-            half, cols = PIECES[piece][0], slice(*PIECES[piece][1:])
-            nc.vector.quantize_mx(
-                out=h_codes[s, half][:, cols].bitcast(E4M3X4), scales=h_planes[s, half][:, cols],
-                in_=h_grp[s, half][:, cols, :].rearrange("p n t -> p (n t)"),
-            )
+            first, stop = PIECES[piece]
+            quantize(h_codes[s][:, first:stop], h_planes[s][:, first:stop], h_grp[s, piece][:].rearrange("p n t -> p (n t)"))
 
-        acc, summed = {}, {}
+        sums = {}
 
         def open_sums(piece):
             for m in range(QTILES):
-                acc[piece, m] = psum.tile([P, 512], F32, name="bank")
+                sums[piece, m] = psum.tile([P, PIECES[piece][1] - PIECES[piece][0]], F32, name="bank")
 
         def update(s, piece, m):
-            half, cols = PIECES[piece][0], slice(*PIECES[piece][1:])
-            summed[piece, m] = summed.get((piece, m), 0) + 1
+            first, stop = PIECES[piece]
             rows = slice(m * P, (m + 1) * P)
             nc.tensor.matmul_mx(
-                out=acc[piece, m][:, : cols.stop - cols.start], lhsT=lam_codes[s][:, rows].bitcast(E4M3X4), lhsT_scale=lam_planes[s][:, rows],
-                rhs=h_codes[s, half][:, cols].bitcast(E4M3X4), rhs_scale=h_planes[s, half][:, cols],
-                start=(summed[piece, m] == 1), stop=(summed[piece, m] == GROUPS),
+                out=sums[piece, m][:], lhsT=lam_codes[s][:, rows].bitcast(E4M3X4), lhsT_scale=lam_planes[s][:, rows],
+                rhs=h_codes[s][:, first:stop].bitcast(E4M3X4), rhs_scale=h_planes[s][:, first:stop],
+                start=(s == 0), stop=(s == GROUPS - 1),
             )
 
-        def store(piece, m, engine):
-            half, first, stop = PIECES[piece]
-            width = stop - first
-            res = work.tile([P, width], F32, name=f"res{piece}", bufs=QTILES)
-            if engine == "scalar":
-                nc.scalar.copy(out=res[:, :width], in_=acc[piece, m][:, :width])
-            else:
-                nc.vector.tensor_copy(out=res[:, :width], in_=acc[piece, m][:, :width])
-            nc.sync.dma_start(out=out[m * P : (m + 1) * P, 512 * half + first : 512 * half + stop], in_=res[:, :width])
+        def store(piece, m, copy):
+            first, stop = PIECES[piece]
+            res = work.tile([P, stop - first], F32, name=f"res{piece}", bufs=QTILES)
+            copy(out=res[:], in_=sums[piece, m][:])
+            nc.sync.dma_start(out=out[m * P : (m + 1) * P, first:stop], in_=res[:])
 
+        on_vector, on_scalar = nc.vector.tensor_copy, nc.scalar.copy
         last = GROUPS - 1
 
-        def encode_tile(j):
-            for half in range(HALVES):
-                encode(j, half)
-                weigh(j, half)
-
-        def score_tile(j):
-            score(j)
-            sigmoid(j)
-
-        def turn_tile(j):
-            turn(j)
-            gather(j)
-
-        def group_work(s):
-            ready = 2 * s + 4
-            return [(ready, lam_mult, (s, 0, 2)), (ready, lam_mult, (s, 1, 2)), (ready, h_interleave, (s + 1, 0)), (ready, lam_quantize, (s, 0, 1)), (ready, h_quantize, (s + 1, 0))]
-
         for j in range(PACK):
-            widen_only(j, nc.scalar.copy if j % 2 else nc.vector.tensor_copy)
+            widen_plain(j, on_scalar if j % 2 else on_vector)
         turn(0)
-        turn(1)
-        v_interleave(0, 0, 2, nc.scalar.copy)
-        spread_out(spread_scales())
-        turn(2)
-        turn(3)
-        for part in range(1, 3):
-            v_interleave(part // 2, part % 2, 2, nc.scalar.copy)
+        spread_scales()
+        for j in range(1, PACK):
+            turn(j)
+        v_interleave(0, 0, RANKERS - P)
         nc.scalar.copy(out=ipw_f[:], in_=ipw_bf[:])
-        v_interleave(1, 1, 2, nc.scalar.copy)
+        v_interleave(0, RANKERS - P, RANKERS)
         for j in range(PACK):
-            scale_turned(j, 0)
+            gather_scaled(j, 0)
             if j > 0:
-                d_quantize(j - 1)
-            scale_turned(j, 1)
-        widen(4)
-        d_quantize(3)
-        widen(5)
-        widen(6)
-        encode_tile(0)
+                d_quantize_tile(j - 1)
+            gather_scaled(j, 1)
+        widen_scaled(4)
+        d_quantize_tile(3)
+        widen_scaled(5)
+        widen_scaled(6)
+        for half in range(HALVES):
+            encode_and_weigh(0, half)
+        v_interleave(1, 0, RANKERS)
         for j in (1, 2):
             for half in range(HALVES):
                 encode(j, half)
@@ -322,108 +275,109 @@ def tile_lambdarank_head_gradient_s11_kernel(tc, d_bytes, d_scale, v, delta, ipw
         weigh(1, 1)
         for half in range(HALVES):
             encode(3, half)
-        turn_tile(5)
-        for j in (2, 3):
-            for half in range(HALVES):
-                weigh(j, half)
-        d_quantize(4)
-        widen(7)
-        d_quantize(5)
-        v_quantize(0)
-        v_quantize(1)
-        encode_tile(4)
-        turn(6)
-        turn(7)
-        gather(6)
-        gather(7)
-        encode_tile(5)
-        score_tile(0)
-        score_tile(1)
-        widen(8)
-        widen(9)
-        d_quantize(6)
-        d_quantize(7)
+        turn(5)
+        weigh(2, 0)
+        gather(5)
+        weigh(2, 1)
+        for half in range(HALVES):
+            weigh(3, half)
+        d_quantize_tile(4)
+        widen_scaled(7)
+        d_quantize_tile(5)
+        v_quantize()
+        for half in range(HALVES):
+            encode(4, half)
+        for j in (6, 7):
+            turn(j)
+        for j in (6, 7):
+            gather(j)
+        for half in range(HALVES):
+            weigh(4, half)
+        for half in range(HALVES):
+            encode_and_weigh(5, half)
+        score(0)
+        score(1)
+        widen_scaled(8)
+        widen_scaled(9)
+        d_quantize_step(3)
 
-        waiting = []
+        middle = RANKERS // 2
+        queue = [(3, h_interleave, (0, 0, on_vector)), (3, h_quantize, (0, 0))]
         for s in range(last - 1):
-            waiting += group_work(s)
-        waiting += [(STEPS - 1, h_interleave, (last, 0))]
-        waiting = [(3, h_interleave, (0, 0)), (3, h_quantize, (0, 0))] + waiting
-        scored = HEAD_SCORES
-        done = []
+            ready = 2 * s + 4
+            queue += [(ready, lam_multiply, (s, 0, middle)), (ready, lam_multiply, (s, middle, RANKERS)), (ready, h_interleave, (s + 1, 0, on_vector)),
+                      (ready, lam_quantize, (s, 0, RANKERS)), (ready, h_quantize, (s + 1, 0))]
+        queue += [(STEPS - 1, h_interleave, (last, 0, on_vector))]
         for p in range(3, STEPS):
-            if True:
-                if p + 1 < STEPS:
-                    turn(2 * p + 2)
-                    turn(2 * p + 3)
-                    gather(2 * p + 2)
-                    gather(2 * p + 3)
-                for j in (2 * p, 2 * p + 1):
-                    encode(j, 0)
-                    weigh(j, 0)
-                    score_tile(scored)
-                    scored += 1
-                    if j < TILES - DEFER:
-                        encode(j, 1)
-                        weigh(j, 1)
-            room = ROOM
-            if p + 2 < STEPS:
-                widen(2 * p + 4)
-                widen(2 * p + 5)
-                room = WROOM
-            todo = []
-            while len(todo) < room and waiting and waiting[0][0] <= p and (waiting[0][1] is not lam_mult or scored >= PACK * waiting[0][2][0] + PACK):
-                todo.append(waiting.pop(0))
+            ahead = (2 * p + 2, 2 * p + 3)
             if p + 1 < STEPS:
-                first = BEFORE if p + 2 < STEPS else BEFORE_LAST
-                todo[first:first] = [(p, d_quantize, (2 * p + 2,)), (p, d_quantize, (2 * p + 3,))]
+                for j in ahead:
+                    turn(j)
+                for j in ahead:
+                    gather(j)
+            for j in (2 * p, 2 * p + 1):
+                encode_and_weigh(j, 0)
+                score(j - SCORE_LAG)
+                if j < last * PACK:
+                    encode_and_weigh(j, 1)
+            if p + 2 < STEPS:
+                widen_scaled(2 * p + 4)
+                widen_scaled(2 * p + 5)
+            room = 2 if p + 2 < STEPS else 5
+            todo = [item for item in queue[:room] if item[0] <= p]
+            queue = queue[len(todo) :]
+            if p + 1 < STEPS:
+                place = 1 if p + 2 < STEPS else PLACE
+                todo = todo[:place] + [(p, d_quantize_step, (p + 1,))] + todo[place:]
             for ready, fn, args in todo:
                 fn(*args)
-        for j in range(scored, TILES):
-            score_tile(j)
-        for j in range(TILES - DEFER, TILES):
-            encode(j, 1)
-            weigh(j, 1)
-        late = (last - 1, last)
+        for j in range(TILES - SCORE_LAG, TILES):
+            score(j)
+        for j in range(last * PACK, TILES):
+            encode_and_weigh(j, 1)
+
         open_sums(0)
         open_sums(1)
         for s in range(FIRST):
-            h_interleave(s, 1, nc.scalar.copy)
-        for ready, fn, args in waiting:
+            h_interleave(s, 1, on_scalar)
+        for ready, fn, args in queue:
             fn(*args)
-        lam_mult(late[0], 0, QTILES)
+        lam_multiply(last - 1, 0, P)
         h_quantize(last, 0)
         for m in range(QTILES):
-            lam_mult(late[1], m, QTILES)
-            lam_quantize(late[0], m, QTILES)
+            first, stop = m * P, (m + 1) * P
+            lam_multiply(last, first, stop)
+            lam_quantize(last - 1, first, stop)
             if m + 1 < QTILES:
-                lam_mult(late[0], m + 1, QTILES)
+                lam_multiply(last - 1, stop, stop + P)
             else:
                 h_quantize(last - 1, 1)
-            lam_quantize(late[1], m, QTILES)
+            lam_quantize(last, first, stop)
             for s in range(GROUPS):
                 update(s, 0, m)
-            store(0, m, "scalar")
+            store(0, m, on_scalar)
             if FIRST + m < GROUPS:
-                h_interleave(FIRST + m, 1, nc.scalar.copy)
+                h_interleave(FIRST + m, 1, on_scalar)
             if 1 <= m < last:
                 h_quantize(m - 1, 1)
                 for n in range(QTILES):
                     update(m - 1, 1, n)
         open_sums(2)
-        h_interleave(0, 2)
-        h_interleave(1, 2)
+        h_interleave(last - 1, 2, on_scalar)
+        h_interleave(0, 2, on_vector)
         h_quantize(last, 1)
-        for s in late:
+        for s in (last - 1, last):
             for m in range(QTILES):
                 update(s, 1, m)
         for m in range(QTILES):
-            store(1, m, "scalar")
+            store(1, m, on_scalar)
+        h_interleave(1, 2, on_vector)
+        h_quantize(0, 2)
+        h_interleave(last, 2, on_vector)
         for s in range(GROUPS):
-            h_quantize(s, 2)
-            if s + 2 < GROUPS:
-                h_interleave(s + 2, 2)
+            if s > 0:
+                h_quantize(s, 2)
             for m in range(QTILES):
                 update(s, 2, m)
         for m in range(QTILES):
-            store(2, m, "vector" if m % 2 == 0 else "scalar")
+            store(2, m, on_scalar if m % 2 else on_vector)

@@ -95,7 +95,7 @@ def tile_lambdarank_head_gradient_s11_kernel(tc, d_bytes, d_scale, v, delta, ipw
                 )
 
         def interleave(copy, planes, grouped):
-            copy(out=grouped.rearrange("p (c i) t -> p c t i", i=4), in_=planes.rearrange("p t (c i) -> p c t i", i=4))
+            copy(out=grouped.rearrange("p (c i) t -> p c t i", i=8), in_=planes.rearrange("p t (c i) -> p c t i", i=8))
 
         def quantize(codes, planes, grouped):
             nc.vector.quantize_mx(out=codes.bitcast(E4M3X4), scales=planes, in_=grouped)
@@ -104,8 +104,8 @@ def tile_lambdarank_head_gradient_s11_kernel(tc, d_bytes, d_scale, v, delta, ipw
         v_planes = keep.tile([P, PASSES * RANKERS], U8, name="v_planes", align_bytes=64)
         v_grp = keep.tile([P, PASSES * RANKERS, PACK], BF16, name="v_grp", align_bytes=64)
 
-        def v_interleave(g, first, stop):
-            interleave(nc.scalar.copy, v_raw[g][:, :, first:stop], v_grp[:, g * RANKERS + first : g * RANKERS + stop, :])
+        def v_interleave(g, first, stop, copy=nc.scalar.copy):
+            interleave(copy, v_raw[g][:, :, first:stop], v_grp[:, g * RANKERS + first : g * RANKERS + stop, :])
 
         def v_quantize():
             quantize(v_codes[:], v_planes[:], v_grp[:].rearrange("p n t -> p (n t)"))
@@ -265,7 +265,7 @@ def tile_lambdarank_head_gradient_s11_kernel(tc, d_bytes, d_scale, v, delta, ipw
         widen_scaled(6)
         for half in range(HALVES):
             encode_and_weigh(0, half)
-        v_interleave(1, 0, RANKERS)
+        v_interleave(1, 0, RANKERS // 2)
         for j in (1, 2):
             for half in range(HALVES):
                 encode(j, half)
@@ -283,6 +283,7 @@ def tile_lambdarank_head_gradient_s11_kernel(tc, d_bytes, d_scale, v, delta, ipw
             weigh(3, half)
         d_quantize_tile(4)
         widen_scaled(7)
+        v_interleave(1, RANKERS // 2, RANKERS, on_vector)
         d_quantize_tile(5)
         v_quantize()
         for half in range(HALVES):
@@ -307,7 +308,7 @@ def tile_lambdarank_head_gradient_s11_kernel(tc, d_bytes, d_scale, v, delta, ipw
             ready = 2 * s + 4
             queue += [(ready, lam_multiply, (s, 0, middle)), (ready, lam_multiply, (s, middle, RANKERS)), (ready, h_interleave, (s + 1, 0, on_vector)),
                       (ready, lam_quantize, (s, 0, RANKERS)), (ready, h_quantize, (s + 1, 0))]
-        queue += [(STEPS - 1, h_interleave, (last, 0, on_vector))]
+        queue += [(STEPS - 1, h_interleave, (0, 2, on_vector)), (STEPS - 1, h_interleave, (last, 0, on_vector))]
         for p in range(3, STEPS):
             ahead = (2 * p + 2, 2 * p + 3)
             if p + 1 < STEPS:
@@ -363,20 +364,17 @@ def tile_lambdarank_head_gradient_s11_kernel(tc, d_bytes, d_scale, v, delta, ipw
                 for n in range(QTILES):
                     update(m - 1, 1, n)
         open_sums(2)
-        h_interleave(last - 1, 2, on_scalar)
-        h_interleave(0, 2, on_vector)
+        h_interleave(1, 2, on_vector)
         h_quantize(last, 1)
         for s in (last - 1, last):
             for m in range(QTILES):
                 update(s, 1, m)
         for m in range(QTILES):
             store(1, m, on_scalar)
-        h_interleave(1, 2, on_vector)
-        h_quantize(0, 2)
-        h_interleave(last, 2, on_vector)
         for s in range(GROUPS):
-            if s > 0:
-                h_quantize(s, 2)
+            h_quantize(s, 2)
+            if s + 2 < GROUPS:
+                h_interleave(s + 2, 2, on_vector)
             for m in range(QTILES):
                 update(s, 2, m)
         for m in range(QTILES):

@@ -12,6 +12,7 @@ FP8 = mybir.dt.float8_e4m3fn
 E4M3X4 = mybir.dt.float8_e4m3fn_x4
 E2M1X4 = mybir.dt.float4_e2m1fn_x4
 MULT = mybir.AluOpType.mult
+ADD = mybir.AluOpType.add
 COPY = mybir.ActivationFunctionType.Copy
 SIGMOID = mybir.ActivationFunctionType.Sigmoid
 
@@ -27,10 +28,10 @@ TILES = PAIRS // P
 STEPS = TILES // 2
 QTILES = RANKERS // P
 BANKS = 8
-PIECES = ((0, 512), (512, 768), (768, 1024))
-SCORE_LAG = 4
-FIRST = 3
-PLACE = 2
+CHUNK = 256
+CHUNKS = FEATS // CHUNK
+
+GRPBUFS = 8
 
 FLOPS = 2 * PAIRS * RAW * RANKERS + 2 * PAIRS * RAW * FEATS + 2 * RANKERS * PAIRS * FEATS
 
@@ -48,11 +49,10 @@ def tile_lambdarank_head_gradient_s11_kernel(tc, d_bytes, d_scale, v, delta, ipw
         ctx.enter_context(tc.manual_schedule())
 
         scale_kp = keep.tile([P, PASSES, PACK], F32, name="scale_kp")
-        scale_row = keep.tile([P, RAW], F32, name="scale_row", align_bytes=64)
         raw = [keep.tile([P, PACK, RAW], U8, name=f"raw{s}", align_bytes=64) for s in range(GROUPS)]
         dlt = [keep.tile([P, PACK, RANKERS], BF16, name=f"dlt{s}", align_bytes=64) for s in range(GROUPS)]
         v_raw = [keep.tile([P, PACK, RANKERS], BF16, name=f"v_raw{g}", align_bytes=64) for g in range(PASSES)]
-        e_w = keep.tile([P, PASSES, 2 * FEATS], U8, name="e_w", align_bytes=64)
+        e_w = [keep.tile([P, PASSES, 2 * BANK], U8, name=f"e_w{h}", align_bytes=64) for h in range(HALVES)]
         e_s = keep.tile([P, PASSES, FEATS], U8, name="e_s", align_bytes=64)
         ipw_bf = keep.tile([P, GROUPS, PACK], BF16, name="ipw_bf")
         ipw_f = keep.tile([P, GROUPS, PACK], F32, name="ipw_f")
@@ -60,104 +60,105 @@ def tile_lambdarank_head_gradient_s11_kernel(tc, d_bytes, d_scale, v, delta, ipw
         d_view = d_bytes.rearrange("(s m t) k -> s m t k", m=P, t=PACK)
         dlt_view = delta.rearrange("(s m t) q -> s m t q", m=P, t=PACK)
         v_view = v.rearrange("(g p t) n -> g p t n", p=P, t=PACK)
+        w_view = e_words.rearrange("g p n -> p g n")
         s_view = e_scales.rearrange("g r n -> r g n")
 
-        nc.vector.memset(e_s[:].bitcast(I32), 0)
         table_in = keep.tile([P, 1], F32, name="table_in")
         table_out = keep.tile([P, 1], F32, name="table_out")
         nc.vector.memset(table_in[:], 0.0)
+        nc.vector.memset(e_s[:].bitcast(I32), 0)
 
-        nc.sync.dma_start(out=raw[0][:, 0:2, :], in_=d_view[0][:, 0:2, :])
-        nc.scalar.dma_start(out=scale_kp[:], in_=d_scale.rearrange("o (g p t) -> p (o g) t", p=P, t=PACK))
-        nc.scalar.activation(out=table_out[:], in_=table_in[:], func=SIGMOID, scale=-1.0)
-        nc.sync.dma_start(out=raw[0][:, 2:4, :], in_=d_view[0][:, 2:4, :])
-        nc.sync.dma_start(out=v_raw[0][:], in_=v_view[0])
-        for quad in range(4):
-            nc.sync.dma_start(out=e_s[32 * quad : 32 * quad + 4].bitcast(I32), in_=s_view[4 * quad : 4 * quad + 4].bitcast(I32))
-        nc.sync.dma_start(out=e_w[:], in_=e_words.rearrange("g p n -> p g n"))
-        nc.sync.dma_start(out=ipw_bf[:], in_=ipw.rearrange("(s m t) -> m s t", m=P, t=PACK))
-        nc.sync.dma_start(out=raw[1][:, 0:2, :], in_=d_view[1][:, 0:2, :])
-        nc.sync.dma_start(out=v_raw[1][:], in_=v_view[1])
-        nc.sync.dma_start(out=raw[1][:, 2:4, :], in_=d_view[1][:, 2:4, :])
-        for s in range(2, GROUPS):
-            nc.sync.dma_start(out=raw[s][:], in_=d_view[s])
-        for s in range(GROUPS):
+        def load_raw(s, first, stop):
+            nc.sync.dma_start(out=raw[s][:, first:stop, :], in_=d_view[s][:, first:stop, :])
+
+        def load_words(h):
+            nc.sync.dma_start(out=e_w[h][:], in_=w_view[:, :, 2 * BANK * h : 2 * BANK * (h + 1)])
+
+        def load_scales():
+            for r in range(PACK):
+                nc.sync.dma_start(out=e_s[r:P:32].bitcast(I32), in_=s_view[r:16:PACK].bitcast(I32))
+
+        def load_v(g):
+            nc.sync.dma_start(out=v_raw[g][:], in_=v_view[g])
+
+        def load_dlt(s):
             nc.sync.dma_start(out=dlt[s][:], in_=dlt_view[s])
 
-        def spread_scales():
-            for g in range(PASSES):
-                bank = psum.tile([P, PACK, P], F32, name="bank")
-                for t in range(PACK):
-                    nc.tensor.transpose(bank[:, t, :], scale_kp[:, g, t : t + 1].to_broadcast([P, P]), ident[:])
-                nc.scalar.copy(
-                    out=scale_row[:, GROUP * g : GROUP * (g + 1)].rearrange("p (q t) -> p q t", t=PACK),
-                    in_=bank[:].rearrange("p t q -> p q t"),
-                )
+        def load_ipw():
+            nc.sync.dma_start(out=ipw_bf[:], in_=ipw.rearrange("(s m t) -> m s t", m=P, t=PACK))
+
+        def on_vector(out, in_):
+            nc.vector.tensor_copy(out=out, in_=in_)
+
+        def on_scalar(out, in_):
+            nc.scalar.copy(out=out, in_=in_)
+
+        def on_gpsimd(out, in_):
+            nc.gpsimd.tensor_scalar(out=out, in0=in_, scalar1=1.0, scalar2=0.0, op0=MULT, op1=ADD)
 
         def interleave(copy, planes, grouped):
-            copy(out=grouped.rearrange("p (c i) t -> p c t i", i=8), in_=planes.rearrange("p t (c i) -> p c t i", i=8))
+            if copy is on_gpsimd:
+                copy(grouped, planes.rearrange("p t n -> p n t"))
+            else:
+                copy(grouped.rearrange("p (c i) t -> p c t i", i=8), planes.rearrange("p t (c i) -> p c t i", i=8))
 
         def quantize(codes, planes, grouped):
             nc.vector.quantize_mx(out=codes.bitcast(E4M3X4), scales=planes, in_=grouped)
 
+        def grouped_tile(copy, width, slot=False):
+            if copy is on_gpsimd or slot:
+                return work.tile([P, width, PACK], BF16, name="g_grp", bufs=1, align_bytes=64)
+            return work.tile([P, width, PACK], BF16, name="grp", bufs=GRPBUFS, align_bytes=64)
+
         v_codes = keep.tile([P, PASSES * RANKERS], U32, name="v_codes", align_bytes=64)
         v_planes = keep.tile([P, PASSES * RANKERS], U8, name="v_planes", align_bytes=64)
-        v_grp = keep.tile([P, PASSES * RANKERS, PACK], BF16, name="v_grp", align_bytes=64)
+        v_grp = {}
 
-        def v_interleave(g, first, stop, copy=nc.scalar.copy):
-            interleave(copy, v_raw[g][:, :, first:stop], v_grp[:, g * RANKERS + first : g * RANKERS + stop, :])
+        def v_interleave(c, copy, slot=False):
+            g, first = divmod(c * CHUNK, RANKERS)
+            v_grp[c] = grouped_tile(copy, CHUNK, slot)
+            interleave(copy, v_raw[g][:, :, first : first + CHUNK], v_grp[c][:])
 
-        def v_quantize():
-            quantize(v_codes[:], v_planes[:], v_grp[:].rearrange("p n t -> p (n t)"))
+        def v_quantize(c):
+            cols = slice(c * CHUNK, (c + 1) * CHUNK)
+            quantize(v_codes[:, cols], v_planes[:, cols], v_grp[c][:].rearrange("p n t -> p (n t)"))
 
         WORDS = PASSES * P
         d_codes = [keep.tile([P, 2 * WORDS], U32, name=f"d_codes{p}", align_bytes=64) for p in range(STEPS)]
         d_planes = [keep.tile([P, 2 * WORDS], U8, name=f"d_planes{p}", align_bytes=64) for p in range(STEPS)]
         wide, turned, d_grp = {}, {}, {}
 
-        def d_bytes_of(j):
-            return raw[j // PACK][:, j % PACK, :].bitcast(FP8)
+        def widen(j, copy=on_scalar, first=0, stop=RAW):
+            if first == 0:
+                wide[j] = work.tile([P, RAW], BF16, name="wide", bufs=4, align_bytes=64)
+            copy(wide[j][:, first:stop], raw[j // PACK][:, j % PACK, first:stop].bitcast(FP8))
+
+        def turn(j, first=0, stop=PASSES):
+            bank = psum.tile([P, 2, PASSES, P], F32, name="bank")
+            words = wide[j][:].bitcast(F32)
+            for g in range(first, stop):
+                turned[j, g] = bank
+                for u in range(2):
+                    nc.tensor.transpose(bank[:, u, g, :], words[:, 256 * g + u : 256 * (g + 1) : 2], ident[:])
 
         def d_grouped(j):
             if j // 2 not in d_grp:
                 d_grp[j // 2] = work.tile([P, 2 * RAW], BF16, name="d_grp", bufs=2, align_bytes=64)
             return d_grp[j // 2][:, RAW * (j % 2) : RAW * (j % 2 + 1)]
 
-        def widen_scaled(j):
-            wide[j] = work.tile([P, RAW], BF16, name="wide", bufs=5, align_bytes=64)
-            nc.vector.tensor_tensor(out=wide[j][:], in0=d_bytes_of(j), in1=scale_row[:], op=MULT)
-
-        def widen_plain(j, copy):
-            wide[j] = work.tile([P, RAW], BF16, name="wide", bufs=5, align_bytes=64)
-            copy(out=wide[j][:], in_=d_bytes_of(j))
-
-        def turn(j):
-            turned[j] = psum.tile([P, PASSES, 2, P], F32, name="bank")
-            words = wide[j][:].bitcast(F32)
-            for g in range(PASSES):
-                for u in range(2):
-                    nc.tensor.transpose(turned[j][:, g, u, :], words[:, 256 * g + u : 256 * (g + 1) : 2], ident[:])
-
-        def gather(j):
-            nc.scalar.copy(
-                out=d_grouped(j).bitcast(F32).rearrange("p (g r u) -> p g r u", g=PASSES, u=2),
-                in_=turned[j][:].rearrange("p g u r -> p g r u"),
-            )
-
-        def gather_scaled(j, g):
+        def scale(j, first=0, stop=PASSES):
+            n = stop - first
             nc.vector.tensor_tensor(
-                out=d_grouped(j)[:, GROUP * g : GROUP * (g + 1)].rearrange("p (r u e) -> p r u e", u=2, e=2),
-                in0=turned[j][:, g].bitcast(BF16).rearrange("p u (r e) -> p r u e", e=2),
-                in1=scale_kp[:, g : g + 1, :].rearrange("p o (u e) -> p o u e", e=2).to_broadcast([P, P, 2, 2]),
+                out=d_grouped(j)[:, GROUP * first : GROUP * stop].rearrange("p (g r u e) -> p g r u e", g=n, u=2, e=2),
+                in0=turned[j, first][:, :, first:stop, :].bitcast(BF16).rearrange("p u g (r e) -> p g r u e", e=2),
+                in1=scale_kp[:, first:stop, :].rearrange("p g (o u e) -> p g o u e", o=1, e=2).to_broadcast([P, n, P, 2, 2]),
                 op=MULT,
             )
 
-        def d_quantize_tile(j):
-            cols = slice(WORDS * (j % 2), WORDS * (j % 2 + 1))
-            quantize(d_codes[j // 2][:, cols], d_planes[j // 2][:, cols], d_grouped(j))
-
-        def d_quantize_step(p):
-            quantize(d_codes[p][:], d_planes[p][:], d_grp[p][:])
+        def d_quantize(first, stop):
+            p = first // (2 * PASSES)
+            lo, hi = first - 2 * PASSES * p, stop - 2 * PASSES * p
+            quantize(d_codes[p][:, P * lo : P * hi], d_planes[p][:, P * lo : P * hi], d_grp[p][:, GROUP * lo : GROUP * hi])
 
         def times_d(j, bank, moving):
             for g in range(PASSES):
@@ -168,7 +169,7 @@ def tile_lambdarank_head_gradient_s11_kernel(tc, d_bytes, d_scale, v, delta, ipw
                     rhs=codes, rhs_scale=planes, start=(g == 0), stop=(g == PASSES - 1),
                 )
 
-        encoded, sig, h_raw = {}, {}, {}
+        sig, h_raw = {}, {}
 
         def score(j):
             s, t = divmod(j, PACK)
@@ -179,18 +180,12 @@ def tile_lambdarank_head_gradient_s11_kernel(tc, d_bytes, d_scale, v, delta, ipw
             nc.scalar.activation(out=sig[s][:, t, :], in_=diff[:], func=SIGMOID, scale=-1.0)
 
         def encode(j, half):
-            encoded[j, half] = psum.tile([P, BANK], F32, name="bank")
-            times_d(j, encoded[j, half], lambda g: (e_w[:, g, 2 * BANK * half : 2 * BANK * (half + 1)].bitcast(E2M1X4), e_s[:, g, BANK * half : BANK * (half + 1)]))
-
-        def weigh(j, half):
             s, t = divmod(j, PACK)
+            encoded = psum.tile([P, BANK], F32, name="bank")
+            times_d(j, encoded, lambda g: (e_w[half][:, g, :].bitcast(E2M1X4), e_s[:, g, BANK * half : BANK * (half + 1)]))
             if t == 0:
                 h_raw[s, half] = work.tile([P, PACK, BANK], BF16, name=f"h_raw{half}", bufs=(2, GROUPS)[half], align_bytes=64)
-            nc.scalar.activation(out=h_raw[s, half][:, t, :], in_=encoded[j, half][:], func=COPY, scale=ipw_f[:, s, t : t + 1])
-
-        def encode_and_weigh(j, half):
-            encode(j, half)
-            weigh(j, half)
+            nc.scalar.activation(out=h_raw[s, half][:, t, :], in_=encoded[:], func=COPY, scale=ipw_f[:, s, t : t + 1])
 
         lam_codes = [keep.tile([P, RANKERS], U32, name=f"lam_codes{s}", align_bytes=64) for s in range(GROUPS)]
         lam_planes = [keep.tile([P, RANKERS], U8, name=f"lam_planes{s}", align_bytes=64) for s in range(GROUPS)]
@@ -211,171 +206,134 @@ def tile_lambdarank_head_gradient_s11_kernel(tc, d_bytes, d_scale, v, delta, ipw
         def lam_quantize(s, first, stop):
             quantize(lam_codes[s][:, first:stop], lam_planes[s][:, first:stop], lam[s][:, first:stop, :].rearrange("p n t -> p (n t)"))
 
-        def h_interleave(s, piece, copy):
-            first, stop = PIECES[piece]
-            half = first // BANK
-            h_grp[s, piece] = work.tile([P, stop - first, PACK], BF16, name=f"h_grp{piece}", bufs=(2, GROUPS, GROUPS)[piece], align_bytes=64)
-            interleave(copy, h_raw[s, half][:, :, first - BANK * half : stop - BANK * half], h_grp[s, piece][:])
+        def h_interleave(s, c, copy, n=1):
+            half, first = divmod(c * CHUNK, BANK)
+            h_grp[s, c] = grouped_tile(copy, n * CHUNK)
+            interleave(copy, h_raw[s, half][:, :, first : first + n * CHUNK], h_grp[s, c][:])
 
-        def h_quantize(s, piece):
-            first, stop = PIECES[piece]
-            quantize(h_codes[s][:, first:stop], h_planes[s][:, first:stop], h_grp[s, piece][:].rearrange("p n t -> p (n t)"))
+        def h_quantize(s, c, n=1):
+            cols = slice(c * CHUNK, (c + n) * CHUNK)
+            quantize(h_codes[s][:, cols], h_planes[s][:, cols], h_grp[s, c][:].rearrange("p n t -> p (n t)"))
 
         sums = {}
 
-        def open_sums(piece):
-            for m in range(QTILES):
-                sums[piece, m] = psum.tile([P, PIECES[piece][1] - PIECES[piece][0]], F32, name="bank")
-
-        def update(s, piece, m):
-            first, stop = PIECES[piece]
+        def update(s, m, first, stop):
+            if s == 0:
+                sums[m, first] = psum.tile([P, stop - first], F32, name="bank")
             rows = slice(m * P, (m + 1) * P)
             nc.tensor.matmul_mx(
-                out=sums[piece, m][:], lhsT=lam_codes[s][:, rows].bitcast(E4M3X4), lhsT_scale=lam_planes[s][:, rows],
+                out=sums[m, first][:], lhsT=lam_codes[s][:, rows].bitcast(E4M3X4), lhsT_scale=lam_planes[s][:, rows],
                 rhs=h_codes[s][:, first:stop].bitcast(E4M3X4), rhs_scale=h_planes[s][:, first:stop],
                 start=(s == 0), stop=(s == GROUPS - 1),
             )
 
-        def store(piece, m, copy):
-            first, stop = PIECES[piece]
-            res = work.tile([P, stop - first], F32, name=f"res{piece}", bufs=QTILES)
-            copy(out=res[:], in_=sums[piece, m][:])
+        def store(m, first, stop, copy):
+            res = work.tile([P, stop - first], F32, name=f"res{first}_{stop}", bufs=QTILES)
+            copy(res[:], sums[m, first][:])
             nc.sync.dma_start(out=out[m * P : (m + 1) * P, first:stop], in_=res[:])
 
-        on_vector, on_scalar = nc.vector.tensor_copy, nc.scalar.copy
-        last = GROUPS - 1
+        load_raw(0, 0, 1)
+        nc.scalar.dma_start(out=scale_kp[:], in_=d_scale.rearrange("o (g p t) -> p (o g) t", p=P, t=PACK))
+        nc.scalar.activation(out=table_out[:], in_=table_in[:], func=SIGMOID, scale=-1.0)
+        load_raw(0, 1, 2)
+        load_raw(0, 2, 4)
+        load_scales()
+        load_words(0)
+        load_ipw()
+        load_words(1)
+        load_raw(1, 0, 2)
+        load_v(0)
+        load_v(1)
+        load_raw(1, 2, 4)
+        load_raw(2, 0, 4)
+        load_dlt(0)
+        load_raw(3, 0, 4)
+        for s in range(1, GROUPS):
+            load_dlt(s)
 
-        for j in range(PACK):
-            widen_plain(j, on_scalar if j % 2 else on_vector)
-        turn(0)
-        spread_scales()
-        for j in range(1, PACK):
-            turn(j)
-        v_interleave(0, 0, RANKERS - P)
+        V, S, G = on_vector, on_scalar, on_gpsimd
+        widen(0, V, 0, GROUP)
+        widen(0, V, GROUP, RAW)
+        widen(1)
+        widen(2)
+        widen(3)
+        turn(0, 0, 1)
+        turn(0, 1, 2)
+        turn(1)
+        turn(2)
+        turn(3)
         nc.scalar.copy(out=ipw_f[:], in_=ipw_bf[:])
-        v_interleave(0, RANKERS - P, RANKERS)
-        for j in range(PACK):
-            gather_scaled(j, 0)
-            if j > 0:
-                d_quantize_tile(j - 1)
-            gather_scaled(j, 1)
-        widen_scaled(4)
-        d_quantize_tile(3)
-        widen_scaled(5)
-        widen_scaled(6)
-        for half in range(HALVES):
-            encode_and_weigh(0, half)
-        v_interleave(1, 0, RANKERS // 2)
-        for j in (1, 2):
-            for half in range(HALVES):
-                encode(j, half)
-        turn(4)
-        weigh(1, 0)
-        gather(4)
-        weigh(1, 1)
-        for half in range(HALVES):
-            encode(3, half)
-        turn(5)
-        weigh(2, 0)
-        gather(5)
-        weigh(2, 1)
-        for half in range(HALVES):
-            weigh(3, half)
-        d_quantize_tile(4)
-        widen_scaled(7)
-        v_interleave(1, RANKERS // 2, RANKERS, on_vector)
-        d_quantize_tile(5)
-        v_quantize()
-        for half in range(HALVES):
-            encode(4, half)
-        for j in (6, 7):
-            turn(j)
-        for j in (6, 7):
-            gather(j)
-        for half in range(HALVES):
-            weigh(4, half)
-        for half in range(HALVES):
-            encode_and_weigh(5, half)
-        score(0)
-        score(1)
-        widen_scaled(8)
-        widen_scaled(9)
-        d_quantize_step(3)
+        scale(0, 0, 1)
+        scale(0, 1, 2)
+        d_quantize(0, 1)
+        scale(1, 0, 1)
+        d_quantize(1, 2)
+        scale(1, 1, 2)
+        d_quantize(2, 3)
 
-        middle = RANKERS // 2
-        queue = [(3, h_interleave, (0, 0, on_vector)), (3, h_quantize, (0, 0))]
-        for s in range(last - 1):
-            ready = 2 * s + 4
-            queue += [(ready, lam_multiply, (s, 0, middle)), (ready, lam_multiply, (s, middle, RANKERS)), (ready, h_interleave, (s + 1, 0, on_vector)),
-                      (ready, lam_quantize, (s, 0, RANKERS)), (ready, h_quantize, (s + 1, 0))]
-        queue += [(STEPS - 1, h_interleave, (0, 2, on_vector)), (STEPS - 1, h_interleave, (last, 0, on_vector))]
-        for p in range(3, STEPS):
-            ahead = (2 * p + 2, 2 * p + 3)
-            if p + 1 < STEPS:
-                for j in ahead:
-                    turn(j)
-                for j in ahead:
-                    gather(j)
-            for j in (2 * p, 2 * p + 1):
-                encode_and_weigh(j, 0)
-                score(j - SCORE_LAG)
-                if j < last * PACK:
-                    encode_and_weigh(j, 1)
+        prods = [[(encode, 0, 0), (v_interleave, 0, S, True), (encode, 0, 1), (encode, 1, 0), (encode, 1, 1)],
+          [(encode, 2, 0), (encode, 2, 1), (encode, 3, 0), (encode, 3, 1)],
+          [(encode, 4, 0), (encode, 4, 1), (encode, 5, 0), (encode, 5, 1), (score, 0), (score, 1)],
+          [(encode, 6, 0), (score, 2), (score, 3), (encode, 7, 0), (score, 4), (score, 5)],
+          [(encode, 8, 0), (score, 6), (score, 7), (encode, 9, 0), (score, 8), (score, 9)],
+          [(encode, 10, 0), (score, 10), (encode, 6, 1), (encode, 11, 0), (score, 11), (encode, 7, 1)],
+          [(encode, 12, 0), (score, 12), (encode, 8, 1), (encode, 13, 0), (score, 13), (encode, 9, 1)],
+          [(encode, 10, 1), (encode, 11, 1), (encode, 14, 0), (encode, 15, 0), (score, 14), (score, 15)]]
+        fill_a = {0: [(v_interleave, 1, V)], 1: [(v_interleave, 3, V)], 2: [(h_interleave, 0, 2, V)], 3: [(h_quantize, 0, 2), (h_interleave, 0, 3, V)], 4: [(lam_multiply, 0, 256, 512)], 5: [(lam_multiply, 1, 0, 256)], 6: [(lam_quantize, 0, 256, 512)], 7: [(h_interleave, 2, 1, V), (lam_multiply, 2, 0, 256), (h_quantize, 2, 1), (lam_quantize, 1, 0, 512), (lam_multiply, 2, 256, 512), (h_interleave, 3, 0, V, 2)]}
+        fill_b = {0: [(v_quantize, 0)], 1: [(v_quantize, 1), (v_quantize, 3), (v_quantize, 2)], 2: [(h_quantize, 0, 0)], 3: [(lam_multiply, 0, 0, 256), (h_quantize, 0, 1)], 4: [(h_quantize, 0, 3), (h_quantize, 1, 0)], 5: [(lam_quantize, 0, 0, 256), (h_quantize, 1, 1)], 6: [(lam_multiply, 1, 256, 512), (h_quantize, 2, 0)], 7: [(lam_quantize, 2, 0, 512), (lam_multiply, 3, 0, 128), (h_quantize, 3, 0, 2), (lam_quantize, 3, 0, 128)]}
+        fill_g = {1: [(v_interleave, 2, G)], 2: [(h_interleave, 0, 0, G)], 3: [(h_interleave, 0, 1, G)], 4: [(h_interleave, 1, 0, G)], 5: [(h_interleave, 1, 1, G)], 6: [(h_interleave, 2, 0, G)]}
+        fill_s = {6: [(h_interleave, 1, 2, S)], 7: [(h_interleave, 1, 3, S)]}
+        def run(items):
+            for item in items:
+                item[0](*item[1:])
+        for p in range(STEPS):
+            if 0 < p < STEPS - 1:
+                turn(2 * p + 2)
+                turn(2 * p + 3)
             if p + 2 < STEPS:
-                widen_scaled(2 * p + 4)
-                widen_scaled(2 * p + 5)
-            room = 2 if p + 2 < STEPS else 5
-            todo = [item for item in queue[:room] if item[0] <= p]
-            queue = queue[len(todo) :]
+                widen(2 * p + 4)
+                widen(2 * p + 5)
+            run(fill_s.get(p, []))
+            run(fill_g.get(p, []))
+            if p == 0:
+                scale(2, 0, 1)
+                d_quantize(3, 4)
+                scale(2, 1, 2)
+                scale(3)
+            elif p + 1 < STEPS:
+                scale(2 * p + 2)
+                scale(2 * p + 3)
+            run(prods[p])
+            run(fill_a.get(p, []))
             if p + 1 < STEPS:
-                place = 1 if p + 2 < STEPS else PLACE
-                todo = todo[:place] + [(p, d_quantize_step, (p + 1,))] + todo[place:]
-            for ready, fn, args in todo:
-                fn(*args)
-        for j in range(TILES - SCORE_LAG, TILES):
-            score(j)
-        for j in range(last * PACK, TILES):
-            encode_and_weigh(j, 1)
+                d_quantize(4 * p + 4, 4 * p + 8)
+            run(fill_b.get(p, []))
 
-        open_sums(0)
-        open_sums(1)
-        for s in range(FIRST):
-            h_interleave(s, 1, on_scalar)
-        for ready, fn, args in queue:
-            fn(*args)
-        lam_multiply(last - 1, 0, P)
-        h_quantize(last, 0)
+        for j in range(12, 16):
+            encode(j, 1)
+        h_interleave(2, 2, S)
+        h_interleave(3, 2, S)
+        for s in range(3):
+            for m in range(QTILES):
+                update(s, m, 0, 512)
         for m in range(QTILES):
-            first, stop = m * P, (m + 1) * P
-            lam_multiply(last, first, stop)
-            lam_quantize(last - 1, first, stop)
             if m + 1 < QTILES:
-                lam_multiply(last - 1, stop, stop + P)
-            else:
-                h_quantize(last - 1, 1)
-            lam_quantize(last, first, stop)
-            for s in range(GROUPS):
-                update(s, 0, m)
-            store(0, m, on_scalar)
-            if FIRST + m < GROUPS:
-                h_interleave(FIRST + m, 1, on_scalar)
-            if 1 <= m < last:
-                h_quantize(m - 1, 1)
-                for n in range(QTILES):
-                    update(m - 1, 1, n)
-        open_sums(2)
-        h_interleave(1, 2, on_vector)
-        h_quantize(last, 1)
-        for s in (last - 1, last):
-            for m in range(QTILES):
-                update(s, 1, m)
+                lam_multiply(3, 128 * (m + 1), 128 * (m + 2))
+                h_quantize(m + 1, 2)
+                lam_quantize(3, 128 * (m + 1), 128 * (m + 2))
+            update(3, m, 0, 512)
+            store(m, 0, 512, S)
+            for n in range(QTILES):
+                update(m, n, 512, 768)
+        h_interleave(2, 3, V)
+        h_quantize(1, 3)
+        h_interleave(3, 3, V)
+        h_quantize(2, 3)
         for m in range(QTILES):
-            store(1, m, on_scalar)
+            store(m, 512, 768, S)
+        h_quantize(3, 3)
         for s in range(GROUPS):
-            h_quantize(s, 2)
-            if s + 2 < GROUPS:
-                h_interleave(s + 2, 2, on_vector)
             for m in range(QTILES):
-                update(s, 2, m)
+                update(s, m, 768, 1024)
         for m in range(QTILES):
-            store(2, m, on_scalar if m % 2 else on_vector)
+            store(m, 768, 1024, S if m % 2 else V)

@@ -165,7 +165,7 @@ def tile_lambdarank_head_gradient_s11_kernel(tc, d_bytes, d_scale, v, delta, ipw
                 cols = slice(WORDS * (j % 2) + g * P, WORDS * (j % 2) + (g + 1) * P)
                 codes, planes = moving(g)
                 nc.tensor.matmul_mx(
-                    out=bank[:], lhsT=d_codes[j // 2][:, cols].bitcast(E4M3X4), lhsT_scale=d_planes[j // 2][:, cols],
+                    out=bank, lhsT=d_codes[j // 2][:, cols].bitcast(E4M3X4), lhsT_scale=d_planes[j // 2][:, cols],
                     rhs=codes, rhs_scale=planes, start=(g == 0), stop=(g == PASSES - 1),
                 )
 
@@ -174,7 +174,7 @@ def tile_lambdarank_head_gradient_s11_kernel(tc, d_bytes, d_scale, v, delta, ipw
         def score(j):
             s, t = divmod(j, PACK)
             diff = psum.tile([P, RANKERS], F32, name="bank")
-            times_d(j, diff, lambda g: (v_codes[:, g * RANKERS : (g + 1) * RANKERS].bitcast(E4M3X4), v_planes[:, g * RANKERS : (g + 1) * RANKERS]))
+            times_d(j, diff[:], lambda g: (v_codes[:, g * RANKERS : (g + 1) * RANKERS].bitcast(E4M3X4), v_planes[:, g * RANKERS : (g + 1) * RANKERS]))
             if t == 0:
                 sig[s] = work.tile([P, PACK, RANKERS], F32, name="sig", bufs=3, align_bytes=64)
             nc.scalar.activation(out=sig[s][:, t, :], in_=diff[:], func=SIGMOID, scale=-1.0)
@@ -182,7 +182,7 @@ def tile_lambdarank_head_gradient_s11_kernel(tc, d_bytes, d_scale, v, delta, ipw
         def encode(j, half):
             s, t = divmod(j, PACK)
             encoded = psum.tile([P, BANK], F32, name="bank")
-            times_d(j, encoded, lambda g: (e_w[half][:, g, :].bitcast(E2M1X4), e_s[:, g, BANK * half : BANK * (half + 1)]))
+            times_d(j, encoded[:], lambda g: (e_w[half][:, g, :].bitcast(E2M1X4), e_s[:, g, BANK * half : BANK * (half + 1)]))
             if t == 0:
                 h_raw[s, half] = work.tile([P, PACK, BANK], BF16, name=f"h_raw{half}", bufs=(2, GROUPS)[half], align_bytes=64)
             nc.scalar.activation(out=h_raw[s, half][:, t, :], in_=encoded[:], func=COPY, scale=ipw_f[:, s, t : t + 1])
@@ -215,6 +215,25 @@ def tile_lambdarank_head_gradient_s11_kernel(tc, d_bytes, d_scale, v, delta, ipw
             cols = slice(c * CHUNK, (c + n) * CHUNK)
             quantize(h_codes[s][:, cols], h_planes[s][:, cols], h_grp[s, c][:].rearrange("p n t -> p (n t)"))
 
+        fused = {}
+
+        def encode_group(s, b):
+            half, first = divmod(b * P, BANK)
+            fused[s, b] = psum.tile([P, PACK, P], F32, name="bank")
+            for t in range(PACK):
+                times_d(PACK * s + t, fused[s, b][:, t, :], lambda g: (e_w[half][:, g, 2 * first : 2 * (first + P)].bitcast(E2M1X4), e_s[:, g, b * P : (b + 1) * P]))
+
+        def weigh_group(s, b):
+            c, first = divmod(b * P, CHUNK)
+            if first == 0:
+                h_grp[s, c] = grouped_tile(on_vector, CHUNK)
+            nc.vector.tensor_tensor(
+                out=h_grp[s, c][:, first : first + P, :].rearrange("p (c i) t -> p c t i", i=2),
+                in0=fused[s, b][:].rearrange("p t (c i) -> p c t i", i=2),
+                in1=ipw_f[:, s, :].rearrange("p (o t i) -> p o t i", o=1, i=1).to_broadcast([P, P // 2, PACK, 2]),
+                op=MULT,
+            )
+
         sums = {}
 
         def update(s, m, first, stop):
@@ -243,8 +262,8 @@ def tile_lambdarank_head_gradient_s11_kernel(tc, d_bytes, d_scale, v, delta, ipw
         load_words(1)
         load_raw(1, 0, 2)
         load_v(0)
-        load_v(1)
         load_raw(1, 2, 4)
+        load_v(1)
         load_raw(2, 0, 4)
         load_dlt(0)
         load_raw(3, 0, 4)
@@ -263,6 +282,9 @@ def tile_lambdarank_head_gradient_s11_kernel(tc, d_bytes, d_scale, v, delta, ipw
         turn(2)
         turn(3)
         nc.scalar.copy(out=ipw_f[:], in_=ipw_bf[:])
+        widen(4)
+        widen(5)
+        v_interleave(1, S, True)
         scale(0, 0, 1)
         scale(0, 1, 2)
         d_quantize(0, 1)
@@ -270,8 +292,20 @@ def tile_lambdarank_head_gradient_s11_kernel(tc, d_bytes, d_scale, v, delta, ipw
         d_quantize(1, 2)
         scale(1, 1, 2)
         d_quantize(2, 3)
+        scale(2, 0, 1)
+        d_quantize(3, 4)
+        scale(2, 1, 2)
+        scale(3, 0, 1)
+        d_quantize(4, 6)
+        scale(3, 1, 2)
+        v_quantize(1)
+        d_quantize(6, 8)
+        widen(6)
+        widen(7)
+        encode(0, 0)
+        encode(0, 1)
 
-        prods = [[(encode, 0, 0), (v_interleave, 0, S, True), (encode, 0, 1), (encode, 1, 0), (encode, 1, 1)],
+        prods = [[(encode, 1, 0), (encode, 1, 1)],
           [(encode, 2, 0), (encode, 2, 1), (encode, 3, 0), (encode, 3, 1)],
           [(encode, 4, 0), (encode, 4, 1), (encode, 5, 0), (encode, 5, 1), (score, 0), (score, 1)],
           [(encode, 6, 0), (score, 2), (score, 3), (encode, 7, 0), (score, 4), (score, 5)],
@@ -279,35 +313,30 @@ def tile_lambdarank_head_gradient_s11_kernel(tc, d_bytes, d_scale, v, delta, ipw
           [(encode, 10, 0), (score, 10), (encode, 6, 1), (encode, 11, 0), (score, 11), (encode, 7, 1)],
           [(encode, 12, 0), (score, 12), (encode, 8, 1), (encode, 13, 0), (score, 13), (encode, 9, 1)],
           [(encode, 10, 1), (encode, 11, 1), (encode, 14, 0), (encode, 15, 0), (score, 14), (score, 15)]]
-        fill_a = {0: [(v_interleave, 1, V)], 1: [(v_interleave, 3, V)], 2: [(h_interleave, 0, 2, V)], 3: [(h_quantize, 0, 2), (h_interleave, 0, 3, V)], 4: [(lam_multiply, 0, 256, 512)], 5: [(lam_multiply, 1, 0, 256)], 6: [(lam_quantize, 0, 256, 512)], 7: [(h_interleave, 2, 1, V), (lam_multiply, 2, 0, 256), (h_quantize, 2, 1), (lam_quantize, 1, 0, 512), (lam_multiply, 2, 256, 512), (h_interleave, 3, 0, V, 2)]}
-        fill_b = {0: [(v_quantize, 0)], 1: [(v_quantize, 1), (v_quantize, 3), (v_quantize, 2)], 2: [(h_quantize, 0, 0)], 3: [(lam_multiply, 0, 0, 256), (h_quantize, 0, 1)], 4: [(h_quantize, 0, 3), (h_quantize, 1, 0)], 5: [(lam_quantize, 0, 0, 256), (h_quantize, 1, 1)], 6: [(lam_multiply, 1, 256, 512), (h_quantize, 2, 0)], 7: [(lam_quantize, 2, 0, 512), (lam_multiply, 3, 0, 128), (h_quantize, 3, 0, 2), (lam_quantize, 3, 0, 128)]}
-        fill_g = {1: [(v_interleave, 2, G)], 2: [(h_interleave, 0, 0, G)], 3: [(h_interleave, 0, 1, G)], 4: [(h_interleave, 1, 0, G)], 5: [(h_interleave, 1, 1, G)], 6: [(h_interleave, 2, 0, G)]}
-        fill_s = {6: [(h_interleave, 1, 2, S)], 7: [(h_interleave, 1, 3, S)]}
+        fill_v = {0: [(v_interleave, 3, V), (v_quantize, 0)], 1: [(v_quantize, 3), (v_quantize, 2)], 2: [(h_interleave, 0, 2, V), (h_quantize, 0, 0)], 3: [(h_quantize, 0, 2), (lam_multiply, 0, 0, 256), (h_quantize, 0, 1)], 4: [(lam_multiply, 0, 256, 512), (h_quantize, 1, 0)], 5: [(lam_multiply, 1, 0, 256), (h_quantize, 1, 1)],
+          6: [(lam_multiply, 1, 256, 512), (lam_quantize, 0, 0, 512), (h_interleave, 2, 0, V, 2), (lam_quantize, 1, 0, 512), (lam_multiply, 2, 0, 256), (h_quantize, 2, 0, 2)],
+          7: [(lam_multiply, 2, 256, 512), (h_interleave, 1, 3, V), (h_interleave, 3, 0, V, 2), (lam_quantize, 2, 0, 512), (lam_multiply, 3, 0, 128), (h_quantize, 3, 0, 2), (lam_quantize, 3, 0, 128)]}
+        fill_g = {0: [(v_interleave, 0, G)], 1: [(v_interleave, 2, G)], 2: [(h_interleave, 0, 0, G)], 3: [(h_interleave, 0, 1, G)], 4: [(h_interleave, 1, 0, G)], 5: [(h_interleave, 1, 1, G)]}
+        fill_s = {5: [(h_interleave, 0, 3, S)], 6: [(h_interleave, 1, 2, S)]}
         def run(items):
             for item in items:
                 item[0](*item[1:])
         for p in range(STEPS):
-            if 0 < p < STEPS - 1:
-                turn(2 * p + 2)
-                turn(2 * p + 3)
             if p + 2 < STEPS:
-                widen(2 * p + 4)
-                widen(2 * p + 5)
+                turn(2 * p + 4)
+                turn(2 * p + 5)
+            if 0 < p < STEPS - 3:
+                widen(2 * p + 6)
+                widen(2 * p + 7)
             run(fill_s.get(p, []))
             run(fill_g.get(p, []))
-            if p == 0:
-                scale(2, 0, 1)
-                d_quantize(3, 4)
-                scale(2, 1, 2)
-                scale(3)
-            elif p + 1 < STEPS:
-                scale(2 * p + 2)
-                scale(2 * p + 3)
+            if p + 2 < STEPS:
+                scale(2 * p + 4)
+                scale(2 * p + 5)
             run(prods[p])
-            run(fill_a.get(p, []))
-            if p + 1 < STEPS:
-                d_quantize(4 * p + 4, 4 * p + 8)
-            run(fill_b.get(p, []))
+            run(fill_v.get(p, []))
+            if p + 2 < STEPS:
+                d_quantize(4 * p + 8, 4 * p + 12)
 
         for j in range(12, 16):
             encode(j, 1)
@@ -325,6 +354,7 @@ def tile_lambdarank_head_gradient_s11_kernel(tc, d_bytes, d_scale, v, delta, ipw
             store(m, 0, 512, S)
             for n in range(QTILES):
                 update(m, n, 512, 768)
+        h_quantize(0, 3)
         h_interleave(2, 3, V)
         h_quantize(1, 3)
         h_interleave(3, 3, V)

@@ -31,7 +31,7 @@ BANKS = 8
 CHUNK = 256
 CHUNKS = FEATS // CHUNK
 
-GRPBUFS = 8
+GRPBUFS = 7
 
 FLOPS = 2 * PAIRS * RAW * RANKERS + 2 * PAIRS * RAW * FEATS + 2 * RANKERS * PAIRS * FEATS
 
@@ -114,14 +114,13 @@ def tile_lambdarank_head_gradient_s11_kernel(tc, d_bytes, d_scale, v, delta, ipw
         v_planes = keep.tile([P, PASSES * RANKERS], U8, name="v_planes", align_bytes=64)
         v_grp = {}
 
-        def v_interleave(c, copy, slot=False):
-            g, first = divmod(c * CHUNK, RANKERS)
-            v_grp[c] = grouped_tile(copy, CHUNK, slot)
-            interleave(copy, v_raw[g][:, :, first : first + CHUNK], v_grp[c][:])
+        def v_interleave(first, stop, copy, slot=False):
+            g = first // RANKERS
+            v_grp[first] = grouped_tile(copy, stop - first, slot)
+            interleave(copy, v_raw[g][:, :, first - g * RANKERS : stop - g * RANKERS], v_grp[first][:])
 
-        def v_quantize(c):
-            cols = slice(c * CHUNK, (c + 1) * CHUNK)
-            quantize(v_codes[:, cols], v_planes[:, cols], v_grp[c][:].rearrange("p n t -> p (n t)"))
+        def v_quantize(base, first, stop):
+            quantize(v_codes[:, first:stop], v_planes[:, first:stop], v_grp[base][:, first - base : stop - base, :].rearrange("p n t -> p (n t)"))
 
         WORDS = PASSES * P
         d_codes = [keep.tile([P, 2 * WORDS], U32, name=f"d_codes{p}", align_bytes=64) for p in range(STEPS)]
@@ -169,7 +168,8 @@ def tile_lambdarank_head_gradient_s11_kernel(tc, d_bytes, d_scale, v, delta, ipw
                     rhs=codes, rhs_scale=planes, start=(g == 0), stop=(g == PASSES - 1),
                 )
 
-        sig, h_raw = {}, {}
+        sig = {}
+        h_raw = [keep.tile([P, PACK, FEATS], BF16, name=f"h_raw{s}", align_bytes=64) for s in range(GROUPS)]
 
         def score(j):
             s, t = divmod(j, PACK)
@@ -183,9 +183,7 @@ def tile_lambdarank_head_gradient_s11_kernel(tc, d_bytes, d_scale, v, delta, ipw
             s, t = divmod(j, PACK)
             encoded = psum.tile([P, BANK], F32, name="bank")
             times_d(j, encoded[:], lambda g: (e_w[half][:, g, :].bitcast(E2M1X4), e_s[:, g, BANK * half : BANK * (half + 1)]))
-            if t == 0:
-                h_raw[s, half] = work.tile([P, PACK, BANK], BF16, name=f"h_raw{half}", bufs=(2, GROUPS)[half], align_bytes=64)
-            nc.scalar.activation(out=h_raw[s, half][:, t, :], in_=encoded[:], func=COPY, scale=ipw_f[:, s, t : t + 1])
+            nc.scalar.activation(out=h_raw[s][:, t, BANK * half : BANK * (half + 1)], in_=encoded[:], func=COPY, scale=ipw_f[:, s, t : t + 1])
 
         lam_codes = [keep.tile([P, RANKERS], U32, name=f"lam_codes{s}", align_bytes=64) for s in range(GROUPS)]
         lam_planes = [keep.tile([P, RANKERS], U8, name=f"lam_planes{s}", align_bytes=64) for s in range(GROUPS)]
@@ -206,33 +204,12 @@ def tile_lambdarank_head_gradient_s11_kernel(tc, d_bytes, d_scale, v, delta, ipw
         def lam_quantize(s, first, stop):
             quantize(lam_codes[s][:, first:stop], lam_planes[s][:, first:stop], lam[s][:, first:stop, :].rearrange("p n t -> p (n t)"))
 
-        def h_interleave(s, c, copy, n=1):
-            half, first = divmod(c * CHUNK, BANK)
-            h_grp[s, c] = grouped_tile(copy, n * CHUNK)
-            interleave(copy, h_raw[s, half][:, :, first : first + n * CHUNK], h_grp[s, c][:])
+        def h_interleave(s, first, stop, copy):
+            h_grp[s, first] = grouped_tile(copy, stop - first)
+            interleave(copy, h_raw[s][:, :, first:stop], h_grp[s, first][:])
 
-        def h_quantize(s, c, n=1):
-            cols = slice(c * CHUNK, (c + n) * CHUNK)
-            quantize(h_codes[s][:, cols], h_planes[s][:, cols], h_grp[s, c][:].rearrange("p n t -> p (n t)"))
-
-        fused = {}
-
-        def encode_group(s, b):
-            half, first = divmod(b * P, BANK)
-            fused[s, b] = psum.tile([P, PACK, P], F32, name="bank")
-            for t in range(PACK):
-                times_d(PACK * s + t, fused[s, b][:, t, :], lambda g: (e_w[half][:, g, 2 * first : 2 * (first + P)].bitcast(E2M1X4), e_s[:, g, b * P : (b + 1) * P]))
-
-        def weigh_group(s, b):
-            c, first = divmod(b * P, CHUNK)
-            if first == 0:
-                h_grp[s, c] = grouped_tile(on_vector, CHUNK)
-            nc.vector.tensor_tensor(
-                out=h_grp[s, c][:, first : first + P, :].rearrange("p (c i) t -> p c t i", i=2),
-                in0=fused[s, b][:].rearrange("p t (c i) -> p c t i", i=2),
-                in1=ipw_f[:, s, :].rearrange("p (o t i) -> p o t i", o=1, i=1).to_broadcast([P, P // 2, PACK, 2]),
-                op=MULT,
-            )
+        def h_quantize(s, base, first, stop):
+            quantize(h_codes[s][:, first:stop], h_planes[s][:, first:stop], h_grp[s, base][:, first - base : stop - base, :].rearrange("p n t -> p (n t)"))
 
         sums = {}
 
@@ -284,7 +261,7 @@ def tile_lambdarank_head_gradient_s11_kernel(tc, d_bytes, d_scale, v, delta, ipw
         nc.scalar.copy(out=ipw_f[:], in_=ipw_bf[:])
         widen(4)
         widen(5)
-        v_interleave(1, S, True)
+        v_interleave(384, 512, S, True)
         scale(0, 0, 1)
         scale(0, 1, 2)
         d_quantize(0, 1)
@@ -298,7 +275,7 @@ def tile_lambdarank_head_gradient_s11_kernel(tc, d_bytes, d_scale, v, delta, ipw
         scale(3, 0, 1)
         d_quantize(4, 6)
         scale(3, 1, 2)
-        v_quantize(1)
+        v_quantize(384, 384, 512)
         d_quantize(6, 8)
         widen(6)
         widen(7)
@@ -309,15 +286,17 @@ def tile_lambdarank_head_gradient_s11_kernel(tc, d_bytes, d_scale, v, delta, ipw
           [(encode, 2, 0), (encode, 2, 1), (encode, 3, 0), (encode, 3, 1)],
           [(encode, 4, 0), (encode, 4, 1), (encode, 5, 0), (encode, 5, 1), (score, 0), (score, 1)],
           [(encode, 6, 0), (score, 2), (score, 3), (encode, 7, 0), (score, 4), (score, 5)],
-          [(encode, 8, 0), (score, 6), (score, 7), (encode, 9, 0), (score, 8), (score, 9)],
-          [(encode, 10, 0), (score, 10), (encode, 6, 1), (encode, 11, 0), (score, 11), (encode, 7, 1)],
+          [(encode, 8, 0), (score, 6), (score, 7), (encode, 9, 0), (encode, 6, 1), (encode, 7, 1)],
+          [(encode, 10, 0), (score, 8), (score, 9), (encode, 11, 0), (score, 10), (score, 11)],
           [(encode, 12, 0), (score, 12), (encode, 8, 1), (encode, 13, 0), (score, 13), (encode, 9, 1)],
           [(encode, 10, 1), (encode, 11, 1), (encode, 14, 0), (encode, 15, 0), (score, 14), (score, 15)]]
-        fill_v = {0: [(v_interleave, 3, V), (v_quantize, 0)], 1: [(v_quantize, 3), (v_quantize, 2)], 2: [(h_interleave, 0, 2, V), (h_quantize, 0, 0)], 3: [(h_quantize, 0, 2), (lam_multiply, 0, 0, 256), (h_quantize, 0, 1)], 4: [(lam_multiply, 0, 256, 512), (h_quantize, 1, 0)], 5: [(lam_multiply, 1, 0, 256), (h_quantize, 1, 1)],
-          6: [(lam_multiply, 1, 256, 512), (lam_quantize, 0, 0, 512), (h_interleave, 2, 0, V, 2), (lam_quantize, 1, 0, 512), (lam_multiply, 2, 0, 256), (h_quantize, 2, 0, 2)],
-          7: [(lam_multiply, 2, 256, 512), (h_interleave, 1, 3, V), (h_interleave, 3, 0, V, 2), (lam_quantize, 2, 0, 512), (lam_multiply, 3, 0, 128), (h_quantize, 3, 0, 2), (lam_quantize, 3, 0, 128)]}
-        fill_g = {0: [(v_interleave, 0, G)], 1: [(v_interleave, 2, G)], 2: [(h_interleave, 0, 0, G)], 3: [(h_interleave, 0, 1, G)], 4: [(h_interleave, 1, 0, G)], 5: [(h_interleave, 1, 1, G)]}
-        fill_s = {5: [(h_interleave, 0, 3, S)], 6: [(h_interleave, 1, 2, S)]}
+        fill_v = {0: [(v_interleave, 512, 640, V), (v_quantize, 0, 0, 256), (v_quantize, 0, 256, 384)], 1: [(v_quantize, 512, 512, 640), (v_quantize, 640, 640, 768), (v_quantize, 640, 768, 1024)],
+          2: [(h_quantize, 0, 0, 0, 256), (h_quantize, 0, 0, 256, 384)], 3: [(lam_multiply, 0, 0, 256), (h_quantize, 0, 384, 384, 512), (h_quantize, 0, 384, 512, 768)],
+          4: [(lam_multiply, 0, 256, 512), (h_quantize, 1, 0, 0, 256), (h_quantize, 1, 0, 256, 384)], 5: [(lam_multiply, 1, 0, 256), (h_quantize, 1, 384, 384, 512), (h_quantize, 1, 384, 512, 768)],
+          6: [(lam_multiply, 1, 256, 512), (lam_quantize, 0, 0, 512), (h_interleave, 2, 0, 512, V), (lam_quantize, 1, 0, 512), (lam_multiply, 2, 0, 256), (h_quantize, 2, 0, 0, 512)],
+          7: [(lam_multiply, 2, 256, 512), (h_interleave, 3, 0, 512, V), (lam_quantize, 2, 0, 512), (lam_multiply, 3, 0, 128), (h_quantize, 3, 0, 0, 512), (lam_quantize, 3, 0, 128)]}
+        fill_g = {0: [(v_interleave, 0, 384, G)], 1: [(v_interleave, 640, 1024, G)], 2: [(h_interleave, 0, 0, 384, G)], 3: [(h_interleave, 0, 384, 768, G)], 4: [(h_interleave, 1, 0, 384, G)], 5: [(h_interleave, 1, 384, 768, G)]}
+        fill_s = {5: [(h_interleave, 0, 768, 1024, S)], 6: [(h_interleave, 1, 768, 1024, S)]}
         def run(items):
             for item in items:
                 item[0](*item[1:])
@@ -340,28 +319,30 @@ def tile_lambdarank_head_gradient_s11_kernel(tc, d_bytes, d_scale, v, delta, ipw
 
         for j in range(12, 16):
             encode(j, 1)
-        h_interleave(2, 2, S)
-        h_interleave(3, 2, S)
+        h_interleave(2, 512, 768, S)
+        h_interleave(3, 512, 768, S)
         for s in range(3):
             for m in range(QTILES):
                 update(s, m, 0, 512)
         for m in range(QTILES):
             if m + 1 < QTILES:
                 lam_multiply(3, 128 * (m + 1), 128 * (m + 2))
-                h_quantize(m + 1, 2)
+                if m == 0:
+                    h_quantize(0, 768, 768, 1024)
+                else:
+                    h_quantize(m + 1, 512, 512, 768)
                 lam_quantize(3, 128 * (m + 1), 128 * (m + 2))
             update(3, m, 0, 512)
             store(m, 0, 512, S)
             for n in range(QTILES):
                 update(m, n, 512, 768)
-        h_quantize(0, 3)
-        h_interleave(2, 3, V)
-        h_quantize(1, 3)
-        h_interleave(3, 3, V)
-        h_quantize(2, 3)
+        h_interleave(2, 768, 1024, V)
+        h_quantize(1, 768, 768, 1024)
+        h_interleave(3, 768, 1024, V)
+        h_quantize(2, 768, 768, 1024)
         for m in range(QTILES):
             store(m, 512, 768, S)
-        h_quantize(3, 3)
+        h_quantize(3, 768, 768, 1024)
         for s in range(GROUPS):
             for m in range(QTILES):
                 update(s, m, 768, 1024)

@@ -31,7 +31,10 @@ BANKS = 8
 CHUNK = 256
 CHUNKS = FEATS // CHUNK
 
-GRPBUFS = 7
+GRPBUFS = 8
+TURN_BANKS = 0
+TURN_FROM = 99
+SUMS_IN_TURN = ()
 
 FLOPS = 2 * PAIRS * RAW * RANKERS + 2 * PAIRS * RAW * FEATS + 2 * RANKERS * PAIRS * FEATS
 
@@ -87,6 +90,11 @@ def tile_lambdarank_head_gradient_s11_kernel(tc, d_bytes, d_scale, v, delta, ipw
         def load_ipw():
             nc.sync.dma_start(out=ipw_bf[:], in_=ipw.rearrange("(s m t) -> m s t", m=P, t=PACK))
 
+        def next_bank(shape, turning=False):
+            if turning:
+                return psum.tile(shape, F32, name="turn_bank", bufs=TURN_BANKS)
+            return psum.tile(shape, F32, name="bank", bufs=BANKS - TURN_BANKS)
+
         def on_vector(out, in_):
             nc.vector.tensor_copy(out=out, in_=in_)
 
@@ -133,22 +141,27 @@ def tile_lambdarank_head_gradient_s11_kernel(tc, d_bytes, d_scale, v, delta, ipw
             copy(wide[j][:, first:stop], raw[j // PACK][:, j % PACK, first:stop].bitcast(FP8))
 
         def turn(j, first=0, stop=PASSES):
-            bank = psum.tile([P, 2, PASSES, P], F32, name="bank")
+            bank = next_bank([P, 2, PASSES, P], j >= TURN_FROM)
             words = wide[j][:].bitcast(F32)
             for g in range(first, stop):
                 turned[j, g] = bank
                 for u in range(2):
                     nc.tensor.transpose(bank[:, u, g, :], words[:, 256 * g + u : 256 * (g + 1) : 2], ident[:])
 
-        def d_grouped(j):
-            if j // 2 not in d_grp:
-                d_grp[j // 2] = work.tile([P, 2 * RAW], BF16, name="d_grp", bufs=2, align_bytes=64)
-            return d_grp[j // 2][:, RAW * (j % 2) : RAW * (j % 2 + 1)]
+        def d_grouped(first, stop):
+            if first < 2 * PASSES:
+                if first not in d_grp:
+                    d_grp[first] = work.tile([P, GROUP], BF16, name="g_grp" if first == 2 else "d_first", bufs=1 if first == 2 else 3, align_bytes=64)
+                return d_grp[first][:]
+            start = first - first % (2 * PASSES)
+            if start not in d_grp:
+                d_grp[start] = work.tile([P, 2 * RAW], BF16, name="d_grp", bufs=2, align_bytes=64)
+            return d_grp[start][:, GROUP * (first - start) : GROUP * (stop - start)]
 
         def scale(j, first=0, stop=PASSES):
             n = stop - first
             nc.vector.tensor_tensor(
-                out=d_grouped(j)[:, GROUP * first : GROUP * stop].rearrange("p (g r u e) -> p g r u e", g=n, u=2, e=2),
+                out=d_grouped(PASSES * j + first, PASSES * j + stop).rearrange("p (g r u e) -> p g r u e", g=n, u=2, e=2),
                 in0=turned[j, first][:, :, first:stop, :].bitcast(BF16).rearrange("p u g (r e) -> p g r u e", e=2),
                 in1=scale_kp[:, first:stop, :].rearrange("p g (o u e) -> p g o u e", o=1, e=2).to_broadcast([P, n, P, 2, 2]),
                 op=MULT,
@@ -156,8 +169,8 @@ def tile_lambdarank_head_gradient_s11_kernel(tc, d_bytes, d_scale, v, delta, ipw
 
         def d_quantize(first, stop):
             p = first // (2 * PASSES)
-            lo, hi = first - 2 * PASSES * p, stop - 2 * PASSES * p
-            quantize(d_codes[p][:, P * lo : P * hi], d_planes[p][:, P * lo : P * hi], d_grp[p][:, GROUP * lo : GROUP * hi])
+            cols = slice(P * (first - 2 * PASSES * p), P * (stop - 2 * PASSES * p))
+            quantize(d_codes[p][:, cols], d_planes[p][:, cols], d_grouped(first, stop))
 
         def times_d(j, bank, moving):
             for g in range(PASSES):
@@ -173,7 +186,7 @@ def tile_lambdarank_head_gradient_s11_kernel(tc, d_bytes, d_scale, v, delta, ipw
 
         def score(j):
             s, t = divmod(j, PACK)
-            diff = psum.tile([P, RANKERS], F32, name="bank")
+            diff = next_bank([P, RANKERS])
             times_d(j, diff[:], lambda g: (v_codes[:, g * RANKERS : (g + 1) * RANKERS].bitcast(E4M3X4), v_planes[:, g * RANKERS : (g + 1) * RANKERS]))
             if t == 0:
                 sig[s] = work.tile([P, PACK, RANKERS], F32, name="sig", bufs=3, align_bytes=64)
@@ -181,7 +194,7 @@ def tile_lambdarank_head_gradient_s11_kernel(tc, d_bytes, d_scale, v, delta, ipw
 
         def encode(j, half):
             s, t = divmod(j, PACK)
-            encoded = psum.tile([P, BANK], F32, name="bank")
+            encoded = next_bank([P, BANK])
             times_d(j, encoded[:], lambda g: (e_w[half][:, g, :].bitcast(E2M1X4), e_s[:, g, BANK * half : BANK * (half + 1)]))
             nc.scalar.activation(out=h_raw[s][:, t, BANK * half : BANK * (half + 1)], in_=encoded[:], func=COPY, scale=ipw_f[:, s, t : t + 1])
 
@@ -215,7 +228,7 @@ def tile_lambdarank_head_gradient_s11_kernel(tc, d_bytes, d_scale, v, delta, ipw
 
         def update(s, m, first, stop):
             if s == 0:
-                sums[m, first] = psum.tile([P, stop - first], F32, name="bank")
+                sums[m, first] = next_bank([P, stop - first], (m, first) in SUMS_IN_TURN)
             rows = slice(m * P, (m + 1) * P)
             nc.tensor.matmul_mx(
                 out=sums[m, first][:], lhsT=lam_codes[s][:, rows].bitcast(E4M3X4), lhsT_scale=lam_planes[s][:, rows],
@@ -236,9 +249,9 @@ def tile_lambdarank_head_gradient_s11_kernel(tc, d_bytes, d_scale, v, delta, ipw
         load_scales()
         load_words(0)
         load_ipw()
-        load_words(1)
         load_raw(1, 0, 2)
         load_v(0)
+        load_words(1)
         load_raw(1, 2, 4)
         load_v(1)
         load_raw(2, 0, 4)
@@ -261,7 +274,7 @@ def tile_lambdarank_head_gradient_s11_kernel(tc, d_bytes, d_scale, v, delta, ipw
         nc.scalar.copy(out=ipw_f[:], in_=ipw_bf[:])
         widen(4)
         widen(5)
-        v_interleave(384, 512, S, True)
+        v_interleave(384, 512, S)
         scale(0, 0, 1)
         scale(0, 1, 2)
         d_quantize(0, 1)
@@ -269,34 +282,35 @@ def tile_lambdarank_head_gradient_s11_kernel(tc, d_bytes, d_scale, v, delta, ipw
         d_quantize(1, 2)
         scale(1, 1, 2)
         d_quantize(2, 3)
-        scale(2, 0, 1)
         d_quantize(3, 4)
-        scale(2, 1, 2)
-        scale(3, 0, 1)
+        v_interleave(0, 384, G)
+        scale(2)
+        scale(3)
         d_quantize(4, 6)
-        scale(3, 1, 2)
         v_quantize(384, 384, 512)
+        v_quantize(0, 0, 256)
+        v_quantize(0, 256, 384)
         d_quantize(6, 8)
-        widen(6)
-        widen(7)
         encode(0, 0)
+        encode(1, 0)
         encode(0, 1)
+        encode(1, 1)
 
-        prods = [[(encode, 1, 0), (encode, 1, 1)],
-          [(encode, 2, 0), (encode, 2, 1), (encode, 3, 0), (encode, 3, 1)],
-          [(encode, 4, 0), (encode, 4, 1), (encode, 5, 0), (encode, 5, 1), (score, 0), (score, 1)],
-          [(encode, 6, 0), (score, 2), (score, 3), (encode, 7, 0), (score, 4), (score, 5)],
-          [(encode, 8, 0), (score, 6), (score, 7), (encode, 9, 0), (encode, 6, 1), (encode, 7, 1)],
-          [(encode, 10, 0), (score, 8), (score, 9), (encode, 11, 0), (score, 10), (score, 11)],
-          [(encode, 12, 0), (score, 12), (encode, 8, 1), (encode, 13, 0), (score, 13), (encode, 9, 1)],
-          [(encode, 10, 1), (encode, 11, 1), (encode, 14, 0), (encode, 15, 0), (score, 14), (score, 15)]]
-        fill_v = {0: [(v_interleave, 512, 640, V), (v_quantize, 0, 0, 256), (v_quantize, 0, 256, 384)], 1: [(v_quantize, 512, 512, 640), (v_quantize, 640, 640, 768), (v_quantize, 640, 768, 1024)],
-          2: [(h_quantize, 0, 0, 0, 256), (h_quantize, 0, 0, 256, 384)], 3: [(lam_multiply, 0, 0, 256), (h_quantize, 0, 384, 384, 512), (h_quantize, 0, 384, 512, 768)],
-          4: [(lam_multiply, 0, 256, 512), (h_quantize, 1, 0, 0, 256), (h_quantize, 1, 0, 256, 384)], 5: [(lam_multiply, 1, 0, 256), (h_quantize, 1, 384, 384, 512), (h_quantize, 1, 384, 512, 768)],
-          6: [(lam_multiply, 1, 256, 512), (lam_quantize, 0, 0, 512), (h_interleave, 2, 0, 512, V), (lam_quantize, 1, 0, 512), (lam_multiply, 2, 0, 256), (h_quantize, 2, 0, 0, 512)],
-          7: [(lam_multiply, 2, 256, 512), (h_interleave, 3, 0, 512, V), (lam_quantize, 2, 0, 512), (lam_multiply, 3, 0, 128), (h_quantize, 3, 0, 0, 512), (lam_quantize, 3, 0, 128)]}
-        fill_g = {0: [(v_interleave, 0, 384, G)], 1: [(v_interleave, 640, 1024, G)], 2: [(h_interleave, 0, 0, 384, G)], 3: [(h_interleave, 0, 384, 768, G)], 4: [(h_interleave, 1, 0, 384, G)], 5: [(h_interleave, 1, 384, 768, G)]}
-        fill_s = {5: [(h_interleave, 0, 768, 1024, S)], 6: [(h_interleave, 1, 768, 1024, S)]}
+        prods = [[(encode, 2, 0), (encode, 3, 0), (encode, 2, 1), (encode, 3, 1)],
+          [(score, 0), (score, 1), (score, 2), (score, 3)],
+          [(encode, 4, 0), (encode, 5, 0), (encode, 4, 1), (encode, 5, 1), (encode, 6, 0), (encode, 7, 0)],
+          [(encode, 6, 1), (encode, 7, 1), (score, 4), (score, 5), (score, 6), (score, 7)],
+          [(encode, 8, 0), (encode, 9, 0), (score, 8), (score, 9), (encode, 10, 0), (encode, 11, 0)],
+          [(score, 10), (score, 11), (encode, 8, 1), (encode, 9, 1), (encode, 12, 0), (encode, 13, 0)],
+          [(score, 12), (score, 13), (encode, 10, 1), (encode, 11, 1)],
+          [(encode, 14, 0), (encode, 15, 0), (score, 14), (score, 15)]]
+        fill_v = {0: [(v_quantize, 512, 512, 640), (v_quantize, 640, 640, 768), (v_quantize, 640, 768, 1024)], 1: [(h_quantize, 0, 0, 0, 256), (h_quantize, 0, 0, 256, 384)],
+          2: [(lam_multiply, 0, 0, 256), (h_quantize, 0, 384, 384, 512), (h_quantize, 0, 384, 512, 768)], 3: [(lam_multiply, 0, 256, 512), (h_quantize, 1, 0, 0, 256), (h_quantize, 1, 0, 256, 384)],
+          4: [(lam_multiply, 1, 0, 256), (h_quantize, 1, 384, 384, 512), (h_quantize, 1, 384, 512, 768)], 5: [(lam_quantize, 0, 0, 512)],
+          6: [(lam_multiply, 1, 256, 512), (h_quantize, 2, 0, 0, 256), (h_quantize, 2, 0, 256, 384), (lam_multiply, 2, 0, 256), (h_quantize, 2, 384, 384, 512), (lam_quantize, 1, 0, 512), (lam_multiply, 2, 256, 512)],
+          7: [(h_interleave, 1, 768, 1024, V), (h_interleave, 3, 0, 512, V), (lam_quantize, 2, 0, 512), (lam_multiply, 3, 0, 128), (h_quantize, 3, 0, 0, 512), (lam_quantize, 3, 0, 128)]}
+        fill_g = {0: [(v_interleave, 640, 1024, G)], 1: [(h_interleave, 0, 0, 384, G)], 2: [(h_interleave, 0, 384, 768, G)], 3: [(h_interleave, 1, 0, 384, G)], 4: [(h_interleave, 1, 384, 768, G)], 5: [(h_interleave, 2, 0, 384, G)]}
+        fill_s = {0: [(v_interleave, 512, 640, S)], 5: [(h_interleave, 0, 768, 1024, S), (h_interleave, 2, 384, 512, S)]}
         def run(items):
             for item in items:
                 item[0](*item[1:])
@@ -304,7 +318,7 @@ def tile_lambdarank_head_gradient_s11_kernel(tc, d_bytes, d_scale, v, delta, ipw
             if p + 2 < STEPS:
                 turn(2 * p + 4)
                 turn(2 * p + 5)
-            if 0 < p < STEPS - 3:
+            if p + 3 < STEPS:
                 widen(2 * p + 6)
                 widen(2 * p + 7)
             run(fill_s.get(p, []))

@@ -31,7 +31,7 @@ BANKS = 8
 CHUNK = 256
 CHUNKS = FEATS // CHUNK
 
-GRPBUFS = 8
+GRPBUFS = 7
 TURN_BANKS = 0
 TURN_FROM = 99
 SUMS_IN_TURN = ()
@@ -133,16 +133,20 @@ def tile_lambdarank_head_gradient_s11_kernel(tc, d_bytes, d_scale, v, delta, ipw
         WORDS = PASSES * P
         d_codes = [keep.tile([P, 2 * WORDS], U32, name=f"d_codes{p}", align_bytes=64) for p in range(STEPS)]
         d_planes = [keep.tile([P, 2 * WORDS], U8, name=f"d_planes{p}", align_bytes=64) for p in range(STEPS)]
-        wide, turned, d_grp = {}, {}, {}
+        wide, wide_all, turned, d_grp = {}, {}, {}, {}
 
-        def widen(j, copy=on_scalar, first=0, stop=RAW):
+        def widen(j, tiles=1, copy=on_scalar, first=0, stop=RAW):
             if first == 0:
-                wide[j] = work.tile([P, RAW], BF16, name="wide", bufs=4, align_bytes=64)
-            copy(wide[j][:, first:stop], raw[j // PACK][:, j % PACK, first:stop].bitcast(FP8))
+                both = work.tile([P, tiles, RAW], BF16, name="wide", bufs=3, align_bytes=64)
+                for i in range(tiles):
+                    wide[j + i] = both[:, i, :]
+                wide_all[j] = both
+            t = j % PACK
+            copy(wide_all[j][:, :, first:stop], raw[j // PACK][:, t : t + tiles, first:stop].bitcast(FP8))
 
         def turn(j, first=0, stop=PASSES):
             bank = next_bank([P, 2, PASSES, P], j >= TURN_FROM)
-            words = wide[j][:].bitcast(F32)
+            words = wide[j].bitcast(F32)
             for g in range(first, stop):
                 turned[j, g] = bank
                 for u in range(2):
@@ -202,7 +206,7 @@ def tile_lambdarank_head_gradient_s11_kernel(tc, d_bytes, d_scale, v, delta, ipw
         lam_planes = [keep.tile([P, RANKERS], U8, name=f"lam_planes{s}", align_bytes=64) for s in range(GROUPS)]
         h_codes = [keep.tile([P, FEATS], U32, name=f"h_codes{s}", align_bytes=64) for s in range(GROUPS)]
         h_planes = [keep.tile([P, FEATS], U8, name=f"h_planes{s}", align_bytes=64) for s in range(GROUPS)]
-        lam, h_grp = {}, {}
+        lam, h_grp, encoded_group = {}, {}, {}
 
         def lam_multiply(s, first, stop):
             if first == 0:
@@ -261,9 +265,9 @@ def tile_lambdarank_head_gradient_s11_kernel(tc, d_bytes, d_scale, v, delta, ipw
             load_dlt(s)
 
         V, S, G = on_vector, on_scalar, on_gpsimd
-        widen(0, V, 0, GROUP)
-        widen(0, V, GROUP, RAW)
-        widen(1)
+        widen(0, 1, V, 0, GROUP)
+        widen(0, 1, V, GROUP, RAW)
+        widen(1, 1, V)
         widen(2)
         widen(3)
         turn(0, 0, 1)
@@ -272,8 +276,7 @@ def tile_lambdarank_head_gradient_s11_kernel(tc, d_bytes, d_scale, v, delta, ipw
         turn(2)
         turn(3)
         nc.scalar.copy(out=ipw_f[:], in_=ipw_bf[:])
-        widen(4)
-        widen(5)
+        widen(4, 2)
         v_interleave(384, 512, S)
         scale(0, 0, 1)
         scale(0, 1, 2)
@@ -304,13 +307,13 @@ def tile_lambdarank_head_gradient_s11_kernel(tc, d_bytes, d_scale, v, delta, ipw
           [(score, 10), (score, 11), (encode, 8, 1), (encode, 9, 1), (encode, 12, 0), (encode, 13, 0)],
           [(score, 12), (score, 13), (encode, 10, 1), (encode, 11, 1)],
           [(encode, 14, 0), (encode, 15, 0), (score, 14), (score, 15)]]
-        fill_v = {0: [(v_quantize, 512, 512, 640), (v_quantize, 640, 640, 768), (v_quantize, 640, 768, 1024)], 1: [(h_quantize, 0, 0, 0, 256), (h_quantize, 0, 0, 256, 384)],
-          2: [(lam_multiply, 0, 0, 256), (h_quantize, 0, 384, 384, 512), (h_quantize, 0, 384, 512, 768)], 3: [(lam_multiply, 0, 256, 512), (h_quantize, 1, 0, 0, 256), (h_quantize, 1, 0, 256, 384)],
+        fill_v = {0: [(v_interleave, 512, 640, V), (v_quantize, 640, 640, 768), (v_quantize, 512, 512, 640), (v_quantize, 640, 768, 1024)], 1: [(h_quantize, 0, 0, 0, 256), (h_quantize, 0, 0, 256, 384)],
+          2: [(widen, 11, 1, V), (lam_multiply, 0, 0, 256), (h_quantize, 0, 384, 384, 512), (h_quantize, 0, 384, 512, 768)], 3: [(lam_multiply, 0, 256, 512), (h_quantize, 1, 0, 0, 256), (h_quantize, 1, 0, 256, 384)],
           4: [(lam_multiply, 1, 0, 256), (h_quantize, 1, 384, 384, 512), (h_quantize, 1, 384, 512, 768)], 5: [(lam_quantize, 0, 0, 512)],
-          6: [(lam_multiply, 1, 256, 512), (h_quantize, 2, 0, 0, 256), (h_quantize, 2, 0, 256, 384), (lam_multiply, 2, 0, 256), (h_quantize, 2, 384, 384, 512), (lam_quantize, 1, 0, 512), (lam_multiply, 2, 256, 512)],
-          7: [(h_interleave, 1, 768, 1024, V), (h_interleave, 3, 0, 512, V), (lam_quantize, 2, 0, 512), (lam_multiply, 3, 0, 128), (h_quantize, 3, 0, 0, 512), (lam_quantize, 3, 0, 128)]}
+          6: [(h_interleave, 2, 384, 512, V), (lam_multiply, 1, 256, 512), (h_quantize, 2, 0, 0, 256), (h_quantize, 2, 0, 256, 384), (lam_multiply, 2, 0, 256), (h_quantize, 2, 384, 384, 512), (lam_quantize, 1, 0, 512), (lam_multiply, 2, 256, 512)],
+          7: [(h_interleave, 3, 0, 512, V), (lam_quantize, 2, 0, 512), (lam_multiply, 3, 0, 128), (h_quantize, 3, 0, 0, 512), (lam_quantize, 3, 0, 128)]}
         fill_g = {0: [(v_interleave, 640, 1024, G)], 1: [(h_interleave, 0, 0, 384, G)], 2: [(h_interleave, 0, 384, 768, G)], 3: [(h_interleave, 1, 0, 384, G)], 4: [(h_interleave, 1, 384, 768, G)], 5: [(h_interleave, 2, 0, 384, G)]}
-        fill_s = {0: [(v_interleave, 512, 640, S)], 5: [(h_interleave, 0, 768, 1024, S), (h_interleave, 2, 384, 512, S)]}
+        fill_s = {5: [(h_interleave, 0, 768, 1024, S)]}
         def run(items):
             for item in items:
                 item[0](*item[1:])
@@ -319,8 +322,10 @@ def tile_lambdarank_head_gradient_s11_kernel(tc, d_bytes, d_scale, v, delta, ipw
                 turn(2 * p + 4)
                 turn(2 * p + 5)
             if p + 3 < STEPS:
-                widen(2 * p + 6)
-                widen(2 * p + 7)
+                if p in (2,):
+                    widen(2 * p + 6)
+                else:
+                    widen(2 * p + 6, 2)
             run(fill_s.get(p, []))
             run(fill_g.get(p, []))
             if p + 2 < STEPS:
@@ -335,6 +340,7 @@ def tile_lambdarank_head_gradient_s11_kernel(tc, d_bytes, d_scale, v, delta, ipw
             encode(j, 1)
         h_interleave(2, 512, 768, S)
         h_interleave(3, 512, 768, S)
+        h_interleave(1, 768, 1024, S)
         for s in range(3):
             for m in range(QTILES):
                 update(s, m, 0, 512)

@@ -23,18 +23,15 @@ GROUP = P * PACK
 GROUPS = PAIRS // GROUP
 PASSES = RAW // GROUP
 BANK = 512
+BANKS = 8
 HALVES = FEATS // BANK
 TILES = PAIRS // P
 STEPS = TILES // 2
 QTILES = RANKERS // P
-BANKS = 8
-CHUNK = 256
-CHUNKS = FEATS // CHUNK
-
-GRPBUFS = 7
-TURN_BANKS = 0
-TURN_FROM = 99
-SUMS_IN_TURN = ()
+WORDS = PASSES * P
+WINDOW = 384
+QUARTER = FEATS // 4
+EARLY_PRODUCTS, LATE_PRODUCTS = 4, 6
 
 FLOPS = 2 * PAIRS * RAW * RANKERS + 2 * PAIRS * RAW * FEATS + 2 * RANKERS * PAIRS * FEATS
 
@@ -55,7 +52,7 @@ def tile_lambdarank_head_gradient_s11_kernel(tc, d_bytes, d_scale, v, delta, ipw
         raw = [keep.tile([P, PACK, RAW], U8, name=f"raw{s}", align_bytes=64) for s in range(GROUPS)]
         dlt = [keep.tile([P, PACK, RANKERS], BF16, name=f"dlt{s}", align_bytes=64) for s in range(GROUPS)]
         v_raw = [keep.tile([P, PACK, RANKERS], BF16, name=f"v_raw{g}", align_bytes=64) for g in range(PASSES)]
-        e_w = [keep.tile([P, PASSES, 2 * BANK], U8, name=f"e_w{h}", align_bytes=64) for h in range(HALVES)]
+        e_w = [keep.tile([P, PASSES, 2 * BANK], U8, name=f"e_w{half}", align_bytes=64) for half in range(HALVES)]
         e_s = keep.tile([P, PASSES, FEATS], U8, name="e_s", align_bytes=64)
         ipw_bf = keep.tile([P, GROUPS, PACK], BF16, name="ipw_bf")
         ipw_f = keep.tile([P, GROUPS, PACK], F32, name="ipw_f")
@@ -74,93 +71,112 @@ def tile_lambdarank_head_gradient_s11_kernel(tc, d_bytes, d_scale, v, delta, ipw
         def load_raw(s, first, stop):
             nc.sync.dma_start(out=raw[s][:, first:stop, :], in_=d_view[s][:, first:stop, :])
 
-        def load_words(h):
-            nc.sync.dma_start(out=e_w[h][:], in_=w_view[:, :, 2 * BANK * h : 2 * BANK * (h + 1)])
+        def load_words(half):
+            nc.sync.dma_start(out=e_w[half][:], in_=w_view[:, :, 2 * BANK * half : 2 * BANK * (half + 1)])
 
-        def load_scales():
-            for r in range(PACK):
-                nc.sync.dma_start(out=e_s[r:P:32].bitcast(I32), in_=s_view[r:16:PACK].bitcast(I32))
-
-        def load_v(g):
-            nc.sync.dma_start(out=v_raw[g][:], in_=v_view[g])
-
-        def load_dlt(s):
+        load_raw(0, 0, 1)
+        nc.scalar.dma_start(out=scale_kp[:], in_=d_scale.rearrange("o (g p t) -> p (o g) t", p=P, t=PACK))
+        nc.scalar.activation(out=table_out[:], in_=table_in[:], func=SIGMOID, scale=-1.0)
+        load_raw(0, 1, 2)
+        load_raw(0, 2, 4)
+        for r in range(PACK):
+            nc.sync.dma_start(out=e_s[r:P:32].bitcast(I32), in_=s_view[r:16:PACK].bitcast(I32))
+        load_words(0)
+        nc.sync.dma_start(out=ipw_bf[:], in_=ipw.rearrange("(s m t) -> m s t", m=P, t=PACK))
+        load_raw(1, 0, 2)
+        nc.sync.dma_start(out=v_raw[0][:], in_=v_view[0])
+        load_words(1)
+        load_raw(1, 2, 4)
+        nc.sync.dma_start(out=v_raw[1][:], in_=v_view[1])
+        load_raw(2, 0, 4)
+        nc.sync.dma_start(out=dlt[0][:], in_=dlt_view[0])
+        load_raw(3, 0, 4)
+        for s in range(1, GROUPS):
             nc.sync.dma_start(out=dlt[s][:], in_=dlt_view[s])
 
-        def load_ipw():
-            nc.sync.dma_start(out=ipw_bf[:], in_=ipw.rearrange("(s m t) -> m s t", m=P, t=PACK))
+        on_vector, on_scalar = nc.vector.tensor_copy, nc.scalar.copy
 
-        def next_bank(shape, turning=False):
-            if turning:
-                return psum.tile(shape, F32, name="turn_bank", bufs=TURN_BANKS)
-            return psum.tile(shape, F32, name="bank", bufs=BANKS - TURN_BANKS)
+        def window_tile(columns):
+            return work.tile([P, columns, PACK], BF16, name="window_tile", bufs=1, align_bytes=64)
 
-        def on_vector(out, in_):
-            nc.vector.tensor_copy(out=out, in_=in_)
+        def interleave(copy, planes):
+            grouped = work.tile([P, planes.shape[2], PACK], BF16, name="grouped", bufs=7, align_bytes=64)
+            copy(out=grouped[:].rearrange("p (c i) t -> p c t i", i=8), in_=planes.rearrange("p t (c i) -> p c t i", i=8))
+            return grouped
 
-        def on_scalar(out, in_):
-            nc.scalar.copy(out=out, in_=in_)
-
-        def on_gpsimd(out, in_):
-            nc.gpsimd.tensor_scalar(out=out, in0=in_, scalar1=1.0, scalar2=0.0, op0=MULT, op1=ADD)
-
-        def interleave(copy, planes, grouped):
-            if copy is on_gpsimd:
-                copy(grouped, planes.rearrange("p t n -> p n t"))
-            else:
-                copy(grouped.rearrange("p (c i) t -> p c t i", i=8), planes.rearrange("p t (c i) -> p c t i", i=8))
+        def interleave_in_window(planes):
+            grouped = window_tile(planes.shape[2])
+            nc.gpsimd.tensor_scalar(out=grouped[:], in0=planes.rearrange("p t n -> p n t"), scalar1=1.0, scalar2=0.0, op0=MULT, op1=ADD)
+            return grouped
 
         def quantize(codes, planes, grouped):
             nc.vector.quantize_mx(out=codes.bitcast(E4M3X4), scales=planes, in_=grouped)
 
-        def grouped_tile(copy, width, slot=False):
-            if copy is on_gpsimd or slot:
-                return work.tile([P, width, PACK], BF16, name="g_grp", bufs=1, align_bytes=64)
-            return work.tile([P, width, PACK], BF16, name="grp", bufs=GRPBUFS, align_bytes=64)
+        names = ["v"] + list(range(GROUPS))
+        codes = {name: keep.tile([P, FEATS], U32, name=f"codes_{name}", align_bytes=64) for name in names}
+        planes = {name: keep.tile([P, FEATS], U8, name=f"planes_{name}", align_bytes=64) for name in names}
+        h_raw = [keep.tile([P, PACK, FEATS], BF16, name=f"h_raw{s}", align_bytes=64) for s in range(GROUPS)]
+        grouped_from = {}
 
-        v_codes = keep.tile([P, PASSES * RANKERS], U32, name="v_codes", align_bytes=64)
-        v_planes = keep.tile([P, PASSES * RANKERS], U8, name="v_planes", align_bytes=64)
-        v_grp = {}
+        def rows_of(name, first, stop):
+            if name == "v":
+                g = first // RANKERS
+                return v_raw[g][:, :, first - g * RANKERS : stop - g * RANKERS]
+            return h_raw[name][:, :, first:stop]
 
-        def v_interleave(first, stop, copy, slot=False):
-            g = first // RANKERS
-            v_grp[first] = grouped_tile(copy, stop - first, slot)
-            interleave(copy, v_raw[g][:, :, first - g * RANKERS : stop - g * RANKERS], v_grp[first][:])
+        def group_columns(name, first, stop, copy):
+            grouped_from[name, first] = interleave(copy, rows_of(name, first, stop))
 
-        def v_quantize(base, first, stop):
-            quantize(v_codes[:, first:stop], v_planes[:, first:stop], v_grp[base][:, first - base : stop - base, :].rearrange("p n t -> p (n t)"))
+        def group_in_window(name, first, stop):
+            grouped_from[name, first] = interleave_in_window(rows_of(name, first, stop))
 
-        WORDS = PASSES * P
+        def quantize_columns(name, first, stop, origin=None):
+            origin = first if origin is None else origin
+            grouped = grouped_from[name, origin][:, first - origin : stop - origin, :]
+            quantize(codes[name][:, first:stop], planes[name][:, first:stop], grouped.rearrange("p n t -> p (n t)"))
+
+        def quantize_window(name, first, stop):
+            cut = first + QUARTER if first % QUARTER == 0 else stop - QUARTER
+            quantize_columns(name, first, cut, first)
+            quantize_columns(name, cut, stop, first)
+
         d_codes = [keep.tile([P, 2 * WORDS], U32, name=f"d_codes{p}", align_bytes=64) for p in range(STEPS)]
         d_planes = [keep.tile([P, 2 * WORDS], U8, name=f"d_planes{p}", align_bytes=64) for p in range(STEPS)]
-        wide, wide_all, turned, d_grp = {}, {}, {}, {}
+        wide, turned, d_grp = {}, {}, {}
+        UNITS = 2 * PASSES
 
-        def widen(j, tiles=1, copy=on_scalar, first=0, stop=RAW):
-            if first == 0:
-                both = work.tile([P, tiles, RAW], BF16, name="wide", bufs=3, align_bytes=64)
-                for i in range(tiles):
-                    wide[j + i] = both[:, i, :]
-                wide_all[j] = both
-            t = j % PACK
-            copy(wide_all[j][:, :, first:stop], raw[j // PACK][:, t : t + tiles, first:stop].bitcast(FP8))
+        def new_wide(j, tiles):
+            both = work.tile([P, tiles, RAW], BF16, name="wide", bufs=3, align_bytes=64)
+            for i in range(tiles):
+                wide[j + i] = both[:, i, :]
+            return both
+
+        def d_bytes_of(j, tiles):
+            return raw[j // PACK][:, j % PACK : j % PACK + tiles, :].bitcast(FP8)
+
+        def widen(j, tiles):
+            nc.scalar.copy(out=new_wide(j, tiles)[:], in_=d_bytes_of(j, tiles))
 
         def turn(j, first=0, stop=PASSES):
-            bank = next_bank([P, 2, PASSES, P], j >= TURN_FROM)
+            bank = psum.tile([P, 2, PASSES, P], F32, name="bank")
             words = wide[j].bitcast(F32)
             for g in range(first, stop):
                 turned[j, g] = bank
                 for u in range(2):
-                    nc.tensor.transpose(bank[:, u, g, :], words[:, 256 * g + u : 256 * (g + 1) : 2], ident[:])
+                    nc.tensor.transpose(bank[:, u, g, :], words[:, 2 * P * g + u : 2 * P * (g + 1) : 2], ident[:])
 
         def d_grouped(first, stop):
-            if first < 2 * PASSES:
+            if first < UNITS:
                 if first not in d_grp:
-                    d_grp[first] = work.tile([P, GROUP], BF16, name="g_grp" if first == 2 else "d_first", bufs=1 if first == 2 else 3, align_bytes=64)
-                return d_grp[first][:]
-            start = first - first % (2 * PASSES)
-            if start not in d_grp:
-                d_grp[start] = work.tile([P, 2 * RAW], BF16, name="d_grp", bufs=2, align_bytes=64)
-            return d_grp[start][:, GROUP * (first - start) : GROUP * (stop - start)]
+                    if first == PASSES:
+                        d_grp[first] = window_tile(P)
+                    else:
+                        d_grp[first] = work.tile([P, P, PACK], BF16, name="d_first", bufs=UNITS - 1, align_bytes=64)
+                return d_grp[first][:].rearrange("p r t -> p (r t)")
+            origin = first - first % UNITS
+            if origin not in d_grp:
+                d_grp[origin] = work.tile([P, 2 * RAW], BF16, name="d_grp", bufs=2, align_bytes=64)
+            return d_grp[origin][:, GROUP * (first - origin) : GROUP * (stop - origin)]
 
         def scale(j, first=0, stop=PASSES):
             n = stop - first
@@ -172,41 +188,39 @@ def tile_lambdarank_head_gradient_s11_kernel(tc, d_bytes, d_scale, v, delta, ipw
             )
 
         def d_quantize(first, stop):
-            p = first // (2 * PASSES)
-            cols = slice(P * (first - 2 * PASSES * p), P * (stop - 2 * PASSES * p))
+            p = first // UNITS
+            cols = slice(P * (first - UNITS * p), P * (stop - UNITS * p))
             quantize(d_codes[p][:, cols], d_planes[p][:, cols], d_grouped(first, stop))
 
         def times_d(j, bank, moving):
             for g in range(PASSES):
                 cols = slice(WORDS * (j % 2) + g * P, WORDS * (j % 2) + (g + 1) * P)
-                codes, planes = moving(g)
+                rhs, rhs_scale = moving(g)
                 nc.tensor.matmul_mx(
-                    out=bank, lhsT=d_codes[j // 2][:, cols].bitcast(E4M3X4), lhsT_scale=d_planes[j // 2][:, cols],
-                    rhs=codes, rhs_scale=planes, start=(g == 0), stop=(g == PASSES - 1),
+                    out=bank[:], lhsT=d_codes[j // 2][:, cols].bitcast(E4M3X4), lhsT_scale=d_planes[j // 2][:, cols],
+                    rhs=rhs, rhs_scale=rhs_scale, start=(g == 0), stop=(g == PASSES - 1),
                 )
 
         sig = {}
-        h_raw = [keep.tile([P, PACK, FEATS], BF16, name=f"h_raw{s}", align_bytes=64) for s in range(GROUPS)]
 
         def score(j):
             s, t = divmod(j, PACK)
-            diff = next_bank([P, RANKERS])
-            times_d(j, diff[:], lambda g: (v_codes[:, g * RANKERS : (g + 1) * RANKERS].bitcast(E4M3X4), v_planes[:, g * RANKERS : (g + 1) * RANKERS]))
+            diff = psum.tile([P, RANKERS], F32, name="bank")
+            times_d(j, diff, lambda g: (codes["v"][:, g * RANKERS : (g + 1) * RANKERS].bitcast(E4M3X4), planes["v"][:, g * RANKERS : (g + 1) * RANKERS]))
             if t == 0:
                 sig[s] = work.tile([P, PACK, RANKERS], F32, name="sig", bufs=3, align_bytes=64)
             nc.scalar.activation(out=sig[s][:, t, :], in_=diff[:], func=SIGMOID, scale=-1.0)
 
         def encode(j, half):
             s, t = divmod(j, PACK)
-            encoded = next_bank([P, BANK])
-            times_d(j, encoded[:], lambda g: (e_w[half][:, g, :].bitcast(E2M1X4), e_s[:, g, BANK * half : BANK * (half + 1)]))
-            nc.scalar.activation(out=h_raw[s][:, t, BANK * half : BANK * (half + 1)], in_=encoded[:], func=COPY, scale=ipw_f[:, s, t : t + 1])
+            cols = slice(BANK * half, BANK * (half + 1))
+            encoded = psum.tile([P, BANK], F32, name="bank")
+            times_d(j, encoded, lambda g: (e_w[half][:, g, :].bitcast(E2M1X4), e_s[:, g, cols]))
+            nc.scalar.activation(out=h_raw[s][:, t, cols], in_=encoded[:], func=COPY, scale=ipw_f[:, s, t : t + 1])
 
         lam_codes = [keep.tile([P, RANKERS], U32, name=f"lam_codes{s}", align_bytes=64) for s in range(GROUPS)]
         lam_planes = [keep.tile([P, RANKERS], U8, name=f"lam_planes{s}", align_bytes=64) for s in range(GROUPS)]
-        h_codes = [keep.tile([P, FEATS], U32, name=f"h_codes{s}", align_bytes=64) for s in range(GROUPS)]
-        h_planes = [keep.tile([P, FEATS], U8, name=f"h_planes{s}", align_bytes=64) for s in range(GROUPS)]
-        lam, h_grp, encoded_group = {}, {}, {}
+        lam = {}
 
         def lam_multiply(s, first, stop):
             if first == 0:
@@ -221,150 +235,142 @@ def tile_lambdarank_head_gradient_s11_kernel(tc, d_bytes, d_scale, v, delta, ipw
         def lam_quantize(s, first, stop):
             quantize(lam_codes[s][:, first:stop], lam_planes[s][:, first:stop], lam[s][:, first:stop, :].rearrange("p n t -> p (n t)"))
 
-        def h_interleave(s, first, stop, copy):
-            h_grp[s, first] = grouped_tile(copy, stop - first)
-            interleave(copy, h_raw[s][:, :, first:stop], h_grp[s, first][:])
-
-        def h_quantize(s, base, first, stop):
-            quantize(h_codes[s][:, first:stop], h_planes[s][:, first:stop], h_grp[s, base][:, first - base : stop - base, :].rearrange("p n t -> p (n t)"))
-
         sums = {}
 
-        def update(s, m, first, stop):
-            if s == 0:
-                sums[m, first] = next_bank([P, stop - first], (m, first) in SUMS_IN_TURN)
+        def update(s, m, first, stop, order, share=1):
+            lead = m - m % share
+            opens, closes = s == order[0] and m == lead, s == order[-1] and m == lead + share - 1
+            if opens:
+                sums[lead, first] = psum.tile([P, share, stop - first], F32, name="bank")
             rows = slice(m * P, (m + 1) * P)
             nc.tensor.matmul_mx(
-                out=sums[m, first][:], lhsT=lam_codes[s][:, rows].bitcast(E4M3X4), lhsT_scale=lam_planes[s][:, rows],
-                rhs=h_codes[s][:, first:stop].bitcast(E4M3X4), rhs_scale=h_planes[s][:, first:stop],
-                start=(s == 0), stop=(s == GROUPS - 1),
+                out=sums[lead, first][:, m - lead, :], lhsT=lam_codes[s][:, rows].bitcast(E4M3X4), lhsT_scale=lam_planes[s][:, rows],
+                rhs=codes[s][:, first:stop].bitcast(E4M3X4), rhs_scale=planes[s][:, first:stop],
+                start=opens, stop=closes,
             )
 
-        def store(m, first, stop, copy):
-            res = work.tile([P, stop - first], F32, name=f"res{first}_{stop}", bufs=QTILES)
-            copy(res[:], sums[m, first][:])
-            nc.sync.dma_start(out=out[m * P : (m + 1) * P, first:stop], in_=res[:])
+        def store(lead, first, stop, copy, share=1):
+            res = work.tile([P, share, stop - first], F32, name=f"res{first}", bufs=QTILES // share)
+            copy(out=res[:], in_=sums[lead, first][:])
+            nc.sync.dma_start(out=out[lead * P : (lead + share) * P, first:stop].rearrange("(m p) c -> p m c", p=P), in_=res[:])
 
-        load_raw(0, 0, 1)
-        nc.scalar.dma_start(out=scale_kp[:], in_=d_scale.rearrange("o (g p t) -> p (o g) t", p=P, t=PACK))
-        nc.scalar.activation(out=table_out[:], in_=table_in[:], func=SIGMOID, scale=-1.0)
-        load_raw(0, 1, 2)
-        load_raw(0, 2, 4)
-        load_scales()
-        load_words(0)
-        load_ipw()
-        load_raw(1, 0, 2)
-        load_v(0)
-        load_words(1)
-        load_raw(1, 2, 4)
-        load_v(1)
-        load_raw(2, 0, 4)
-        load_dlt(0)
-        load_raw(3, 0, 4)
-        for s in range(1, GROUPS):
-            load_dlt(s)
+        products = []
+        for s in range(2):
+            for j in (PACK * s, PACK * s + 2):
+                products.extend((encode, i, half) for half in range(HALVES) for i in (j, j + 1))
+            products.extend((score, j) for j in range(PACK * s, PACK * (s + 1)))
+        for j in range(2 * PACK, TILES + 2, 2):
+            if j < TILES:
+                products.extend([(encode, j, 0), (encode, j + 1, 0), (score, j), (score, j + 1)])
+            if j > 2 * PACK:
+                products.extend([(encode, j - 2, 1), (encode, j - 1, 1)])
 
-        V, S, G = on_vector, on_scalar, on_gpsimd
-        widen(0, 1, V, 0, GROUP)
-        widen(0, 1, V, GROUP, RAW)
-        widen(1, 1, V)
-        widen(2)
-        widen(3)
-        turn(0, 0, 1)
-        turn(0, 1, 2)
-        turn(1)
-        turn(2)
-        turn(3)
+        def multiply(count):
+            for item in products[:count]:
+                item[0](*item[1:])
+            return products[count:]
+
+        windows = [("v", 0, WINDOW), ("v", FEATS - WINDOW, FEATS)]
+        for s in range(2):
+            windows.extend([(s, 0, WINDOW), (s, WINDOW, 2 * WINDOW)])
+        windows.append((2, 0, WINDOW))
+        lam_halves = [(s, first, first + RANKERS // 2) for s in range(GROUPS - 1) for first in (0, RANKERS // 2)]
+
+        first_tile = new_wide(0, 1)
+        on_scalar(out=first_tile[:, :, 0:GROUP], in_=d_bytes_of(0, 1)[:, :, 0:GROUP])
+        on_vector(out=first_tile[:, :, GROUP:RAW], in_=d_bytes_of(0, 1)[:, :, GROUP:RAW])
+        widen(1, 1)
+        widen(2, 1)
+        for g in range(PASSES):
+            turn(0, g, g + 1)
+        widen(3, 1)
+        for j in range(1, PACK):
+            turn(j)
         nc.scalar.copy(out=ipw_f[:], in_=ipw_bf[:])
         widen(4, 2)
-        v_interleave(384, 512, S)
+        group_columns("v", WINDOW, RANKERS, on_scalar)
         scale(0, 0, 1)
-        scale(0, 1, 2)
-        d_quantize(0, 1)
-        scale(1, 0, 1)
-        d_quantize(1, 2)
-        scale(1, 1, 2)
-        d_quantize(2, 3)
-        d_quantize(3, 4)
-        v_interleave(0, 384, G)
+        for unit in range(1, UNITS):
+            scale(unit // PASSES, unit % PASSES, unit % PASSES + 1)
+            d_quantize(unit - 1, unit)
+        d_quantize(UNITS - 1, UNITS)
+        group_in_window(*windows[0])
         scale(2)
         scale(3)
         d_quantize(4, 6)
-        v_quantize(384, 384, 512)
-        v_quantize(0, 0, 256)
-        v_quantize(0, 256, 384)
+        quantize_columns("v", WINDOW, RANKERS)
+        quantize_window(*windows[0])
         d_quantize(6, 8)
-        encode(0, 0)
-        encode(1, 0)
-        encode(0, 1)
-        encode(1, 1)
+        products = multiply(EARLY_PRODUCTS)
 
-        prods = [[(encode, 2, 0), (encode, 3, 0), (encode, 2, 1), (encode, 3, 1)],
-          [(score, 0), (score, 1), (score, 2), (score, 3)],
-          [(encode, 4, 0), (encode, 5, 0), (encode, 4, 1), (encode, 5, 1), (encode, 6, 0), (encode, 7, 0)],
-          [(encode, 6, 1), (encode, 7, 1), (score, 4), (score, 5), (score, 6), (score, 7)],
-          [(encode, 8, 0), (encode, 9, 0), (score, 8), (score, 9), (encode, 10, 0), (encode, 11, 0)],
-          [(score, 10), (score, 11), (encode, 8, 1), (encode, 9, 1), (encode, 12, 0), (encode, 13, 0)],
-          [(score, 12), (score, 13), (encode, 10, 1), (encode, 11, 1)],
-          [(encode, 14, 0), (encode, 15, 0), (score, 14), (score, 15)]]
-        fill_v = {0: [(v_interleave, 512, 640, V), (v_quantize, 640, 640, 768), (v_quantize, 512, 512, 640), (v_quantize, 640, 768, 1024)], 1: [(h_quantize, 0, 0, 0, 256), (h_quantize, 0, 0, 256, 384)],
-          2: [(widen, 11, 1, V), (lam_multiply, 0, 0, 256), (h_quantize, 0, 384, 384, 512), (h_quantize, 0, 384, 512, 768)], 3: [(lam_multiply, 0, 256, 512), (h_quantize, 1, 0, 0, 256), (h_quantize, 1, 0, 256, 384)],
-          4: [(lam_multiply, 1, 0, 256), (h_quantize, 1, 384, 384, 512), (h_quantize, 1, 384, 512, 768)], 5: [(lam_quantize, 0, 0, 512)],
-          6: [(h_interleave, 2, 384, 512, V), (lam_multiply, 1, 256, 512), (h_quantize, 2, 0, 0, 256), (h_quantize, 2, 0, 256, 384), (lam_multiply, 2, 0, 256), (h_quantize, 2, 384, 384, 512), (lam_quantize, 1, 0, 512), (lam_multiply, 2, 256, 512)],
-          7: [(h_interleave, 3, 0, 512, V), (lam_quantize, 2, 0, 512), (lam_multiply, 3, 0, 128), (h_quantize, 3, 0, 0, 512), (lam_quantize, 3, 0, 128)]}
-        fill_g = {0: [(v_interleave, 640, 1024, G)], 1: [(h_interleave, 0, 0, 384, G)], 2: [(h_interleave, 0, 384, 768, G)], 3: [(h_interleave, 1, 0, 384, G)], 4: [(h_interleave, 1, 384, 768, G)], 5: [(h_interleave, 2, 0, 384, G)]}
-        fill_s = {5: [(h_interleave, 0, 768, 1024, S)]}
-        def run(items):
-            for item in items:
-                item[0](*item[1:])
-        for p in range(STEPS):
-            if p + 2 < STEPS:
-                turn(2 * p + 4)
-                turn(2 * p + 5)
-            if p + 3 < STEPS:
-                if p in (2,):
-                    widen(2 * p + 6)
-                else:
-                    widen(2 * p + 6, 2)
-            run(fill_s.get(p, []))
-            run(fill_g.get(p, []))
-            if p + 2 < STEPS:
-                scale(2 * p + 4)
-                scale(2 * p + 5)
-            run(prods[p])
-            run(fill_v.get(p, []))
-            if p + 2 < STEPS:
-                d_quantize(4 * p + 8, 4 * p + 12)
+        for p in range(2, STEPS):
+            window = windows[p - 1]
+            turn(2 * p)
+            turn(2 * p + 1)
+            if p + 1 < STEPS:
+                widen(2 * p + 2, 2)
+            else:
+                group_columns(0, 2 * WINDOW, FEATS, on_scalar)
+            group_in_window(*window)
+            scale(2 * p)
+            scale(2 * p + 1)
+            products = multiply(EARLY_PRODUCTS if p < 4 else LATE_PRODUCTS)
+            if p == 2:
+                group_columns("v", RANKERS, FEATS - WINDOW, on_vector)
+                quantize_columns("v", FEATS - WINDOW, FEATS - QUARTER)
+                quantize_columns("v", RANKERS, FEATS - WINDOW)
+                quantize_columns("v", FEATS - QUARTER, FEATS, FEATS - WINDOW)
+            else:
+                if p >= 4:
+                    lam_multiply(*lam_halves[p - 4])
+                quantize_window(*window)
+            d_quantize(UNITS * p, UNITS * (p + 1))
 
-        for j in range(12, 16):
-            encode(j, 1)
-        h_interleave(2, 512, 768, S)
-        h_interleave(3, 512, 768, S)
-        h_interleave(1, 768, 1024, S)
-        for s in range(3):
+        last = GROUPS - 1
+        in_order = tuple(range(GROUPS))
+        products = multiply(EARLY_PRODUCTS)
+        lam_quantize(0, 0, RANKERS)
+        group_columns(2, WINDOW, BANK, on_vector)
+        lam_multiply(*lam_halves[4])
+        quantize_columns(2, WINDOW, BANK)
+        lam_quantize(1, 0, RANKERS)
+        lam_multiply(*lam_halves[5])
+        products = multiply(len(products))
+        group_columns(last, 0, BANK, on_vector)
+        lam_quantize(2, 0, RANKERS)
+        lam_multiply(last, 0, P)
+        quantize_columns(last, 0, BANK)
+        lam_quantize(last, 0, P)
+
+        third, fourth = BANK, BANK + QUARTER
+        for s in (2, last):
+            group_columns(s, third, fourth, on_scalar)
+        for s in range(last):
             for m in range(QTILES):
-                update(s, m, 0, 512)
+                update(s, m, 0, BANK, in_order)
         for m in range(QTILES):
             if m + 1 < QTILES:
-                lam_multiply(3, 128 * (m + 1), 128 * (m + 2))
+                lam_multiply(last, P * (m + 1), P * (m + 2))
                 if m == 0:
-                    h_quantize(0, 768, 768, 1024)
+                    quantize_columns(0, fourth, FEATS)
                 else:
-                    h_quantize(m + 1, 512, 512, 768)
-                lam_quantize(3, 128 * (m + 1), 128 * (m + 2))
-            update(3, m, 0, 512)
-            store(m, 0, 512, S)
+                    quantize_columns(m + 1, third, fourth)
+                lam_quantize(last, P * (m + 1), P * (m + 2))
+            update(last, m, 0, BANK, in_order)
+            store(m, 0, BANK, on_scalar)
+            if m == 0:
+                group_columns(1, fourth, FEATS, on_scalar)
             for n in range(QTILES):
-                update(m, n, 512, 768)
-        h_interleave(2, 768, 1024, V)
-        h_quantize(1, 768, 768, 1024)
-        h_interleave(3, 768, 1024, V)
-        h_quantize(2, 768, 768, 1024)
-        for m in range(QTILES):
-            store(m, 512, 768, S)
-        h_quantize(3, 768, 768, 1024)
-        for s in range(GROUPS):
+                update(m, n, third, fourth, in_order, 2)
+        for s in (2, last):
+            group_columns(s, fourth, FEATS, on_vector)
+        ready = (0, 2, 1, last)
+        for s in ready[1:]:
+            quantize_columns(s, fourth, FEATS)
+        for lead in (0, 2):
+            store(lead, third, fourth, on_scalar, 2)
+        for s in ready:
             for m in range(QTILES):
-                update(s, m, 768, 1024)
+                update(s, m, fourth, FEATS, ready)
         for m in range(QTILES):
-            store(m, 768, 1024, S if m % 2 else V)
+            store(m, fourth, FEATS, on_scalar if m % 2 else on_vector)

@@ -80,13 +80,13 @@ def tile_lambdarank_head_gradient_s11_kernel(tc, d_bytes, d_scale, v, delta, ipw
         load_raw(0, 1, 2)
         load_raw(0, 2, 4)
         for r in range(PACK):
-            nc.sync.dma_start(out=e_s[r:P:32].bitcast(I32), in_=s_view[r:16:PACK].bitcast(I32))
+            nc.gpsimd.dma_start(out=e_s[r:P:32].bitcast(I32), in_=s_view[r:16:PACK].bitcast(I32))
         load_words(0)
         nc.sync.dma_start(out=ipw_bf[:], in_=ipw.rearrange("(s m t) -> m s t", m=P, t=PACK))
         load_raw(1, 0, 2)
         nc.sync.dma_start(out=v_raw[0][:], in_=v_view[0])
-        load_words(1)
         load_raw(1, 2, 4)
+        load_words(1)
         nc.sync.dma_start(out=v_raw[1][:], in_=v_view[1])
         load_raw(2, 0, 4)
         nc.sync.dma_start(out=dlt[0][:], in_=dlt_view[0])
@@ -277,8 +277,9 @@ def tile_lambdarank_head_gradient_s11_kernel(tc, d_bytes, d_scale, v, delta, ipw
         lam_halves = [(s, first, first + RANKERS // 2) for s in range(GROUPS - 1) for first in (0, RANKERS // 2)]
 
         first_tile = new_wide(0, 1)
-        on_scalar(out=first_tile[:, :, 0:GROUP], in_=d_bytes_of(0, 1)[:, :, 0:GROUP])
-        on_vector(out=first_tile[:, :, GROUP:RAW], in_=d_bytes_of(0, 1)[:, :, GROUP:RAW])
+        for first in range(0, RAW, QUARTER):
+            copy = on_scalar if first % GROUP else on_vector
+            copy(out=first_tile[:, :, first : first + QUARTER], in_=d_bytes_of(0, 1)[:, :, first : first + QUARTER])
         widen(1, 1)
         widen(2, 1)
         for g in range(PASSES):
@@ -289,6 +290,7 @@ def tile_lambdarank_head_gradient_s11_kernel(tc, d_bytes, d_scale, v, delta, ipw
         nc.scalar.copy(out=ipw_f[:], in_=ipw_bf[:])
         widen(4, 2)
         group_columns("v", WINDOW, RANKERS, on_scalar)
+        widen(6, 2)
         scale(0, 0, 1)
         for unit in range(1, UNITS):
             scale(unit // PASSES, unit % PASSES, unit % PASSES + 1)
@@ -307,23 +309,21 @@ def tile_lambdarank_head_gradient_s11_kernel(tc, d_bytes, d_scale, v, delta, ipw
             window = windows[p - 1]
             turn(2 * p)
             turn(2 * p + 1)
-            if p + 1 < STEPS:
-                widen(2 * p + 2, 2)
+            if p + 2 < STEPS:
+                widen(2 * p + 4, 2)
             else:
-                group_columns(0, 2 * WINDOW, FEATS, on_scalar)
+                group_columns(p + 2 - STEPS, 2 * WINDOW, FEATS, on_scalar)
+            if p == 2:
+                group_columns("v", RANKERS, FEATS - WINDOW, on_scalar)
             group_in_window(*window)
             scale(2 * p)
             scale(2 * p + 1)
             products = multiply(EARLY_PRODUCTS if p < 4 else LATE_PRODUCTS)
             if p == 2:
-                group_columns("v", RANKERS, FEATS - WINDOW, on_vector)
-                quantize_columns("v", FEATS - WINDOW, FEATS - QUARTER)
                 quantize_columns("v", RANKERS, FEATS - WINDOW)
-                quantize_columns("v", FEATS - QUARTER, FEATS, FEATS - WINDOW)
-            else:
-                if p >= 4:
-                    lam_multiply(*lam_halves[p - 4])
-                quantize_window(*window)
+            if p >= 4:
+                lam_multiply(*lam_halves[p - 4])
+            quantize_window(*window)
             d_quantize(UNITS * p, UNITS * (p + 1))
 
         last = GROUPS - 1
@@ -358,19 +358,16 @@ def tile_lambdarank_head_gradient_s11_kernel(tc, d_bytes, d_scale, v, delta, ipw
                 lam_quantize(last, P * (m + 1), P * (m + 2))
             update(last, m, 0, BANK, in_order)
             store(m, 0, BANK, on_scalar)
-            if m == 0:
-                group_columns(1, fourth, FEATS, on_scalar)
             for n in range(QTILES):
                 update(m, n, third, fourth, in_order, 2)
         for s in (2, last):
             group_columns(s, fourth, FEATS, on_vector)
-        ready = (0, 2, 1, last)
-        for s in ready[1:]:
-            quantize_columns(s, fourth, FEATS)
-        for lead in (0, 2):
-            store(lead, third, fourth, on_scalar, 2)
-        for s in ready:
+            quantize_columns(s - 1, fourth, FEATS)
+        quantize_columns(last, fourth, FEATS)
+        store(0, third, fourth, on_scalar, 2)
+        store(2, third, fourth, on_vector, 2)
+        for s in range(GROUPS):
             for m in range(QTILES):
-                update(s, m, fourth, FEATS, ready)
+                update(s, m, fourth, FEATS, in_order)
         for m in range(QTILES):
             store(m, fourth, FEATS, on_scalar if m % 2 else on_vector)

@@ -76,17 +76,16 @@ def tile_lambdarank_head_gradient_s11_kernel(tc, d_bytes, d_scale, v, delta, ipw
 
         load_raw(0, 0, 1)
         nc.scalar.dma_start(out=scale_kp[:], in_=d_scale.rearrange("o (g p t) -> p (o g) t", p=P, t=PACK))
+        nc.scalar.dma_start(out=ipw_bf[:], in_=ipw.rearrange("(s m t) -> m s t", m=P, t=PACK))
         nc.scalar.activation(out=table_out[:], in_=table_in[:], func=SIGMOID, scale=-1.0)
-        load_raw(0, 1, 2)
-        load_raw(0, 2, 4)
-        for r in range(PACK):
-            nc.gpsimd.dma_start(out=e_s[r:P:32].bitcast(I32), in_=s_view[r:16:PACK].bitcast(I32))
+        load_raw(0, 1, 4)
         load_words(0)
-        nc.sync.dma_start(out=ipw_bf[:], in_=ipw.rearrange("(s m t) -> m s t", m=P, t=PACK))
         load_raw(1, 0, 2)
+        for r in range(PACK):
+            nc.sync.dma_start(out=e_s[r:P:32].bitcast(I32), in_=s_view[r:16:PACK].bitcast(I32))
         nc.sync.dma_start(out=v_raw[0][:], in_=v_view[0])
-        load_raw(1, 2, 4)
         load_words(1)
+        load_raw(1, 2, 4)
         nc.sync.dma_start(out=v_raw[1][:], in_=v_view[1])
         load_raw(2, 0, 4)
         nc.sync.dma_start(out=dlt[0][:], in_=dlt_view[0])
@@ -313,17 +312,19 @@ def tile_lambdarank_head_gradient_s11_kernel(tc, d_bytes, d_scale, v, delta, ipw
                 widen(2 * p + 4, 2)
             else:
                 group_columns(p + 2 - STEPS, 2 * WINDOW, FEATS, on_scalar)
-            if p == 2:
-                group_columns("v", RANKERS, FEATS - WINDOW, on_scalar)
             group_in_window(*window)
             scale(2 * p)
             scale(2 * p + 1)
             products = multiply(EARLY_PRODUCTS if p < 4 else LATE_PRODUCTS)
             if p == 2:
+                group_columns("v", RANKERS, FEATS - WINDOW, on_vector)
+                quantize_columns("v", FEATS - WINDOW, FEATS - QUARTER)
                 quantize_columns("v", RANKERS, FEATS - WINDOW)
-            if p >= 4:
-                lam_multiply(*lam_halves[p - 4])
-            quantize_window(*window)
+                quantize_columns("v", FEATS - QUARTER, FEATS, FEATS - WINDOW)
+            else:
+                if p >= 4:
+                    lam_multiply(*lam_halves[p - 4])
+                quantize_window(*window)
             d_quantize(UNITS * p, UNITS * (p + 1))
 
         last = GROUPS - 1

@@ -53,7 +53,7 @@ def tile_lambdarank_head_gradient_s11_kernel(tc, d_bytes, d_scale, v, delta, ipw
         dlt = [keep.tile([P, PACK, RANKERS], BF16, name=f"dlt{s}", align_bytes=64) for s in range(GROUPS)]
         v_raw = [keep.tile([P, PACK, RANKERS], BF16, name=f"v_raw{g}", align_bytes=64) for g in range(PASSES)]
         e_w = [keep.tile([P, PASSES, 2 * BANK], U8, name=f"e_w{half}", align_bytes=64) for half in range(HALVES)]
-        e_s = keep.tile([P, PASSES, FEATS], U8, name="e_s", align_bytes=64)
+        e_s = [keep.tile([P, PASSES, BANK], U8, name=f"e_s{half}", align_bytes=64) for half in range(HALVES)]
         ipw_bf = keep.tile([P, GROUPS, PACK], BF16, name="ipw_bf")
         ipw_f = keep.tile([P, GROUPS, PACK], F32, name="ipw_f")
 
@@ -66,7 +66,8 @@ def tile_lambdarank_head_gradient_s11_kernel(tc, d_bytes, d_scale, v, delta, ipw
         table_in = keep.tile([P, 1], F32, name="table_in")
         table_out = keep.tile([P, 1], F32, name="table_out")
         nc.vector.memset(table_in[:], 0.0)
-        nc.vector.memset(e_s[:].bitcast(I32), 0)
+        for half in range(HALVES):
+            nc.vector.memset(e_s[half][:].bitcast(I32), 0)
 
         def load_raw(s, first, stop):
             nc.sync.dma_start(out=raw[s][:, first:stop, :], in_=d_view[s][:, first:stop, :])
@@ -74,18 +75,22 @@ def tile_lambdarank_head_gradient_s11_kernel(tc, d_bytes, d_scale, v, delta, ipw
         def load_words(half):
             nc.sync.dma_start(out=e_w[half][:], in_=w_view[:, :, 2 * BANK * half : 2 * BANK * (half + 1)])
 
+        def load_scales(half):
+            for r in range(PACK):
+                nc.sync.dma_start(out=e_s[half][r:P:32].bitcast(I32), in_=s_view[r:16:PACK, :, BANK * half : BANK * (half + 1)].bitcast(I32))
+
         load_raw(0, 0, 1)
         nc.scalar.dma_start(out=scale_kp[:], in_=d_scale.rearrange("o (g p t) -> p (o g) t", p=P, t=PACK))
         nc.scalar.dma_start(out=ipw_bf[:], in_=ipw.rearrange("(s m t) -> m s t", m=P, t=PACK))
         nc.scalar.activation(out=table_out[:], in_=table_in[:], func=SIGMOID, scale=-1.0)
         load_raw(0, 1, 4)
+        load_scales(0)
         load_words(0)
         load_raw(1, 0, 2)
-        for r in range(PACK):
-            nc.sync.dma_start(out=e_s[r:P:32].bitcast(I32), in_=s_view[r:16:PACK].bitcast(I32))
         nc.sync.dma_start(out=v_raw[0][:], in_=v_view[0])
-        load_words(1)
         load_raw(1, 2, 4)
+        load_scales(1)
+        load_words(1)
         nc.sync.dma_start(out=v_raw[1][:], in_=v_view[1])
         load_raw(2, 0, 4)
         nc.sync.dma_start(out=dlt[0][:], in_=dlt_view[0])
@@ -214,7 +219,7 @@ def tile_lambdarank_head_gradient_s11_kernel(tc, d_bytes, d_scale, v, delta, ipw
             s, t = divmod(j, PACK)
             cols = slice(BANK * half, BANK * (half + 1))
             encoded = psum.tile([P, BANK], F32, name="bank")
-            times_d(j, encoded, lambda g: (e_w[half][:, g, :].bitcast(E2M1X4), e_s[:, g, cols]))
+            times_d(j, encoded, lambda g: (e_w[half][:, g, :].bitcast(E2M1X4), e_s[half][:, g, :]))
             nc.scalar.activation(out=h_raw[s][:, t, cols], in_=encoded[:], func=COPY, scale=ipw_f[:, s, t : t + 1])
 
         lam_codes = [keep.tile([P, RANKERS], U32, name=f"lam_codes{s}", align_bytes=64) for s in range(GROUPS)]

@@ -31,7 +31,6 @@ QTILES = RANKERS // P
 WORDS = PASSES * P
 WINDOW = 384
 QUARTER = FEATS // 4
-EARLY_PRODUCTS, LATE_PRODUCTS = 4, 6
 
 FLOPS = 2 * PAIRS * RAW * RANKERS + 2 * PAIRS * RAW * FEATS + 2 * RANKERS * PAIRS * FEATS
 
@@ -53,7 +52,7 @@ def tile_lambdarank_head_gradient_s11_kernel(tc, d_bytes, d_scale, v, delta, ipw
         dlt = [keep.tile([P, PACK, RANKERS], BF16, name=f"dlt{s}", align_bytes=64) for s in range(GROUPS)]
         v_raw = [keep.tile([P, PACK, RANKERS], BF16, name=f"v_raw{g}", align_bytes=64) for g in range(PASSES)]
         e_w = [keep.tile([P, PASSES, 2 * BANK], U8, name=f"e_w{half}", align_bytes=64) for half in range(HALVES)]
-        e_s = [keep.tile([P, PASSES, BANK], U8, name=f"e_s{half}", align_bytes=64) for half in range(HALVES)]
+        e_s = keep.tile([P, PASSES, FEATS], U8, name="e_s", align_bytes=64)
         ipw_bf = keep.tile([P, GROUPS, PACK], BF16, name="ipw_bf")
         ipw_f = keep.tile([P, GROUPS, PACK], F32, name="ipw_f")
 
@@ -65,9 +64,16 @@ def tile_lambdarank_head_gradient_s11_kernel(tc, d_bytes, d_scale, v, delta, ipw
 
         table_in = keep.tile([P, 1], F32, name="table_in")
         table_out = keep.tile([P, 1], F32, name="table_out")
+        warm = keep.tile([P, BANK], BF16, name="warm", align_bytes=64)
+        nc.vector.memset(warm[:].bitcast(I32), 0)
         nc.vector.memset(table_in[:], 0.0)
-        for half in range(HALVES):
-            nc.vector.memset(e_s[half][:].bitcast(I32), 0)
+
+        def warm_up(count):
+            idle = psum.tile([P, BANK], F32, name="bank")
+            for i in range(count):
+                nc.tensor.matmul(out=idle[:], lhsT=warm[:, :P], rhs=warm[:], start=True, stop=True)
+
+        nc.vector.memset(e_s[:].bitcast(I32), 0)
 
         def load_raw(s, first, stop):
             nc.sync.dma_start(out=raw[s][:, first:stop, :], in_=d_view[s][:, first:stop, :])
@@ -75,22 +81,19 @@ def tile_lambdarank_head_gradient_s11_kernel(tc, d_bytes, d_scale, v, delta, ipw
         def load_words(half):
             nc.sync.dma_start(out=e_w[half][:], in_=w_view[:, :, 2 * BANK * half : 2 * BANK * (half + 1)])
 
-        def load_scales(half):
-            for r in range(PACK):
-                nc.sync.dma_start(out=e_s[half][r:P:32].bitcast(I32), in_=s_view[r:16:PACK, :, BANK * half : BANK * (half + 1)].bitcast(I32))
-
         load_raw(0, 0, 1)
         nc.scalar.dma_start(out=scale_kp[:], in_=d_scale.rearrange("o (g p t) -> p (o g) t", p=P, t=PACK))
-        nc.scalar.dma_start(out=ipw_bf[:], in_=ipw.rearrange("(s m t) -> m s t", m=P, t=PACK))
         nc.scalar.activation(out=table_out[:], in_=table_in[:], func=SIGMOID, scale=-1.0)
-        load_raw(0, 1, 4)
-        load_scales(0)
+        load_raw(0, 1, 2)
+        load_raw(0, 2, 4)
+        for r in range(PACK):
+            nc.sync.dma_start(out=e_s[r:P:32].bitcast(I32), in_=s_view[r:16:PACK].bitcast(I32))
         load_words(0)
+        nc.sync.dma_start(out=ipw_bf[:], in_=ipw.rearrange("(s m t) -> m s t", m=P, t=PACK))
         load_raw(1, 0, 2)
         nc.sync.dma_start(out=v_raw[0][:], in_=v_view[0])
-        load_raw(1, 2, 4)
-        load_scales(1)
         load_words(1)
+        load_raw(1, 2, 4)
         nc.sync.dma_start(out=v_raw[1][:], in_=v_view[1])
         load_raw(2, 0, 4)
         nc.sync.dma_start(out=dlt[0][:], in_=dlt_view[0])
@@ -100,49 +103,52 @@ def tile_lambdarank_head_gradient_s11_kernel(tc, d_bytes, d_scale, v, delta, ipw
 
         on_vector, on_scalar = nc.vector.tensor_copy, nc.scalar.copy
 
-        def window_tile(columns):
-            return work.tile([P, columns, PACK], BF16, name="window_tile", bufs=1, align_bytes=64)
+        names = ["v"] + [(kind, s) for kind in ("h", "lam") for s in range(GROUPS)]
+        width = {name: RANKERS if name[0] == "lam" else FEATS for name in names}
+        codes = {name: keep.tile([P, width[name]], U32, name=f"codes{i}", align_bytes=64) for i, name in enumerate(names)}
+        planes = {name: keep.tile([P, width[name]], U8, name=f"planes{i}", align_bytes=64) for i, name in enumerate(names)}
+        h_raw = [keep.tile([P, PACK, (FEATS, BANK, BANK)[s]], BF16, name=f"h_raw{s}", align_bytes=64) for s in range(GROUPS - 1)]
+        grouped = {}
 
-        def interleave(copy, planes):
-            grouped = work.tile([P, planes.shape[2], PACK], BF16, name="grouped", bufs=7, align_bytes=64)
-            copy(out=grouped[:].rearrange("p (c i) t -> p c t i", i=8), in_=planes.rearrange("p t (c i) -> p c t i", i=8))
-            return grouped
-
-        def interleave_in_window(planes):
-            grouped = window_tile(planes.shape[2])
-            nc.gpsimd.tensor_scalar(out=grouped[:], in0=planes.rearrange("p t n -> p n t"), scalar1=1.0, scalar2=0.0, op0=MULT, op1=ADD)
-            return grouped
-
-        def quantize(codes, planes, grouped):
-            nc.vector.quantize_mx(out=codes.bitcast(E4M3X4), scales=planes, in_=grouped)
-
-        names = ["v"] + list(range(GROUPS))
-        codes = {name: keep.tile([P, FEATS], U32, name=f"codes_{name}", align_bytes=64) for name in names}
-        planes = {name: keep.tile([P, FEATS], U8, name=f"planes_{name}", align_bytes=64) for name in names}
-        h_raw = [keep.tile([P, PACK, FEATS], BF16, name=f"h_raw{s}", align_bytes=64) for s in range(GROUPS)]
-        grouped_from = {}
+        def new_grouped(name, first, stop, tag, bufs):
+            tile = work.tile([P, stop - first, PACK], BF16, name=tag, bufs=bufs, align_bytes=64)
+            grouped[name, first] = tile
+            return tile
 
         def rows_of(name, first, stop):
             if name == "v":
                 g = first // RANKERS
                 return v_raw[g][:, :, first - g * RANKERS : stop - g * RANKERS]
-            return h_raw[name][:, :, first:stop]
+            return h_raw[name[1]][:, :, first:stop]
 
-        def group_columns(name, first, stop, copy):
-            grouped_from[name, first] = interleave(copy, rows_of(name, first, stop))
+        def interleave(name, first, stop, copy):
+            tile = new_grouped(name, first, stop, "grouped", 6)
+            copy(out=tile[:].rearrange("p (c i) t -> p c t i", i=8), in_=rows_of(name, first, stop).rearrange("p t (c i) -> p c t i", i=8))
 
-        def group_in_window(name, first, stop):
-            grouped_from[name, first] = interleave_in_window(rows_of(name, first, stop))
+        def lam_product(engine, tile, s, first, stop):
+            engine.tensor_tensor(
+                out=tile[:].rearrange("p (c i) t -> p c t i", i=2),
+                in0=sig[s][:, :, first:stop].rearrange("p t (c i) -> p c t i", i=2),
+                in1=dlt[s][:, :, first:stop].rearrange("p t (c i) -> p c t i", i=2),
+                op=MULT,
+            )
 
-        def quantize_columns(name, first, stop, origin=None):
-            origin = first if origin is None else origin
-            grouped = grouped_from[name, origin][:, first - origin : stop - origin, :]
-            quantize(codes[name][:, first:stop], planes[name][:, first:stop], grouped.rearrange("p n t -> p (n t)"))
+        def in_window(jobs):
+            for i, (name, first, stop) in enumerate(jobs):
+                tile = new_grouped(name, first, stop, f"window{i}", 1)
+                if name[0] == "lam":
+                    lam_product(nc.gpsimd, tile, name[1], first, stop)
+                else:
+                    nc.gpsimd.tensor_scalar(out=tile[:], in0=rows_of(name, first, stop).rearrange("p t n -> p n t"), scalar1=1.0, scalar2=0.0, op0=MULT, op1=ADD)
 
-        def quantize_window(name, first, stop):
-            cut = first + QUARTER if first % QUARTER == 0 else stop - QUARTER
-            quantize_columns(name, first, cut, first)
-            quantize_columns(name, cut, stop, first)
+        def lam_on_vector(s, first, stop):
+            lam_product(nc.vector, new_grouped(("lam", s), first, stop, "lam", 2), s, first, stop)
+
+        def quantize(out, scales, in_):
+            nc.vector.quantize_mx(out=out.bitcast(E4M3X4), scales=scales, in_=in_)
+
+        def quantize_columns(name, first, stop):
+            quantize(codes[name][:, first:stop], planes[name][:, first:stop], grouped[name, first][:].rearrange("p n t -> p (n t)"))
 
         d_codes = [keep.tile([P, 2 * WORDS], U32, name=f"d_codes{p}", align_bytes=64) for p in range(STEPS)]
         d_planes = [keep.tile([P, 2 * WORDS], U8, name=f"d_planes{p}", align_bytes=64) for p in range(STEPS)]
@@ -173,7 +179,7 @@ def tile_lambdarank_head_gradient_s11_kernel(tc, d_bytes, d_scale, v, delta, ipw
             if first < UNITS:
                 if first not in d_grp:
                     if first == PASSES:
-                        d_grp[first] = window_tile(P)
+                        d_grp[first] = work.tile([P, P, PACK], BF16, name="window0", bufs=1, align_bytes=64)
                     else:
                         d_grp[first] = work.tile([P, P, PACK], BF16, name="d_first", bufs=UNITS - 1, align_bytes=64)
                 return d_grp[first][:].rearrange("p r t -> p (r t)")
@@ -196,89 +202,77 @@ def tile_lambdarank_head_gradient_s11_kernel(tc, d_bytes, d_scale, v, delta, ipw
             cols = slice(P * (first - UNITS * p), P * (stop - UNITS * p))
             quantize(d_codes[p][:, cols], d_planes[p][:, cols], d_grouped(first, stop))
 
-        def times_d(j, bank, moving):
+        def times_d(j, out, moving):
             for g in range(PASSES):
                 cols = slice(WORDS * (j % 2) + g * P, WORDS * (j % 2) + (g + 1) * P)
                 rhs, rhs_scale = moving(g)
                 nc.tensor.matmul_mx(
-                    out=bank[:], lhsT=d_codes[j // 2][:, cols].bitcast(E4M3X4), lhsT_scale=d_planes[j // 2][:, cols],
+                    out=out, lhsT=d_codes[j // 2][:, cols].bitcast(E4M3X4), lhsT_scale=d_planes[j // 2][:, cols],
                     rhs=rhs, rhs_scale=rhs_scale, start=(g == 0), stop=(g == PASSES - 1),
                 )
+
+        def e_columns(first, stop):
+            half, origin = first // BANK, first - first % BANK
+            return lambda g: (e_w[half][:, g, 2 * (first - origin) : 2 * (stop - origin)].bitcast(E2M1X4), e_s[:, g, first:stop])
 
         sig = {}
 
         def score(j):
             s, t = divmod(j, PACK)
             diff = psum.tile([P, RANKERS], F32, name="bank")
-            times_d(j, diff, lambda g: (codes["v"][:, g * RANKERS : (g + 1) * RANKERS].bitcast(E4M3X4), planes["v"][:, g * RANKERS : (g + 1) * RANKERS]))
+            times_d(j, diff[:], lambda g: (codes["v"][:, g * RANKERS : (g + 1) * RANKERS].bitcast(E4M3X4), planes["v"][:, g * RANKERS : (g + 1) * RANKERS]))
             if t == 0:
                 sig[s] = work.tile([P, PACK, RANKERS], F32, name="sig", bufs=3, align_bytes=64)
             nc.scalar.activation(out=sig[s][:, t, :], in_=diff[:], func=SIGMOID, scale=-1.0)
 
-        def encode(j, half):
+        def encode(j, first, stop):
             s, t = divmod(j, PACK)
-            cols = slice(BANK * half, BANK * (half + 1))
-            encoded = psum.tile([P, BANK], F32, name="bank")
-            times_d(j, encoded, lambda g: (e_w[half][:, g, :].bitcast(E2M1X4), e_s[half][:, g, :]))
-            nc.scalar.activation(out=h_raw[s][:, t, cols], in_=encoded[:], func=COPY, scale=ipw_f[:, s, t : t + 1])
+            encoded = psum.tile([P, stop - first], F32, name="bank")
+            times_d(j, encoded[:], e_columns(first, stop))
+            nc.scalar.activation(out=h_raw[s][:, t, first:stop], in_=encoded[:], func=COPY, scale=ipw_f[:, s, t : t + 1])
 
-        lam_codes = [keep.tile([P, RANKERS], U32, name=f"lam_codes{s}", align_bytes=64) for s in range(GROUPS)]
-        lam_planes = [keep.tile([P, RANKERS], U8, name=f"lam_planes{s}", align_bytes=64) for s in range(GROUPS)]
-        lam = {}
+        stacked = {}
 
-        def lam_multiply(s, first, stop):
-            if first == 0:
-                lam[s] = work.tile([P, RANKERS, PACK], BF16, name="lam", bufs=2, align_bytes=64)
-            nc.vector.tensor_tensor(
-                out=lam[s][:, first:stop, :].rearrange("p (c i) t -> p c t i", i=2),
-                in0=sig[s][:, :, first:stop].rearrange("p t (c i) -> p c t i", i=2),
-                in1=dlt[s][:, :, first:stop].rearrange("p t (c i) -> p c t i", i=2),
-                op=MULT,
-            )
+        def encode_stacked(s, first, stop):
+            for col in range(first, stop, P):
+                stacked[s, col] = psum.tile([P, PACK, P], F32, name="bank")
+                for t in range(PACK):
+                    times_d(PACK * s + t, stacked[s, col][:, t, :], e_columns(col, col + P))
 
-        def lam_quantize(s, first, stop):
-            quantize(lam_codes[s][:, first:stop], lam_planes[s][:, first:stop], lam[s][:, first:stop, :].rearrange("p n t -> p (n t)"))
+        def weigh(s, first, stop):
+            tile = new_grouped(("h", s), first, stop, "weighed", 3)
+            for col in range(first, stop, P):
+                nc.vector.tensor_tensor(
+                    out=tile[:, col - first : col - first + P, :],
+                    in0=stacked[s, col][:].rearrange("p t n -> p n t"),
+                    in1=ipw_f[:, s : s + 1, :].to_broadcast([P, P, PACK]),
+                    op=MULT,
+                )
 
         sums = {}
 
-        def update(s, m, first, stop, order, share=1):
-            lead = m - m % share
-            opens, closes = s == order[0] and m == lead, s == order[-1] and m == lead + share - 1
-            if opens:
-                sums[lead, first] = psum.tile([P, share, stop - first], F32, name="bank")
+        def update(m, first, stop, groups):
             rows = slice(m * P, (m + 1) * P)
-            nc.tensor.matmul_mx(
-                out=sums[lead, first][:, m - lead, :], lhsT=lam_codes[s][:, rows].bitcast(E4M3X4), lhsT_scale=lam_planes[s][:, rows],
-                rhs=codes[s][:, first:stop].bitcast(E4M3X4), rhs_scale=planes[s][:, first:stop],
-                start=opens, stop=closes,
-            )
+            for s in groups:
+                if s == 0:
+                    sums[m, first] = psum.tile([P, stop - first], F32, name="bank")
+                nc.tensor.matmul_mx(
+                    out=sums[m, first][:], lhsT=codes["lam", s][:, rows].bitcast(E4M3X4), lhsT_scale=planes["lam", s][:, rows],
+                    rhs=codes["h", s][:, first:stop].bitcast(E4M3X4), rhs_scale=planes["h", s][:, first:stop],
+                    start=(s == 0), stop=(s == GROUPS - 1),
+                )
 
-        def store(lead, first, stop, copy, share=1):
-            res = work.tile([P, share, stop - first], F32, name=f"res{first}", bufs=QTILES // share)
-            copy(out=res[:], in_=sums[lead, first][:])
-            nc.sync.dma_start(out=out[lead * P : (lead + share) * P, first:stop].rearrange("(m p) c -> p m c", p=P), in_=res[:])
+        def store(m, first, stop, copy):
+            res = work.tile([P, stop - first], F32, name="res", bufs=6)
+            copy(out=res[:], in_=sums[m, first][:])
+            nc.sync.dma_start(out=out[m * P : (m + 1) * P, first:stop], in_=res[:])
 
-        products = []
-        for s in range(2):
-            for j in (PACK * s, PACK * s + 2):
-                products.extend((encode, i, half) for half in range(HALVES) for i in (j, j + 1))
-            products.extend((score, j) for j in range(PACK * s, PACK * (s + 1)))
-        for j in range(2 * PACK, TILES + 2, 2):
-            if j < TILES:
-                products.extend([(encode, j, 0), (encode, j + 1, 0), (score, j), (score, j + 1)])
-            if j > 2 * PACK:
-                products.extend([(encode, j - 2, 1), (encode, j - 1, 1)])
+        def run(calls):
+            for call in calls:
+                call[0](*call[1:])
 
-        def multiply(count):
-            for item in products[:count]:
-                item[0](*item[1:])
-            return products[count:]
-
-        windows = [("v", 0, WINDOW), ("v", FEATS - WINDOW, FEATS)]
-        for s in range(2):
-            windows.extend([(s, 0, WINDOW), (s, WINDOW, 2 * WINDOW)])
-        windows.append((2, 0, WINDOW))
-        lam_halves = [(s, first, first + RANKERS // 2) for s in range(GROUPS - 1) for first in (0, RANKERS // 2)]
+        h = [("h", s) for s in range(GROUPS)]
+        lam = [("lam", s) for s in range(GROUPS)]
 
         first_tile = new_wide(0, 1)
         for first in range(0, RAW, QUARTER):
@@ -286,94 +280,121 @@ def tile_lambdarank_head_gradient_s11_kernel(tc, d_bytes, d_scale, v, delta, ipw
             copy(out=first_tile[:, :, first : first + QUARTER], in_=d_bytes_of(0, 1)[:, :, first : first + QUARTER])
         widen(1, 1)
         widen(2, 1)
+        warm_up(4)
         for g in range(PASSES):
             turn(0, g, g + 1)
         widen(3, 1)
-        for j in range(1, PACK):
+        turn(1)
+        warm_up(2)
+        for j in range(2, PACK):
             turn(j)
         nc.scalar.copy(out=ipw_f[:], in_=ipw_bf[:])
         widen(4, 2)
-        group_columns("v", WINDOW, RANKERS, on_scalar)
-        widen(6, 2)
         scale(0, 0, 1)
         for unit in range(1, UNITS):
             scale(unit // PASSES, unit % PASSES, unit % PASSES + 1)
             d_quantize(unit - 1, unit)
         d_quantize(UNITS - 1, UNITS)
-        group_in_window(*windows[0])
+
+        def low(*tiles):
+            return [(encode, j, 0, BANK) for j in tiles]
+
+        def high(*tiles):
+            return [(encode, j, BANK, FEATS) for j in tiles]
+
+        def scores(*tiles):
+            return [(score, j) for j in tiles]
+
+        def turns(p):
+            return [(turn, 2 * p), (turn, 2 * p + 1)]
+
+        def by_scalar(name, first, stop):
+            return [(interleave, name, first, stop, on_scalar)]
+
+        windows = {
+            2: [("v", FEATS - WINDOW, FEATS)],
+            3: [(h[0], 0, WINDOW)],
+            4: [(lam[0], 0, 256)],
+            5: [(lam[0], 256, 512)],
+            6: [(lam[1], 0, 256)],
+            7: [(lam[1], 256, 512)],
+        }
+        direct = {p: (1, BANK + P * (p - 4), BANK + P * (p - 3)) for p in range(4, STEPS)}
+        behind = {
+            1: by_scalar("v", RANKERS, FEATS - WINDOW) + low(2, 3) + turns(3) + [(widen, 8, 2)] + high(2, 3),
+            2: scores(0, 1, 2, 3) + turns(4) + [(widen, 10, 2)],
+            3: low(4, 5) + [(encode_stacked, *direct[4])] + turns(5) + [(widen, 12, 2)] + by_scalar(h[0], 384, 512),
+            4: [(encode_stacked, *direct[5])] + scores(4, 5, 6, 7) + turns(6) + [(widen, 14, 2)],
+            5: [(encode_stacked, *direct[6])] + low(6, 7) + by_scalar(h[0], 512, 768) + scores(8, 9) + turns(7) + by_scalar(h[0], 768, 1024),
+            6: [(encode_stacked, *direct[7])] + scores(10, 11) + by_scalar(h[1], 0, 256) + low(8, 9) + [(encode_stacked, 2, BANK, FEATS)] + by_scalar(h[1], 256, 512),
+            7: [],
+        }
+        also = {2: [("v", RANKERS, FEATS - WINDOW)], 5: [(h[0], 384, 512)], 7: []}
+        run(low(0, 1) + by_scalar("v", WINDOW, RANKERS) + high(0, 1) + turns(2) + [(widen, 6, 2)])
+        in_window([("v", 0, WINDOW)])
         scale(2)
         scale(3)
         d_quantize(4, 6)
-        quantize_columns("v", WINDOW, RANKERS)
-        quantize_window(*windows[0])
         d_quantize(6, 8)
-        products = multiply(EARLY_PRODUCTS)
-
+        quantize_columns("v", 0, WINDOW)
+        quantize_columns("v", WINDOW, RANKERS)
+        run(behind[1])
         for p in range(2, STEPS):
-            window = windows[p - 1]
-            turn(2 * p)
-            turn(2 * p + 1)
-            if p + 2 < STEPS:
-                widen(2 * p + 4, 2)
-            else:
-                group_columns(p + 2 - STEPS, 2 * WINDOW, FEATS, on_scalar)
-            group_in_window(*window)
+            in_window(windows[p])
             scale(2 * p)
             scale(2 * p + 1)
-            products = multiply(EARLY_PRODUCTS if p < 4 else LATE_PRODUCTS)
-            if p == 2:
-                group_columns("v", RANKERS, FEATS - WINDOW, on_vector)
-                quantize_columns("v", FEATS - WINDOW, FEATS - QUARTER)
-                quantize_columns("v", RANKERS, FEATS - WINDOW)
-                quantize_columns("v", FEATS - QUARTER, FEATS, FEATS - WINDOW)
-            else:
-                if p >= 4:
-                    lam_multiply(*lam_halves[p - 4])
-                quantize_window(*window)
-            d_quantize(UNITS * p, UNITS * (p + 1))
+            if p in direct:
+                weigh(*direct[p])
+            d_quantize(UNITS * p, UNITS * p + PASSES)
+            for job in also.get(p, []):
+                quantize_columns(*job)
+            if p in direct:
+                quantize_columns(h[1], *direct[p][1:])
+            quantize_columns(*windows[p][0])
+            d_quantize(UNITS * p + PASSES, UNITS * (p + 1))
+            run(behind[p])
 
         last = GROUPS - 1
-        in_order = tuple(range(GROUPS))
-        products = multiply(EARLY_PRODUCTS)
-        lam_quantize(0, 0, RANKERS)
-        group_columns(2, WINDOW, BANK, on_vector)
-        lam_multiply(*lam_halves[4])
-        quantize_columns(2, WINDOW, BANK)
-        lam_quantize(1, 0, RANKERS)
-        lam_multiply(*lam_halves[5])
-        products = multiply(len(products))
-        group_columns(last, 0, BANK, on_vector)
-        lam_quantize(2, 0, RANKERS)
-        lam_multiply(last, 0, P)
-        quantize_columns(last, 0, BANK)
-        lam_quantize(last, 0, P)
+        in_window([(lam[2], 0, 256)])
+        weigh(2, BANK, FEATS)
+        run(scores(12, 13, 14, 15) + low(10, 11) + by_scalar(h[2], 0, BANK))
+        for job in ((h[0], 512, 768), (h[0], 768, 1024), (h[1], 0, 256), (lam[2], 0, 256), (h[2], BANK, FEATS), (h[1], 256, 512)):
+            quantize_columns(*job)
+        in_window([(lam[2], 256, 512), (lam[3], 0, 128)])
+        for first in (BANK, 0):
+            encode_stacked(last, first, first + BANK)
+            weigh(last, first, first + BANK)
+        for job in ((h[last], BANK, FEATS), (lam[last], 0, P)):
+            quantize_columns(*job)
+        lam_on_vector(last, P, 2 * P)
+        quantize_columns(h[last], 0, BANK)
+        quantize_columns(lam[last], P, 2 * P)
+        quantize_columns(h[2], 0, BANK)
+        lam_on_vector(last, 2 * P, 3 * P)
+        quantize_columns(lam[2], 256, 512)
+        lam_on_vector(last, 3 * P, 4 * P)
+        quantize_columns(lam[last], 2 * P, 3 * P)
+        quantize_columns(lam[last], 3 * P, 4 * P)
 
-        third, fourth = BANK, BANK + QUARTER
-        for s in (2, last):
-            group_columns(s, third, fourth, on_scalar)
-        for s in range(last):
-            for m in range(QTILES):
-                update(s, m, 0, BANK, in_order)
+        def close(m, first):
+            update(m, first, first + BANK, (2, 3))
+            store(m, first, first + BANK, on_scalar)
+
+        def whole(m, first):
+            update(m, first, first + BANK, (0, 1))
+            close(m, first)
+
         for m in range(QTILES):
-            if m + 1 < QTILES:
-                lam_multiply(last, P * (m + 1), P * (m + 2))
-                if m == 0:
-                    quantize_columns(0, fourth, FEATS)
-                else:
-                    quantize_columns(m + 1, third, fourth)
-                lam_quantize(last, P * (m + 1), P * (m + 2))
-            update(last, m, 0, BANK, in_order)
-            store(m, 0, BANK, on_scalar)
-            for n in range(QTILES):
-                update(m, n, third, fourth, in_order, 2)
-        for s in (2, last):
-            group_columns(s, fourth, FEATS, on_vector)
-            quantize_columns(s - 1, fourth, FEATS)
-        quantize_columns(last, fourth, FEATS)
-        store(0, third, fourth, on_scalar, 2)
-        store(2, third, fourth, on_vector, 2)
-        for s in range(GROUPS):
-            for m in range(QTILES):
-                update(s, m, fourth, FEATS, in_order)
-        for m in range(QTILES):
-            store(m, fourth, FEATS, on_scalar if m % 2 else on_vector)
+            update(m, BANK, FEATS, (0, 1))
+        update(0, 0, BANK, (0, 1))
+        close(0, BANK)
+        update(1, 0, BANK, (0, 1))
+        close(1, BANK)
+        close(0, 0)
+        close(1, 0)
+        close(2, BANK)
+        close(3, BANK)
+        whole(2, 0)
+        for first, copy in ((0, on_scalar), (QUARTER, on_vector)):
+            update(QTILES - 1, first, first + QUARTER, range(GROUPS))
+            store(QTILES - 1, first, first + QUARTER, copy)

@@ -125,11 +125,11 @@ def tile_lambdarank_head_gradient_s11_kernel(tc, d_bytes, d_scale, v, delta, ipw
             tile = new_grouped(name, first, stop, "grouped", 6)
             copy(out=tile[:].rearrange("p (c i) t -> p c t i", i=8), in_=rows_of(name, first, stop).rearrange("p t (c i) -> p c t i", i=8))
 
-        def lam_product(engine, tile, s, first, stop):
+        def lam_product(engine, tile, s, first, stop, run):
             engine.tensor_tensor(
-                out=tile[:].rearrange("p (c i) t -> p c t i", i=2),
-                in0=sig[s][:, :, first:stop].rearrange("p t (c i) -> p c t i", i=2),
-                in1=dlt[s][:, :, first:stop].rearrange("p t (c i) -> p c t i", i=2),
+                out=tile[:].rearrange("p (c i) t -> p c t i", i=run),
+                in0=sig[s][:, :, first:stop].rearrange("p t (c i) -> p c t i", i=run),
+                in1=dlt[s][:, :, first:stop].rearrange("p t (c i) -> p c t i", i=run),
                 op=MULT,
             )
 
@@ -137,12 +137,12 @@ def tile_lambdarank_head_gradient_s11_kernel(tc, d_bytes, d_scale, v, delta, ipw
             for i, (name, first, stop) in enumerate(jobs):
                 tile = new_grouped(name, first, stop, f"window{i}", 1)
                 if name[0] == "lam":
-                    lam_product(nc.gpsimd, tile, name[1], first, stop)
+                    lam_product(nc.gpsimd, tile, name[1], first, stop, 8)
                 else:
                     nc.gpsimd.tensor_scalar(out=tile[:], in0=rows_of(name, first, stop).rearrange("p t n -> p n t"), scalar1=1.0, scalar2=0.0, op0=MULT, op1=ADD)
 
         def lam_on_vector(s, first, stop):
-            lam_product(nc.vector, new_grouped(("lam", s), first, stop, "lam", 2), s, first, stop)
+            lam_product(nc.vector, new_grouped(("lam", s), first, stop, "lam", 2), s, first, stop, 2)
 
         def quantize(out, scales, in_):
             nc.vector.quantize_mx(out=out.bitcast(E4M3X4), scales=scales, in_=in_)
@@ -243,9 +243,9 @@ def tile_lambdarank_head_gradient_s11_kernel(tc, d_bytes, d_scale, v, delta, ipw
             tile = new_grouped(("h", s), first, stop, "weighed", 3)
             for col in range(first, stop, P):
                 nc.vector.tensor_tensor(
-                    out=tile[:, col - first : col - first + P, :],
-                    in0=stacked[s, col][:].rearrange("p t n -> p n t"),
-                    in1=ipw_f[:, s : s + 1, :].to_broadcast([P, P, PACK]),
+                    out=tile[:, col - first : col - first + P, :].rearrange("p (c i) t -> p c t i", i=2),
+                    in0=stacked[s, col][:].rearrange("p t (c i) -> p c t i", i=2),
+                    in1=ipw_f[:, s, :].rearrange("p (c t i) -> p c t i", c=1, i=1).to_broadcast([P, P // 2, PACK, 2]),
                     op=MULT,
                 )
 

@@ -68,8 +68,9 @@ def tile_lambdarank_head_gradient_s11_kernel(tc, d_bytes, d_scale, v, delta, ipw
         nc.vector.memset(warm[:].bitcast(I32), 0)
         nc.vector.memset(table_in[:], 0.0)
 
+        idle = psum.tile([P, BANK], F32, name="bank")
+
         def warm_up(count):
-            idle = psum.tile([P, BANK], F32, name="bank")
             for i in range(count):
                 nc.tensor.matmul(out=idle[:], lhsT=warm[:, :P], rhs=warm[:], start=True, stop=True)
 
@@ -83,14 +84,14 @@ def tile_lambdarank_head_gradient_s11_kernel(tc, d_bytes, d_scale, v, delta, ipw
 
         load_raw(0, 0, 1)
         nc.scalar.dma_start(out=scale_kp[:], in_=d_scale.rearrange("o (g p t) -> p (o g) t", p=P, t=PACK))
+        nc.scalar.dma_start(out=ipw_bf[:], in_=ipw.rearrange("(s m t) -> m s t", m=P, t=PACK))
         nc.scalar.activation(out=table_out[:], in_=table_in[:], func=SIGMOID, scale=-1.0)
         load_raw(0, 1, 2)
         load_raw(0, 2, 4)
+        load_raw(1, 0, 2)
         for r in range(PACK):
             nc.sync.dma_start(out=e_s[r:P:32].bitcast(I32), in_=s_view[r:16:PACK].bitcast(I32))
         load_words(0)
-        nc.sync.dma_start(out=ipw_bf[:], in_=ipw.rearrange("(s m t) -> m s t", m=P, t=PACK))
-        load_raw(1, 0, 2)
         nc.sync.dma_start(out=v_raw[0][:], in_=v_view[0])
         load_words(1)
         load_raw(1, 2, 4)
@@ -107,7 +108,7 @@ def tile_lambdarank_head_gradient_s11_kernel(tc, d_bytes, d_scale, v, delta, ipw
         width = {name: RANKERS if name[0] == "lam" else FEATS for name in names}
         codes = {name: keep.tile([P, width[name]], U32, name=f"codes{i}", align_bytes=64) for i, name in enumerate(names)}
         planes = {name: keep.tile([P, width[name]], U8, name=f"planes{i}", align_bytes=64) for i, name in enumerate(names)}
-        h_raw = [keep.tile([P, PACK, (FEATS, BANK, BANK)[s]], BF16, name=f"h_raw{s}", align_bytes=64) for s in range(GROUPS - 1)]
+        h_raw = [keep.tile([P, PACK, FEATS if s == 0 else BANK], BF16, name=f"h_raw{s}", align_bytes=64) for s in range(GROUPS)]
         grouped = {}
 
         def new_grouped(name, first, stop, tag, bufs):
@@ -142,13 +143,18 @@ def tile_lambdarank_head_gradient_s11_kernel(tc, d_bytes, d_scale, v, delta, ipw
                     nc.gpsimd.tensor_scalar(out=tile[:], in0=rows_of(name, first, stop).rearrange("p t n -> p n t"), scalar1=1.0, scalar2=0.0, op0=MULT, op1=ADD)
 
         def lam_on_vector(s, first, stop):
-            lam_product(nc.vector, new_grouped(("lam", s), first, stop, "lam", 2), s, first, stop, 2)
+            lam_product(nc.vector, new_grouped(("lam", s), first, stop, "lam", 3), s, first, stop, 2)
 
         def quantize(out, scales, in_):
             nc.vector.quantize_mx(out=out.bitcast(E4M3X4), scales=scales, in_=in_)
 
         def quantize_columns(name, first, stop):
-            quantize(codes[name][:, first:stop], planes[name][:, first:stop], grouped[name, first][:].rearrange("p n t -> p (n t)"))
+            start = first
+            for part in (4 * P, 3 * P, 2 * P, P, P // 2):
+                if stop - start >= part:
+                    cols = slice(start, start + part)
+                    quantize(codes[name][:, cols], planes[name][:, cols], grouped[name, first][:, start - first : start - first + part, :].rearrange("p n t -> p (n t)"))
+                    start += part
 
         d_codes = [keep.tile([P, 2 * WORDS], U32, name=f"d_codes{p}", align_bytes=64) for p in range(STEPS)]
         d_planes = [keep.tile([P, 2 * WORDS], U8, name=f"d_planes{p}", align_bytes=64) for p in range(STEPS)]
@@ -263,7 +269,7 @@ def tile_lambdarank_head_gradient_s11_kernel(tc, d_bytes, d_scale, v, delta, ipw
                 )
 
         def store(m, first, stop, copy):
-            res = work.tile([P, stop - first], F32, name="res", bufs=6)
+            res = work.tile([P, stop - first], F32, name="res", bufs=9)
             copy(out=res[:], in_=sums[m, first][:])
             nc.sync.dma_start(out=out[m * P : (m + 1) * P, first:stop], in_=res[:])
 
@@ -283,13 +289,15 @@ def tile_lambdarank_head_gradient_s11_kernel(tc, d_bytes, d_scale, v, delta, ipw
         warm_up(4)
         for g in range(PASSES):
             turn(0, g, g + 1)
+        warm_up(1)
         widen(3, 1)
         turn(1)
-        warm_up(2)
+        warm_up(1)
         for j in range(2, PACK):
             turn(j)
-        nc.scalar.copy(out=ipw_f[:], in_=ipw_bf[:])
+        warm_up(1)
         widen(4, 2)
+        nc.scalar.copy(out=ipw_f[:], in_=ipw_bf[:])
         scale(0, 0, 1)
         for unit in range(1, UNITS):
             scale(unit // PASSES, unit % PASSES, unit % PASSES + 1)
@@ -323,21 +331,21 @@ def tile_lambdarank_head_gradient_s11_kernel(tc, d_bytes, d_scale, v, delta, ipw
         behind = {
             1: by_scalar("v", RANKERS, FEATS - WINDOW) + low(2, 3) + turns(3) + [(widen, 8, 2)] + high(2, 3),
             2: scores(0, 1, 2, 3) + turns(4) + [(widen, 10, 2)],
-            3: low(4, 5) + [(encode_stacked, *direct[4])] + turns(5) + [(widen, 12, 2)] + by_scalar(h[0], 384, 512),
-            4: [(encode_stacked, *direct[5])] + scores(4, 5, 6, 7) + turns(6) + [(widen, 14, 2)],
-            5: [(encode_stacked, *direct[6])] + low(6, 7) + by_scalar(h[0], 512, 768) + scores(8, 9) + turns(7) + by_scalar(h[0], 768, 1024),
-            6: [(encode_stacked, *direct[7])] + scores(10, 11) + by_scalar(h[1], 0, 256) + low(8, 9) + [(encode_stacked, 2, BANK, FEATS)] + by_scalar(h[1], 256, 512),
+            3: low(4, 5) + [(encode_stacked, *direct[4])] + scores(4) + turns(5) + [(widen, 12, 2)] + by_scalar(h[0], 384, 512),
+            4: scores(5, 6, 7) + [(encode_stacked, *direct[5])] + low(6) + turns(6) + [(widen, 14, 2)],
+            5: low(7) + by_scalar(h[0], 512, 768) + scores(8, 9) + [(encode_stacked, *direct[6])] + scores(10) + turns(7) + by_scalar(h[0], 768, 1024),
+            6: scores(11) + low(8, 9) + [(encode_stacked, *direct[7])] + low(10, 11) + by_scalar(h[1], 0, 256) + [(encode_stacked, 2, BANK, FEATS)] + by_scalar(h[1], 256, 512),
             7: [],
         }
         also = {2: [("v", RANKERS, FEATS - WINDOW)], 5: [(h[0], 384, 512)], 7: []}
-        run(low(0, 1) + by_scalar("v", WINDOW, RANKERS) + high(0, 1) + turns(2) + [(widen, 6, 2)])
-        in_window([("v", 0, WINDOW)])
+        run(low(0, 1) + turns(2) + by_scalar("v", 320, RANKERS) + [(widen, 6, 2)] + high(0, 1))
+        in_window([("v", 0, 320)])
         scale(2)
         scale(3)
         d_quantize(4, 6)
         d_quantize(6, 8)
-        quantize_columns("v", 0, WINDOW)
-        quantize_columns("v", WINDOW, RANKERS)
+        quantize_columns("v", 0, 320)
+        quantize_columns("v", 320, RANKERS)
         run(behind[1])
         for p in range(2, STEPS):
             in_window(windows[p])
@@ -345,56 +353,52 @@ def tile_lambdarank_head_gradient_s11_kernel(tc, d_bytes, d_scale, v, delta, ipw
             scale(2 * p + 1)
             if p in direct:
                 weigh(*direct[p])
-            d_quantize(UNITS * p, UNITS * p + PASSES)
+            if p > 2:
+                d_quantize(UNITS * p, UNITS * p + PASSES)
             for job in also.get(p, []):
                 quantize_columns(*job)
             if p in direct:
                 quantize_columns(h[1], *direct[p][1:])
             quantize_columns(*windows[p][0])
+            if p == 2:
+                d_quantize(UNITS * p, UNITS * p + PASSES)
             d_quantize(UNITS * p + PASSES, UNITS * (p + 1))
             run(behind[p])
 
         last = GROUPS - 1
         in_window([(lam[2], 0, 256)])
         weigh(2, BANK, FEATS)
-        run(scores(12, 13, 14, 15) + low(10, 11) + by_scalar(h[2], 0, BANK))
+        run(scores(12, 13, 14, 15) + by_scalar(h[2], 0, BANK))
+        encode_stacked(last, BANK, FEATS)
+        run(low(12, 13, 14, 15) + by_scalar(h[last], 0, BANK))
         for job in ((h[0], 512, 768), (h[0], 768, 1024), (h[1], 0, 256), (lam[2], 0, 256), (h[2], BANK, FEATS), (h[1], 256, 512)):
             quantize_columns(*job)
-        in_window([(lam[2], 256, 512), (lam[3], 0, 128)])
-        for first in (BANK, 0):
-            encode_stacked(last, first, first + BANK)
-            weigh(last, first, first + BANK)
-        for job in ((h[last], BANK, FEATS), (lam[last], 0, P)):
-            quantize_columns(*job)
-        lam_on_vector(last, P, 2 * P)
-        quantize_columns(h[last], 0, BANK)
-        quantize_columns(lam[last], P, 2 * P)
-        quantize_columns(h[2], 0, BANK)
-        lam_on_vector(last, 2 * P, 3 * P)
+        in_window([(lam[2], 256, 512)])
+        weigh(last, BANK, FEATS)
+        lam_on_vector(last, 0, P)
         quantize_columns(lam[2], 256, 512)
-        lam_on_vector(last, 3 * P, 4 * P)
-        quantize_columns(lam[last], 2 * P, 3 * P)
-        quantize_columns(lam[last], 3 * P, 4 * P)
+        quantize_columns(h[last], BANK, FEATS)
+        for m in range(QTILES):
+            if m + 1 < QTILES:
+                lam_on_vector(last, (m + 1) * P, (m + 2) * P)
+            else:
+                quantize_columns(h[2], 0, BANK)
+            quantize_columns(lam[last], m * P, (m + 1) * P)
+        quantize_columns(h[last], 0, BANK)
 
-        def close(m, first):
-            update(m, first, first + BANK, (2, 3))
-            store(m, first, first + BANK, on_scalar)
-
-        def whole(m, first):
-            update(m, first, first + BANK, (0, 1))
-            close(m, first)
+        def finish(m, first, stop, groups, copy=on_scalar):
+            update(m, first, stop, groups)
+            store(m, first, stop, copy)
 
         for m in range(QTILES):
-            update(m, BANK, FEATS, (0, 1))
-        update(0, 0, BANK, (0, 1))
-        close(0, BANK)
-        update(1, 0, BANK, (0, 1))
-        close(1, BANK)
-        close(0, 0)
-        close(1, 0)
-        close(2, BANK)
-        close(3, BANK)
-        whole(2, 0)
-        for first, copy in ((0, on_scalar), (QUARTER, on_vector)):
-            update(QTILES - 1, first, first + QUARTER, range(GROUPS))
-            store(QTILES - 1, first, first + QUARTER, copy)
+            update(m, BANK, FEATS, range(last))
+        for m in (0, 1):
+            finish(m, BANK, FEATS, (last,))
+        for m in (0, 1):
+            update(m, 0, BANK, (0, 1))
+            finish(m + 2, BANK, FEATS, (last,))
+        for m in (0, 1):
+            finish(m, 0, BANK, (2, last), on_vector if m == 0 else on_scalar)
+        pieces = [(2, 0, QUARTER), (2, QUARTER, BANK), (3, 0, QUARTER), (3, QUARTER, QUARTER + P), (3, QUARTER + P, BANK)]
+        for i, piece in enumerate(pieces):
+            finish(*piece, range(GROUPS), on_scalar if i % 2 else on_vector)

@@ -337,15 +337,14 @@ def tile_lambdarank_head_gradient_s11_kernel(tc, d_bytes, d_scale, v, delta, ipw
             6: scores(11) + low(8, 9) + [(encode_stacked, *direct[7])] + low(10, 11) + by_scalar(h[1], 0, 256) + [(encode_stacked, 2, BANK, FEATS)] + by_scalar(h[1], 256, 512),
             7: [],
         }
-        also = {2: [("v", RANKERS, FEATS - WINDOW)], 5: [(h[0], 384, 512)], 7: []}
+        also = {2: [("v", 320, RANKERS), ("v", RANKERS, FEATS - WINDOW)], 5: [(h[0], 384, 512)], 7: []}
         run(low(0, 1) + turns(2) + by_scalar("v", 320, RANKERS) + [(widen, 6, 2)] + high(0, 1))
         in_window([("v", 0, 320)])
         scale(2)
         scale(3)
         d_quantize(4, 6)
-        d_quantize(6, 8)
         quantize_columns("v", 0, 320)
-        quantize_columns("v", 320, RANKERS)
+        d_quantize(6, 8)
         run(behind[1])
         for p in range(2, STEPS):
             in_window(windows[p])
@@ -370,7 +369,7 @@ def tile_lambdarank_head_gradient_s11_kernel(tc, d_bytes, d_scale, v, delta, ipw
         weigh(2, BANK, FEATS)
         run(scores(12, 13, 14, 15) + by_scalar(h[2], 0, BANK))
         encode_stacked(last, BANK, FEATS)
-        run(low(12, 13, 14, 15) + by_scalar(h[last], 0, BANK))
+        run(low(12, 13, 14, 15) + by_scalar(h[last], 0, WINDOW))
         for job in ((h[0], 512, 768), (h[0], 768, 1024), (h[1], 0, 256), (lam[2], 0, 256), (h[2], BANK, FEATS), (h[1], 256, 512)):
             quantize_columns(*job)
         in_window([(lam[2], 256, 512)])
@@ -384,7 +383,9 @@ def tile_lambdarank_head_gradient_s11_kernel(tc, d_bytes, d_scale, v, delta, ipw
             else:
                 quantize_columns(h[2], 0, BANK)
             quantize_columns(lam[last], m * P, (m + 1) * P)
-        quantize_columns(h[last], 0, BANK)
+        interleave(h[last], WINDOW, BANK, on_vector)
+        quantize_columns(h[last], 0, WINDOW)
+        quantize_columns(h[last], WINDOW, BANK)
 
         def finish(m, first, stop, groups, copy=on_scalar):
             update(m, first, stop, groups)

@@ -112,9 +112,11 @@ def tile_lambdarank_head_gradient_s11_kernel(tc, d_bytes, d_scale, v, delta, ipw
         grouped = {}
 
         def new_grouped(name, first, stop, tag, bufs):
-            tile = work.tile([P, stop - first, PACK], BF16, name=tag, bufs=bufs, align_bytes=64)
-            grouped[name, first] = tile
-            return tile
+            grouped[name, first] = work.tile([P, stop - first, PACK], BF16, name=tag, bufs=bufs, align_bytes=64)
+
+        def grouped_columns(name, first, stop):
+            origin = max(start for (other, start) in grouped if other == name and start <= first)
+            return grouped[name, origin][:, first - origin : stop - origin, :]
 
         def rows_of(name, first, stop):
             if name == "v":
@@ -123,38 +125,28 @@ def tile_lambdarank_head_gradient_s11_kernel(tc, d_bytes, d_scale, v, delta, ipw
             return h_raw[name[1]][:, :, first:stop]
 
         def interleave(name, first, stop, copy):
-            tile = new_grouped(name, first, stop, "grouped", 6)
-            copy(out=tile[:].rearrange("p (c i) t -> p c t i", i=8), in_=rows_of(name, first, stop).rearrange("p t (c i) -> p c t i", i=8))
+            copy(out=grouped_columns(name, first, stop).rearrange("p (c i) t -> p c t i", i=8), in_=rows_of(name, first, stop).rearrange("p t (c i) -> p c t i", i=8))
 
-        def lam_product(engine, tile, s, first, stop, run):
+        def lam_product(engine, s, first, stop, run):
             engine.tensor_tensor(
-                out=tile[:].rearrange("p (c i) t -> p c t i", i=run),
+                out=grouped_columns(("lam", s), first, stop).rearrange("p (c i) t -> p c t i", i=run),
                 in0=sig[s][:, :, first:stop].rearrange("p t (c i) -> p c t i", i=run),
                 in1=dlt[s][:, :, first:stop].rearrange("p t (c i) -> p c t i", i=run),
                 op=MULT,
             )
 
-        def in_window(jobs):
-            for i, (name, first, stop) in enumerate(jobs):
-                tile = new_grouped(name, first, stop, f"window{i}", 1)
-                if name[0] == "lam":
-                    lam_product(nc.gpsimd, tile, name[1], first, stop, 8)
-                else:
-                    nc.gpsimd.tensor_scalar(out=tile[:], in0=rows_of(name, first, stop).rearrange("p t n -> p n t"), scalar1=1.0, scalar2=0.0, op0=MULT, op1=ADD)
-
-        def lam_on_vector(s, first, stop):
-            lam_product(nc.vector, new_grouped(("lam", s), first, stop, "lam", 3), s, first, stop, 2)
+        def in_window(name, first, stop):
+            new_grouped(name, first, stop, "window0", 1)
+            if name[0] == "lam":
+                lam_product(nc.gpsimd, name[1], first, stop, 8)
+            else:
+                nc.gpsimd.tensor_scalar(out=grouped_columns(name, first, stop), in0=rows_of(name, first, stop).rearrange("p t n -> p n t"), scalar1=1.0, scalar2=0.0, op0=MULT, op1=ADD)
 
         def quantize(out, scales, in_):
             nc.vector.quantize_mx(out=out.bitcast(E4M3X4), scales=scales, in_=in_)
 
         def quantize_columns(name, first, stop):
-            start = first
-            for part in (4 * P, 3 * P, 2 * P, P, P // 2):
-                if stop - start >= part:
-                    cols = slice(start, start + part)
-                    quantize(codes[name][:, cols], planes[name][:, cols], grouped[name, first][:, start - first : start - first + part, :].rearrange("p n t -> p (n t)"))
-                    start += part
+            quantize(codes[name][:, first:stop], planes[name][:, first:stop], grouped_columns(name, first, stop).rearrange("p n t -> p (n t)"))
 
         d_codes = [keep.tile([P, 2 * WORDS], U32, name=f"d_codes{p}", align_bytes=64) for p in range(STEPS)]
         d_planes = [keep.tile([P, 2 * WORDS], U8, name=f"d_planes{p}", align_bytes=64) for p in range(STEPS)]
@@ -231,11 +223,20 @@ def tile_lambdarank_head_gradient_s11_kernel(tc, d_bytes, d_scale, v, delta, ipw
                 sig[s] = work.tile([P, PACK, RANKERS], F32, name="sig", bufs=3, align_bytes=64)
             nc.scalar.activation(out=sig[s][:, t, :], in_=diff[:], func=SIGMOID, scale=-1.0)
 
+        encoded = {}
+
+        def encode_product(j, first, stop):
+            encoded[j, first] = psum.tile([P, stop - first], F32, name="bank")
+            times_d(j, encoded[j, first][:], e_columns(first, stop))
+
         def encode(j, first, stop):
             s, t = divmod(j, PACK)
-            encoded = psum.tile([P, stop - first], F32, name="bank")
-            times_d(j, encoded[:], e_columns(first, stop))
-            nc.scalar.activation(out=h_raw[s][:, t, first:stop], in_=encoded[:], func=COPY, scale=ipw_f[:, s, t : t + 1])
+            encode_product(j, first, stop)
+            nc.scalar.activation(out=h_raw[s][:, t, first:stop], in_=encoded[j, first][:], func=COPY, scale=ipw_f[:, s, t : t + 1])
+
+        def weigh_rows(j, first, stop):
+            s, t = divmod(j, PACK)
+            nc.vector.tensor_scalar(out=h_raw[s][:, t, first:stop], in0=encoded[j, first][:], scalar1=ipw_f[:, s, t : t + 1], scalar2=None, op0=MULT)
 
         stacked = {}
 
@@ -246,10 +247,9 @@ def tile_lambdarank_head_gradient_s11_kernel(tc, d_bytes, d_scale, v, delta, ipw
                     times_d(PACK * s + t, stacked[s, col][:, t, :], e_columns(col, col + P))
 
         def weigh(s, first, stop):
-            tile = new_grouped(("h", s), first, stop, "weighed", 3)
             for col in range(first, stop, P):
                 nc.vector.tensor_tensor(
-                    out=tile[:, col - first : col - first + P, :].rearrange("p (c i) t -> p c t i", i=2),
+                    out=grouped_columns(("h", s), col, col + P).rearrange("p (c i) t -> p c t i", i=2),
                     in0=stacked[s, col][:].rearrange("p t (c i) -> p c t i", i=2),
                     in1=ipw_f[:, s, :].rearrange("p (c t i) -> p c t i", c=1, i=1).to_broadcast([P, P // 2, PACK, 2]),
                     op=MULT,
@@ -319,73 +319,80 @@ def tile_lambdarank_head_gradient_s11_kernel(tc, d_bytes, d_scale, v, delta, ipw
         def by_scalar(name, first, stop):
             return [(interleave, name, first, stop, on_scalar)]
 
+        def room(name, first, stop):
+            return [(new_grouped, name, first, stop, "grouped", 8)]
+
         windows = {
-            2: [("v", FEATS - WINDOW, FEATS)],
-            3: [(h[0], 0, WINDOW)],
-            4: [(lam[0], 0, 256)],
-            5: [(lam[0], 256, 512)],
-            6: [(lam[1], 0, 256)],
-            7: [(lam[1], 256, 512)],
+            2: ("v", FEATS - WINDOW, FEATS),
+            3: (h[0], 0, WINDOW),
+            4: (lam[0], 0, 256),
+            5: (lam[0], 256, 512),
+            6: (lam[1], 0, 256),
+            7: (lam[1], 256, 512),
         }
         direct = {p: (1, BANK + P * (p - 4), BANK + P * (p - 3)) for p in range(4, STEPS)}
         behind = {
             1: by_scalar("v", RANKERS, FEATS - WINDOW) + low(2, 3) + turns(3) + [(widen, 8, 2)] + high(2, 3),
             2: scores(0, 1, 2, 3) + turns(4) + [(widen, 10, 2)],
-            3: low(4, 5) + [(encode_stacked, *direct[4])] + scores(4) + turns(5) + [(widen, 12, 2)] + by_scalar(h[0], 384, 512),
+            3: low(4, 5) + [(encode_stacked, *direct[4])] + scores(4) + turns(5) + [(widen, 12, 2)] + room(h[0], WINDOW, BANK) + by_scalar(h[0], WINDOW, BANK) + room(h[1], BANK, FEATS),
             4: scores(5, 6, 7) + [(encode_stacked, *direct[5])] + low(6) + turns(6) + [(widen, 14, 2)],
-            5: low(7) + by_scalar(h[0], 512, 768) + scores(8, 9) + [(encode_stacked, *direct[6])] + scores(10) + turns(7) + by_scalar(h[0], 768, 1024),
-            6: scores(11) + low(8, 9) + [(encode_stacked, *direct[7])] + low(10, 11) + by_scalar(h[1], 0, 256) + [(encode_stacked, 2, BANK, FEATS)] + by_scalar(h[1], 256, 512),
+            5: low(7) + room(h[0], BANK, FEATS) + by_scalar(h[0], 512, 768) + scores(8, 9) + [(encode_stacked, *direct[6])] + scores(10) + turns(7) + by_scalar(h[0], 768, 1024),
+            6: scores(11) + low(8, 9) + [(encode_stacked, *direct[7])] + low(10, 11) + room(h[1], 0, BANK) + by_scalar(h[1], 0, 256) + [(encode_stacked, 2, BANK, FEATS)] + by_scalar(h[1], 256, 512),
             7: [],
         }
-        also = {2: [("v", 320, RANKERS), ("v", RANKERS, FEATS - WINDOW)], 5: [(h[0], 384, 512)], 7: []}
-        run(low(0, 1) + turns(2) + by_scalar("v", 320, RANKERS) + [(widen, 6, 2)] + high(0, 1))
-        in_window([("v", 0, 320)])
+        after = {5: (h[0], WINDOW, BANK), 7: (h[1], BANK, FEATS)}
+        run(low(0) + [(encode_product, 1, 0, BANK)] + turns(2) + room("v", QUARTER, FEATS - WINDOW) + by_scalar("v", QUARTER, RANKERS) + [(widen, 6, 2)] + high(0, 1))
+        in_window("v", 0, QUARTER)
         scale(2)
         scale(3)
+        weigh_rows(1, 0, BANK)
         d_quantize(4, 6)
-        quantize_columns("v", 0, 320)
+        quantize_columns("v", 0, QUARTER)
         d_quantize(6, 8)
         run(behind[1])
         for p in range(2, STEPS):
-            in_window(windows[p])
+            in_window(*windows[p])
             scale(2 * p)
             scale(2 * p + 1)
-            if p in direct:
-                weigh(*direct[p])
-            if p > 2:
-                d_quantize(UNITS * p, UNITS * p + PASSES)
-            for job in also.get(p, []):
-                quantize_columns(*job)
-            if p in direct:
-                quantize_columns(h[1], *direct[p][1:])
-            quantize_columns(*windows[p][0])
             if p == 2:
+                quantize_columns("v", QUARTER, FEATS - WINDOW)
+                quantize_columns(*windows[p])
+                d_quantize(UNITS * p, UNITS * (p + 1))
+            elif p == 3:
                 d_quantize(UNITS * p, UNITS * p + PASSES)
-            d_quantize(UNITS * p + PASSES, UNITS * (p + 1))
+                quantize_columns(*windows[p])
+                d_quantize(UNITS * p + PASSES, UNITS * (p + 1))
+            else:
+                weigh(*direct[p])
+                d_quantize(UNITS * p, UNITS * (p + 1))
+                quantize_columns(*windows[p])
+            if p in after:
+                quantize_columns(*after[p])
             run(behind[p])
 
         last = GROUPS - 1
-        in_window([(lam[2], 0, 256)])
+        in_window(lam[2], 0, 256)
+        run(room(h[2], BANK, FEATS))
         weigh(2, BANK, FEATS)
-        run(scores(12, 13, 14, 15) + by_scalar(h[2], 0, BANK))
+        run(scores(12, 13, 14, 15) + room(h[2], 0, BANK) + by_scalar(h[2], 0, BANK))
         encode_stacked(last, BANK, FEATS)
-        run(low(12, 13, 14, 15) + by_scalar(h[last], 0, WINDOW))
-        for job in ((h[0], 512, 768), (h[0], 768, 1024), (h[1], 0, 256), (lam[2], 0, 256), (h[2], BANK, FEATS), (h[1], 256, 512)):
+        run(low(12, 13, 14, 15) + room(h[last], 0, BANK) + by_scalar(h[last], 0, WINDOW))
+        for job in ((h[0], BANK, FEATS), (h[1], 0, BANK), (lam[2], 0, 256), (h[2], BANK, FEATS)):
             quantize_columns(*job)
-        in_window([(lam[2], 256, 512)])
+        in_window(lam[2], 256, 512)
+        run(room(h[last], BANK, FEATS) + room(lam[last], 0, RANKERS))
         weigh(last, BANK, FEATS)
-        lam_on_vector(last, 0, P)
+        lam_product(nc.vector, last, 0, P, 2)
         quantize_columns(lam[2], 256, 512)
         quantize_columns(h[last], BANK, FEATS)
         for m in range(QTILES):
             if m + 1 < QTILES:
-                lam_on_vector(last, (m + 1) * P, (m + 2) * P)
+                lam_product(nc.vector, last, (m + 1) * P, (m + 2) * P, 2)
             else:
-                quantize_columns(h[2], 0, BANK)
+                interleave(h[last], WINDOW, BANK, on_vector)
             quantize_columns(lam[last], m * P, (m + 1) * P)
-        interleave(h[last], WINDOW, BANK, on_vector)
-        quantize_columns(h[last], 0, WINDOW)
-        quantize_columns(h[last], WINDOW, BANK)
+        quantize_columns(h[2], 0, BANK)
+        quantize_columns(h[last], 0, BANK)
 
         def finish(m, first, stop, groups, copy=on_scalar):
             update(m, first, stop, groups)

@@ -40,7 +40,17 @@ def tile_lambdarank_head_gradient_s11_kernel(tc, d_bytes, d_scale, v, delta, ipw
     with ExitStack() as ctx:
         keep = ctx.enter_context(tc.tile_pool(name="keep", bufs=1))
         work = ctx.enter_context(tc.tile_pool(name="work", bufs=1))
-        psum = ctx.enter_context(tc.psum_pool(name="psum", bufs=BANKS))
+        psum = ctx.enter_context(tc.psum_pool(name="psum", bufs=1))
+        ring = [[bank, False] for bank in range(BANKS)]
+
+        def next_bank(shape, late=False):
+            place = 0
+            while ring[place][1]:
+                ring[place][1] = False
+                place += 1
+            bank = ring.pop(place)[0]
+            ring.append([bank, late])
+            return psum.tile(shape, F32, name=f"bank{bank}")
 
         ident = keep.tile([P, P], F32, name="ident")
         make_identity(nc, ident[:])
@@ -51,8 +61,8 @@ def tile_lambdarank_head_gradient_s11_kernel(tc, d_bytes, d_scale, v, delta, ipw
         raw = [keep.tile([P, PACK, RAW], U8, name=f"raw{s}", align_bytes=64) for s in range(GROUPS)]
         dlt = [keep.tile([P, PACK, RANKERS], BF16, name=f"dlt{s}", align_bytes=64) for s in range(GROUPS)]
         v_raw = [keep.tile([P, PACK, RANKERS], BF16, name=f"v_raw{g}", align_bytes=64) for g in range(PASSES)]
-        e_w = [keep.tile([P, PASSES, 2 * BANK], U8, name=f"e_w{half}", align_bytes=64) for half in range(HALVES)]
-        e_s = keep.tile([P, PASSES, FEATS], U8, name="e_s", align_bytes=64)
+        e_w = [keep.tile([P, PASSES, 2 * BANK], U8, name=f"e_w{half}", align_bytes=256) for half in range(HALVES)]
+        e_s = keep.tile([P, PASSES, FEATS], U8, name="e_s", align_bytes=256)
         ipw_bf = keep.tile([P, GROUPS, PACK], BF16, name="ipw_bf")
         ipw_f = keep.tile([P, GROUPS, PACK], F32, name="ipw_f")
 
@@ -68,10 +78,10 @@ def tile_lambdarank_head_gradient_s11_kernel(tc, d_bytes, d_scale, v, delta, ipw
         nc.vector.memset(warm[:].bitcast(I32), 0)
         nc.vector.memset(table_in[:], 0.0)
 
-        idle = psum.tile([P, BANK], F32, name="bank")
+        idle = next_bank([P, BANK])
 
-        def warm_up(count):
-            for i in range(count):
+        def warm_up(passes):
+            for _ in range(passes):
                 nc.tensor.matmul(out=idle[:], lhsT=warm[:, :P], rhs=warm[:], start=True, stop=True)
 
         nc.vector.memset(e_s[:].bitcast(I32), 0)
@@ -106,8 +116,8 @@ def tile_lambdarank_head_gradient_s11_kernel(tc, d_bytes, d_scale, v, delta, ipw
 
         names = ["v"] + [(kind, s) for kind in ("h", "lam") for s in range(GROUPS)]
         width = {name: RANKERS if name[0] == "lam" else FEATS for name in names}
-        codes = {name: keep.tile([P, width[name]], U32, name=f"codes{i}", align_bytes=64) for i, name in enumerate(names)}
-        planes = {name: keep.tile([P, width[name]], U8, name=f"planes{i}", align_bytes=64) for i, name in enumerate(names)}
+        codes = {name: keep.tile([P, width[name]], U32, name=f"codes{i}", align_bytes=256) for i, name in enumerate(names)}
+        planes = {name: keep.tile([P, width[name]], U8, name=f"planes{i}", align_bytes=256) for i, name in enumerate(names)}
         h_raw = [keep.tile([P, PACK, FEATS if s == 0 else BANK], BF16, name=f"h_raw{s}", align_bytes=64) for s in range(GROUPS)]
         grouped = {}
 
@@ -148,8 +158,8 @@ def tile_lambdarank_head_gradient_s11_kernel(tc, d_bytes, d_scale, v, delta, ipw
         def quantize_columns(name, first, stop):
             quantize(codes[name][:, first:stop], planes[name][:, first:stop], grouped_columns(name, first, stop).rearrange("p n t -> p (n t)"))
 
-        d_codes = [keep.tile([P, 2 * WORDS], U32, name=f"d_codes{p}", align_bytes=64) for p in range(STEPS)]
-        d_planes = [keep.tile([P, 2 * WORDS], U8, name=f"d_planes{p}", align_bytes=64) for p in range(STEPS)]
+        d_codes = [keep.tile([P, 2 * WORDS], U32, name=f"d_codes{p}", align_bytes=256) for p in range(STEPS)]
+        d_planes = [keep.tile([P, 2 * WORDS], U8, name=f"d_planes{p}", align_bytes=256) for p in range(STEPS)]
         wide, turned, d_grp = {}, {}, {}
         UNITS = 2 * PASSES
 
@@ -166,7 +176,7 @@ def tile_lambdarank_head_gradient_s11_kernel(tc, d_bytes, d_scale, v, delta, ipw
             nc.scalar.copy(out=new_wide(j, tiles)[:], in_=d_bytes_of(j, tiles))
 
         def turn(j, first=0, stop=PASSES):
-            bank = psum.tile([P, 2, PASSES, P], F32, name="bank")
+            bank = next_bank([P, 2, PASSES, P], late=True)
             words = wide[j].bitcast(F32)
             for g in range(first, stop):
                 turned[j, g] = bank
@@ -217,7 +227,7 @@ def tile_lambdarank_head_gradient_s11_kernel(tc, d_bytes, d_scale, v, delta, ipw
 
         def score(j):
             s, t = divmod(j, PACK)
-            diff = psum.tile([P, RANKERS], F32, name="bank")
+            diff = next_bank([P, RANKERS])
             times_d(j, diff[:], lambda g: (codes["v"][:, g * RANKERS : (g + 1) * RANKERS].bitcast(E4M3X4), planes["v"][:, g * RANKERS : (g + 1) * RANKERS]))
             if t == 0:
                 sig[s] = work.tile([P, PACK, RANKERS], F32, name="sig", bufs=3, align_bytes=64)
@@ -226,7 +236,7 @@ def tile_lambdarank_head_gradient_s11_kernel(tc, d_bytes, d_scale, v, delta, ipw
         encoded = {}
 
         def encode_product(j, first, stop):
-            encoded[j, first] = psum.tile([P, stop - first], F32, name="bank")
+            encoded[j, first] = next_bank([P, stop - first])
             times_d(j, encoded[j, first][:], e_columns(first, stop))
 
         def encode(j, first, stop):
@@ -242,7 +252,7 @@ def tile_lambdarank_head_gradient_s11_kernel(tc, d_bytes, d_scale, v, delta, ipw
 
         def encode_stacked(s, first, stop):
             for col in range(first, stop, P):
-                stacked[s, col] = psum.tile([P, PACK, P], F32, name="bank")
+                stacked[s, col] = next_bank([P, PACK, P])
                 for t in range(PACK):
                     times_d(PACK * s + t, stacked[s, col][:, t, :], e_columns(col, col + P))
 
@@ -261,7 +271,7 @@ def tile_lambdarank_head_gradient_s11_kernel(tc, d_bytes, d_scale, v, delta, ipw
             rows = slice(m * P, (m + 1) * P)
             for s in groups:
                 if s == 0:
-                    sums[m, first] = psum.tile([P, stop - first], F32, name="bank")
+                    sums[m, first] = next_bank([P, stop - first])
                 nc.tensor.matmul_mx(
                     out=sums[m, first][:], lhsT=codes["lam", s][:, rows].bitcast(E4M3X4), lhsT_scale=planes["lam", s][:, rows],
                     rhs=codes["h", s][:, first:stop].bitcast(E4M3X4), rhs_scale=planes["h", s][:, first:stop],

@@ -210,8 +210,8 @@ def tile_lambdarank_head_gradient_s11_kernel(tc, d_bytes, d_scale, v, delta, ipw
             cols = slice(P * (first - UNITS * p), P * (stop - UNITS * p))
             quantize(d_codes[p][:, cols], d_planes[p][:, cols], d_grouped(first, stop))
 
-        def times_d(j, out, moving):
-            for g in range(PASSES):
+        def times_d(j, out, moving, passes=range(PASSES)):
+            for g in passes:
                 cols = slice(WORDS * (j % 2) + g * P, WORDS * (j % 2) + (g + 1) * P)
                 rhs, rhs_scale = moving(g)
                 nc.tensor.matmul_mx(
@@ -225,13 +225,24 @@ def tile_lambdarank_head_gradient_s11_kernel(tc, d_bytes, d_scale, v, delta, ipw
 
         sig = {}
 
-        def score(j):
+        diff = {}
+
+        def score_pass(j, g):
+            if g == 0:
+                diff[j] = next_bank([P, RANKERS])
+            cols = slice(g * RANKERS, (g + 1) * RANKERS)
+            times_d(j, diff[j][:], lambda g: (codes["v"][:, cols].bitcast(E4M3X4), planes["v"][:, cols]), (g,))
+
+        def squash(j):
             s, t = divmod(j, PACK)
-            diff = next_bank([P, RANKERS])
-            times_d(j, diff[:], lambda g: (codes["v"][:, g * RANKERS : (g + 1) * RANKERS].bitcast(E4M3X4), planes["v"][:, g * RANKERS : (g + 1) * RANKERS]))
+            score_pass(j, PASSES - 1)
             if t == 0:
                 sig[s] = work.tile([P, PACK, RANKERS], F32, name="sig", bufs=3, align_bytes=64)
-            nc.scalar.activation(out=sig[s][:, t, :], in_=diff[:], func=SIGMOID, scale=-1.0)
+            nc.scalar.activation(out=sig[s][:, t, :], in_=diff[j][:], func=SIGMOID, scale=-1.0)
+
+        def score(j):
+            score_pass(j, 0)
+            squash(j)
 
         encoded = {}
 
@@ -342,10 +353,10 @@ def tile_lambdarank_head_gradient_s11_kernel(tc, d_bytes, d_scale, v, delta, ipw
         }
         direct = {p: (1, BANK + P * (p - 4), BANK + P * (p - 3)) for p in range(4, STEPS)}
         behind = {
-            1: by_scalar("v", RANKERS, FEATS - WINDOW) + low(2, 3) + turns(3) + [(widen, 8, 2)] + high(2, 3),
-            2: scores(0, 1, 2, 3) + turns(4) + [(widen, 10, 2)],
-            3: low(4, 5) + [(encode_stacked, *direct[4])] + scores(4) + turns(5) + [(widen, 12, 2)] + room(h[0], WINDOW, BANK) + by_scalar(h[0], WINDOW, BANK) + room(h[1], BANK, FEATS),
-            4: scores(5, 6, 7) + [(encode_stacked, *direct[5])] + low(6) + turns(6) + [(widen, 14, 2)],
+            1: by_scalar("v", RANKERS, FEATS - WINDOW) + low(2) + high(2) + low(3) + [(widen, 8, 2)] + turns(3) + high(3) + [(score_pass, j, 0) for j in range(PACK)],
+            2: [(squash, j) for j in range(PACK)] + turns(4) + [(widen, 10, 2)],
+            3: low(4, 5) + [(encode_stacked, *direct[4])] + scores(4, 5) + turns(5) + [(widen, 12, 2)] + room(h[0], WINDOW, BANK) + by_scalar(h[0], WINDOW, BANK) + room(h[1], BANK, FEATS),
+            4: scores(6, 7) + [(encode_stacked, *direct[5])] + low(6) + turns(6) + [(widen, 14, 2)],
             5: low(7) + room(h[0], BANK, FEATS) + by_scalar(h[0], 512, 768) + scores(8, 9) + [(encode_stacked, *direct[6])] + scores(10) + turns(7) + by_scalar(h[0], 768, 1024),
             6: scores(11) + low(8, 9) + [(encode_stacked, *direct[7])] + low(10, 11) + room(h[1], 0, BANK) + by_scalar(h[1], 0, 256) + [(encode_stacked, 2, BANK, FEATS)] + by_scalar(h[1], 256, 512),
             7: [],
@@ -357,6 +368,7 @@ def tile_lambdarank_head_gradient_s11_kernel(tc, d_bytes, d_scale, v, delta, ipw
         scale(3)
         weigh_rows(1, 0, BANK)
         d_quantize(4, 6)
+        quantize_columns("v", QUARTER, RANKERS)
         quantize_columns("v", 0, QUARTER)
         d_quantize(6, 8)
         run(behind[1])
@@ -365,7 +377,7 @@ def tile_lambdarank_head_gradient_s11_kernel(tc, d_bytes, d_scale, v, delta, ipw
             scale(2 * p)
             scale(2 * p + 1)
             if p == 2:
-                quantize_columns("v", QUARTER, FEATS - WINDOW)
+                quantize_columns("v", RANKERS, FEATS - WINDOW)
                 quantize_columns(*windows[p])
                 d_quantize(UNITS * p, UNITS * (p + 1))
             elif p == 3:

@@ -30,7 +30,9 @@ STEPS = TILES // 2
 QTILES = RANKERS // P
 WORDS = PASSES * P
 WINDOW = 384
+SHARE = 320
 QUARTER = FEATS // 4
+A, B = 0, 1
 
 FLOPS = 2 * PAIRS * RAW * RANKERS + 2 * PAIRS * RAW * FEATS + 2 * RANKERS * PAIRS * FEATS
 
@@ -41,14 +43,17 @@ def tile_lambdarank_head_gradient_s11_kernel(tc, d_bytes, d_scale, v, delta, ipw
         keep = ctx.enter_context(tc.tile_pool(name="keep", bufs=1))
         work = ctx.enter_context(tc.tile_pool(name="work", bufs=1))
         psum = ctx.enter_context(tc.psum_pool(name="psum", bufs=1))
-        ring = [[bank, False] for bank in range(BANKS)]
+        ring = [[bank, 0] for bank in range(BANKS)]
 
-        def next_bank(shape, late=False):
+        def take_bank():
             place = 0
-            while ring[place][1]:
-                ring[place][1] = False
+            while place < len(ring) and ring[place][1]:
+                ring[place][1] -= 1
                 place += 1
-            bank = ring.pop(place)[0]
+            return ring.pop(place % len(ring))[0]
+
+        def next_bank(shape, late=0):
+            bank = take_bank()
             ring.append([bank, late])
             return psum.tile(shape, F32, name=f"bank{bank}")
 
@@ -77,6 +82,7 @@ def tile_lambdarank_head_gradient_s11_kernel(tc, d_bytes, d_scale, v, delta, ipw
         warm = keep.tile([P, BANK], BF16, name="warm", align_bytes=64)
         nc.vector.memset(warm[:].bitcast(I32), 0)
         nc.vector.memset(table_in[:], 0.0)
+        nc.vector.memset(e_s[:].bitcast(I32), 0)
 
         idle = next_bank([P, BANK])
 
@@ -84,13 +90,21 @@ def tile_lambdarank_head_gradient_s11_kernel(tc, d_bytes, d_scale, v, delta, ipw
             for _ in range(passes):
                 nc.tensor.matmul(out=idle[:], lhsT=warm[:, :P], rhs=warm[:], start=True, stop=True)
 
-        nc.vector.memset(e_s[:].bitcast(I32), 0)
-
         def load_raw(s, first, stop):
             nc.sync.dma_start(out=raw[s][:, first:stop, :], in_=d_view[s][:, first:stop, :])
 
         def load_words(half):
             nc.sync.dma_start(out=e_w[half][:], in_=w_view[:, :, 2 * BANK * half : 2 * BANK * (half + 1)])
+
+        def load_scales():
+            for r in range(PACK):
+                nc.sync.dma_start(out=e_s[r:P:32].bitcast(I32), in_=s_view[r:16:PACK].bitcast(I32))
+
+        def load_v(g):
+            nc.sync.dma_start(out=v_raw[g][:], in_=v_view[g])
+
+        def load_delta(s):
+            nc.sync.dma_start(out=dlt[s][:], in_=dlt_view[s])
 
         load_raw(0, 0, 1)
         nc.scalar.dma_start(out=scale_kp[:], in_=d_scale.rearrange("o (g p t) -> p (o g) t", p=P, t=PACK))
@@ -99,18 +113,17 @@ def tile_lambdarank_head_gradient_s11_kernel(tc, d_bytes, d_scale, v, delta, ipw
         load_raw(0, 1, 2)
         load_raw(0, 2, 4)
         load_raw(1, 0, 2)
-        for r in range(PACK):
-            nc.sync.dma_start(out=e_s[r:P:32].bitcast(I32), in_=s_view[r:16:PACK].bitcast(I32))
-        load_words(0)
-        nc.sync.dma_start(out=v_raw[0][:], in_=v_view[0])
-        load_words(1)
+        load_scales()
+        load_words(B)
+        load_v(0)
+        load_words(A)
         load_raw(1, 2, 4)
-        nc.sync.dma_start(out=v_raw[1][:], in_=v_view[1])
+        load_v(1)
         load_raw(2, 0, 4)
-        nc.sync.dma_start(out=dlt[0][:], in_=dlt_view[0])
+        load_delta(0)
         load_raw(3, 0, 4)
         for s in range(1, GROUPS):
-            nc.sync.dma_start(out=dlt[s][:], in_=dlt_view[s])
+            load_delta(s)
 
         on_vector, on_scalar = nc.vector.tensor_copy, nc.scalar.copy
 
@@ -121,8 +134,8 @@ def tile_lambdarank_head_gradient_s11_kernel(tc, d_bytes, d_scale, v, delta, ipw
         h_raw = [keep.tile([P, PACK, FEATS if s == 0 else BANK], BF16, name=f"h_raw{s}", align_bytes=64) for s in range(GROUPS)]
         grouped = {}
 
-        def new_grouped(name, first, stop, tag, bufs):
-            grouped[name, first] = work.tile([P, stop - first, PACK], BF16, name=tag, bufs=bufs, align_bytes=64)
+        def room(name, first, stop, slot):
+            grouped[name, first] = work.tile([P, stop - first, PACK], BF16, name=slot, align_bytes=64)
 
         def grouped_columns(name, first, stop):
             origin = max(start for (other, start) in grouped if other == name and start <= first)
@@ -134,7 +147,7 @@ def tile_lambdarank_head_gradient_s11_kernel(tc, d_bytes, d_scale, v, delta, ipw
                 return v_raw[g][:, :, first - g * RANKERS : stop - g * RANKERS]
             return h_raw[name[1]][:, :, first:stop]
 
-        def interleave(name, first, stop, copy):
+        def interleave(name, first, stop, copy=on_scalar):
             copy(out=grouped_columns(name, first, stop).rearrange("p (c i) t -> p c t i", i=8), in_=rows_of(name, first, stop).rearrange("p t (c i) -> p c t i", i=8))
 
         def lam_product(engine, s, first, stop, run):
@@ -145,8 +158,11 @@ def tile_lambdarank_head_gradient_s11_kernel(tc, d_bytes, d_scale, v, delta, ipw
                 op=MULT,
             )
 
-        def in_window(name, first, stop):
-            new_grouped(name, first, stop, "window0", 1)
+        def in_window(name, first, stop, slot):
+            room(name, first, stop, slot)
+            by_gpsimd(name, first, stop)
+
+        def by_gpsimd(name, first, stop):
             if name[0] == "lam":
                 lam_product(nc.gpsimd, name[1], first, stop, 8)
             else:
@@ -155,7 +171,7 @@ def tile_lambdarank_head_gradient_s11_kernel(tc, d_bytes, d_scale, v, delta, ipw
         def quantize(out, scales, in_):
             nc.vector.quantize_mx(out=out.bitcast(E4M3X4), scales=scales, in_=in_)
 
-        def quantize_columns(name, first, stop):
+        def quant(name, first, stop):
             quantize(codes[name][:, first:stop], planes[name][:, first:stop], grouped_columns(name, first, stop).rearrange("p n t -> p (n t)"))
 
         d_codes = [keep.tile([P, 2 * WORDS], U32, name=f"d_codes{p}", align_bytes=256) for p in range(STEPS)]
@@ -169,31 +185,31 @@ def tile_lambdarank_head_gradient_s11_kernel(tc, d_bytes, d_scale, v, delta, ipw
                 wide[j + i] = both[:, i, :]
             return both
 
-        def d_bytes_of(j, tiles):
-            return raw[j // PACK][:, j % PACK : j % PACK + tiles, :].bitcast(FP8)
+        def cast(copy, out, in_):
+            copy(out=out.rearrange("p j (g u m e) -> p (j g) u m e", u=2, m=P, e=2), in_=in_.bitcast(FP8).rearrange("p j (g m u e) -> p (j g) u m e", m=P, u=2, e=2))
+
+        def cast_in_order(out, in_):
+            on_vector(out=out.rearrange("p (u m e) -> p m u e", u=2, e=2), in_=in_.bitcast(FP8).rearrange("p (m u e) -> p m u e", u=2, e=2))
 
         def widen(j, tiles):
-            nc.scalar.copy(out=new_wide(j, tiles)[:], in_=d_bytes_of(j, tiles))
+            cast(on_scalar, new_wide(j, tiles)[:], raw[j // PACK][:, j % PACK : j % PACK + tiles, :])
 
         def turn(j, first=0, stop=PASSES):
-            bank = next_bank([P, 2, PASSES, P], late=True)
+            bank = next_bank([P, 2, PASSES, P], late=2 if j > 1 else 0)
             words = wide[j].bitcast(F32)
             for g in range(first, stop):
                 turned[j, g] = bank
                 for u in range(2):
-                    nc.tensor.transpose(bank[:, u, g, :], words[:, 2 * P * g + u : 2 * P * (g + 1) : 2], ident[:])
+                    nc.tensor.transpose(bank[:, u, g, :], words[:, P * (2 * g + u) : P * (2 * g + u + 1)], ident[:])
 
         def d_grouped(first, stop):
             if first < UNITS:
                 if first not in d_grp:
-                    if first == PASSES:
-                        d_grp[first] = work.tile([P, P, PACK], BF16, name="window0", bufs=1, align_bytes=64)
-                    else:
-                        d_grp[first] = work.tile([P, P, PACK], BF16, name="d_first", bufs=UNITS - 1, align_bytes=64)
-                return d_grp[first][:].rearrange("p r t -> p (r t)")
-            origin = first - first % UNITS
+                    d_grp[first] = work.tile([P, GROUP], BF16, name=f"unit{first}", align_bytes=64)
+                return d_grp[first][:]
+            origin = first - first % PASSES
             if origin not in d_grp:
-                d_grp[origin] = work.tile([P, 2 * RAW], BF16, name="d_grp", bufs=2, align_bytes=64)
+                d_grp[origin] = work.tile([P, RAW], BF16, name=f"tile{origin // PASSES}", align_bytes=64)
             return d_grp[origin][:, GROUP * (first - origin) : GROUP * (stop - origin)]
 
         def scale(j, first=0, stop=PASSES):
@@ -205,7 +221,7 @@ def tile_lambdarank_head_gradient_s11_kernel(tc, d_bytes, d_scale, v, delta, ipw
                 op=MULT,
             )
 
-        def d_quantize(first, stop):
+        def d_quant(first, stop):
             p = first // UNITS
             cols = slice(P * (first - UNITS * p), P * (stop - UNITS * p))
             quantize(d_codes[p][:, cols], d_planes[p][:, cols], d_grouped(first, stop))
@@ -223,9 +239,7 @@ def tile_lambdarank_head_gradient_s11_kernel(tc, d_bytes, d_scale, v, delta, ipw
             half, origin = first // BANK, first - first % BANK
             return lambda g: (e_w[half][:, g, 2 * (first - origin) : 2 * (stop - origin)].bitcast(E2M1X4), e_s[:, g, first:stop])
 
-        sig = {}
-
-        diff = {}
+        sig, diff = {}, {}
 
         def score_pass(j, g):
             if g == 0:
@@ -240,31 +254,44 @@ def tile_lambdarank_head_gradient_s11_kernel(tc, d_bytes, d_scale, v, delta, ipw
                 sig[s] = work.tile([P, PACK, RANKERS], F32, name="sig", bufs=3, align_bytes=64)
             nc.scalar.activation(out=sig[s][:, t, :], in_=diff[j][:], func=SIGMOID, scale=-1.0)
 
-        def score(j):
-            score_pass(j, 0)
-            squash(j)
+        def scores(*tiles):
+            for j in tiles:
+                score_pass(j, 0)
+                squash(j)
 
         encoded = {}
 
-        def encode_product(j, first, stop):
-            encoded[j, first] = next_bank([P, stop - first])
-            times_d(j, encoded[j, first][:], e_columns(first, stop))
+        def encode_product(j, half):
+            encoded[j, half] = next_bank([P, BANK])
+            times_d(j, encoded[j, half][:], e_columns(BANK * half, BANK * (half + 1)))
 
-        def encode(j, first, stop):
+        def weigh_on_scalar(j, half):
             s, t = divmod(j, PACK)
-            encode_product(j, first, stop)
-            nc.scalar.activation(out=h_raw[s][:, t, first:stop], in_=encoded[j, first][:], func=COPY, scale=ipw_f[:, s, t : t + 1])
+            nc.scalar.activation(out=h_raw[s][:, t, BANK * half : BANK * (half + 1)], in_=encoded[j, half][:], func=COPY, scale=ipw_f[:, s, t : t + 1])
 
-        def weigh_rows(j, first, stop):
+        def encode(half, *tiles):
+            for j in tiles:
+                encode_product(j, half)
+                weigh_on_scalar(j, half)
+
+        def encode_part(first, stop, *tiles):
+            for j in tiles:
+                s, t = divmod(j, PACK)
+                part = next_bank([P, stop - first])
+                times_d(j, part[:], e_columns(first, stop))
+                nc.scalar.activation(out=h_raw[s][:, t, first:stop], in_=part[:], func=COPY, scale=ipw_f[:, s, t : t + 1])
+
+        def weigh_rows(j, half):
             s, t = divmod(j, PACK)
-            nc.vector.tensor_scalar(out=h_raw[s][:, t, first:stop], in0=encoded[j, first][:], scalar1=ipw_f[:, s, t : t + 1], scalar2=None, op0=MULT)
+            nc.vector.tensor_scalar(out=h_raw[s][:, t, BANK * half : BANK * (half + 1)], in0=encoded[j, half][:], scalar1=ipw_f[:, s, t : t + 1], scalar2=None, op0=MULT)
 
         stacked = {}
 
-        def encode_stacked(s, first, stop):
+        def stack(s, first, stop, tiles=range(PACK)):
             for col in range(first, stop, P):
-                stacked[s, col] = next_bank([P, PACK, P])
-                for t in range(PACK):
+                if (s, col) not in stacked:
+                    stacked[s, col] = next_bank([P, PACK, P], late=0)
+                for t in tiles:
                     times_d(PACK * s + t, stacked[s, col][:, t, :], e_columns(col, col + P))
 
         def weigh(s, first, stop):
@@ -276,35 +303,47 @@ def tile_lambdarank_head_gradient_s11_kernel(tc, d_bytes, d_scale, v, delta, ipw
                     op=MULT,
                 )
 
-        sums = {}
+        sums, held = {}, {}
 
         def update(m, first, stop, groups):
             rows = slice(m * P, (m + 1) * P)
             for s in groups:
-                if s == 0:
-                    sums[m, first] = next_bank([P, stop - first])
+                opening = (m, first) not in sums
+                if opening:
+                    held[m, first] = [take_bank(), GROUPS]
+                    sums[m, first] = psum.tile([P, stop - first], F32, name=f"bank{held[m, first][0]}")
+                held[m, first][1] -= 1
                 nc.tensor.matmul_mx(
                     out=sums[m, first][:], lhsT=codes["lam", s][:, rows].bitcast(E4M3X4), lhsT_scale=planes["lam", s][:, rows],
                     rhs=codes["h", s][:, first:stop].bitcast(E4M3X4), rhs_scale=planes["h", s][:, first:stop],
-                    start=(s == 0), stop=(s == GROUPS - 1),
+                    start=opening, stop=(held[m, first][1] == 0),
                 )
 
-        def store(m, first, stop, copy):
-            res = work.tile([P, stop - first], F32, name="res", bufs=9)
+        def store(m, first, stop, copy, slot):
+            res = work.tile([P, stop - first], F32, name=slot, align_bytes=64)
             copy(out=res[:], in_=sums[m, first][:])
+            ring.append([held[m, first][0], 0])
             nc.sync.dma_start(out=out[m * P : (m + 1) * P, first:stop], in_=res[:])
 
-        def run(calls):
-            for call in calls:
-                call[0](*call[1:])
+        def turns(p):
+            turn(2 * p)
+            turn(2 * p + 1)
+
+        def scales(p):
+            scale(2 * p)
+            scale(2 * p + 1)
+
+        def step_quant(p):
+            d_quant(UNITS * p, UNITS * p + PASSES)
+            d_quant(UNITS * p + PASSES, UNITS * (p + 1))
 
         h = [("h", s) for s in range(GROUPS)]
         lam = [("lam", s) for s in range(GROUPS)]
+        LOW, HIGH = (0, BANK), (BANK, FEATS)
 
         first_tile = new_wide(0, 1)
-        for first in range(0, RAW, QUARTER):
-            copy = on_scalar if first % GROUP else on_vector
-            copy(out=first_tile[:, :, first : first + QUARTER], in_=d_bytes_of(0, 1)[:, :, first : first + QUARTER])
+        cast_in_order(first_tile[:, 0, :GROUP], raw[0][:, 0, :GROUP])
+        cast(on_scalar, first_tile[:, :, GROUP:], raw[0][:, 0:1, GROUP:])
         widen(1, 1)
         widen(2, 1)
         warm_up(4)
@@ -314,121 +353,143 @@ def tile_lambdarank_head_gradient_s11_kernel(tc, d_bytes, d_scale, v, delta, ipw
         widen(3, 1)
         turn(1)
         warm_up(1)
-        for j in range(2, PACK):
-            turn(j)
+        turns(1)
         warm_up(1)
         widen(4, 2)
         nc.scalar.copy(out=ipw_f[:], in_=ipw_bf[:])
         scale(0, 0, 1)
         for unit in range(1, UNITS):
             scale(unit // PASSES, unit % PASSES, unit % PASSES + 1)
-            d_quantize(unit - 1, unit)
-        d_quantize(UNITS - 1, UNITS)
-
-        def low(*tiles):
-            return [(encode, j, 0, BANK) for j in tiles]
-
-        def high(*tiles):
-            return [(encode, j, BANK, FEATS) for j in tiles]
-
-        def scores(*tiles):
-            return [(score, j) for j in tiles]
-
-        def turns(p):
-            return [(turn, 2 * p), (turn, 2 * p + 1)]
-
-        def by_scalar(name, first, stop):
-            return [(interleave, name, first, stop, on_scalar)]
-
-        def room(name, first, stop):
-            return [(new_grouped, name, first, stop, "grouped", 8)]
-
-        windows = {
-            2: ("v", FEATS - WINDOW, FEATS),
-            3: (h[0], 0, WINDOW),
-            4: (lam[0], 0, 256),
-            5: (lam[0], 256, 512),
-            6: (lam[1], 0, 256),
-            7: (lam[1], 256, 512),
-        }
-        direct = {p: (1, BANK + P * (p - 4), BANK + P * (p - 3)) for p in range(4, STEPS)}
-        behind = {
-            1: by_scalar("v", RANKERS, FEATS - WINDOW) + low(2) + high(2) + low(3) + [(widen, 8, 2)] + turns(3) + high(3) + [(score_pass, j, 0) for j in range(PACK)],
-            2: [(squash, j) for j in range(PACK)] + turns(4) + [(widen, 10, 2)],
-            3: low(4, 5) + [(encode_stacked, *direct[4])] + scores(4, 5) + turns(5) + [(widen, 12, 2)] + room(h[0], WINDOW, BANK) + by_scalar(h[0], WINDOW, BANK) + room(h[1], BANK, FEATS),
-            4: scores(6, 7) + [(encode_stacked, *direct[5])] + low(6) + turns(6) + [(widen, 14, 2)],
-            5: low(7) + room(h[0], BANK, FEATS) + by_scalar(h[0], 512, 768) + scores(8, 9) + [(encode_stacked, *direct[6])] + scores(10) + turns(7) + by_scalar(h[0], 768, 1024),
-            6: scores(11) + low(8, 9) + [(encode_stacked, *direct[7])] + low(10, 11) + room(h[1], 0, BANK) + by_scalar(h[1], 0, 256) + [(encode_stacked, 2, BANK, FEATS)] + by_scalar(h[1], 256, 512),
-            7: [],
-        }
-        after = {5: (h[0], WINDOW, BANK), 7: (h[1], BANK, FEATS)}
-        run(low(0) + [(encode_product, 1, 0, BANK)] + turns(2) + room("v", QUARTER, FEATS - WINDOW) + by_scalar("v", QUARTER, RANKERS) + [(widen, 6, 2)] + high(0, 1))
-        in_window("v", 0, QUARTER)
-        scale(2)
-        scale(3)
-        weigh_rows(1, 0, BANK)
-        d_quantize(4, 6)
-        quantize_columns("v", QUARTER, RANKERS)
-        quantize_columns("v", 0, QUARTER)
-        d_quantize(6, 8)
-        run(behind[1])
-        for p in range(2, STEPS):
-            in_window(*windows[p])
-            scale(2 * p)
-            scale(2 * p + 1)
-            if p == 2:
-                quantize_columns("v", RANKERS, FEATS - WINDOW)
-                quantize_columns(*windows[p])
-                d_quantize(UNITS * p, UNITS * (p + 1))
-            elif p == 3:
-                d_quantize(UNITS * p, UNITS * p + PASSES)
-                quantize_columns(*windows[p])
-                d_quantize(UNITS * p + PASSES, UNITS * (p + 1))
-            else:
-                weigh(*direct[p])
-                d_quantize(UNITS * p, UNITS * (p + 1))
-                quantize_columns(*windows[p])
-            if p in after:
-                quantize_columns(*after[p])
-            run(behind[p])
-
-        last = GROUPS - 1
-        in_window(lam[2], 0, 256)
-        run(room(h[2], BANK, FEATS))
-        weigh(2, BANK, FEATS)
-        run(scores(12, 13, 14, 15) + room(h[2], 0, BANK) + by_scalar(h[2], 0, BANK))
-        encode_stacked(last, BANK, FEATS)
-        run(low(12, 13, 14, 15) + room(h[last], 0, BANK) + by_scalar(h[last], 0, WINDOW))
-        for job in ((h[0], BANK, FEATS), (h[1], 0, BANK), (lam[2], 0, 256), (h[2], BANK, FEATS)):
-            quantize_columns(*job)
-        in_window(lam[2], 256, 512)
-        run(room(h[last], BANK, FEATS) + room(lam[last], 0, RANKERS))
-        weigh(last, BANK, FEATS)
-        lam_product(nc.vector, last, 0, P, 2)
-        quantize_columns(lam[2], 256, 512)
-        quantize_columns(h[last], BANK, FEATS)
-        for m in range(QTILES):
-            if m + 1 < QTILES:
-                lam_product(nc.vector, last, (m + 1) * P, (m + 2) * P, 2)
-            else:
-                interleave(h[last], WINDOW, BANK, on_vector)
-            quantize_columns(lam[last], m * P, (m + 1) * P)
-        quantize_columns(h[2], 0, BANK)
-        quantize_columns(h[last], 0, BANK)
-
-        def finish(m, first, stop, groups, copy=on_scalar):
-            update(m, first, stop, groups)
-            store(m, first, stop, copy)
-
-        for m in range(QTILES):
-            update(m, BANK, FEATS, range(last))
-        for m in (0, 1):
-            finish(m, BANK, FEATS, (last,))
-        for m in (0, 1):
-            update(m, 0, BANK, (0, 1))
-            finish(m + 2, BANK, FEATS, (last,))
-        for m in (0, 1):
-            finish(m, 0, BANK, (2, last), on_vector if m == 0 else on_scalar)
-        pieces = [(2, 0, QUARTER), (2, QUARTER, BANK), (3, 0, QUARTER), (3, QUARTER, QUARTER + P), (3, QUARTER + P, BANK)]
-        for i, piece in enumerate(pieces):
-            finish(*piece, range(GROUPS), on_scalar if i % 2 else on_vector)
+            d_quant(unit - 1, unit)
+        d_quant(UNITS - 1, UNITS)
+        encode(B, 0)
+        encode_product(1, B)
+        turns(2)
+        room("v", QUARTER, RANKERS, "spare0")
+        interleave("v", QUARTER, RANKERS)
+        weigh_on_scalar(1, B)
+        widen(6, 2)
+        encode(A, 0, 1)
+        in_window("v", 0, QUARTER, "unit2")
+        scales(1)
+        d_quant(4, 6)
+        quant("v", QUARTER, RANKERS)
+        quant("v", 0, QUARTER)
+        d_quant(6, 8)
+        room("v", RANKERS, FEATS - WINDOW, "unit0")
+        interleave("v", RANKERS, FEATS - WINDOW)
+        encode(B, 2)
+        encode(A, 2)
+        encode_product(3, B)
+        turns(3)
+        widen(8, 2)
+        encode(A, 3)
+        for j in range(PACK):
+            score_pass(j, 0)
+        in_window("v", FEATS - WINDOW, FEATS, "unit2")
+        scales(2)
+        weigh_rows(3, B)
+        quant("v", RANKERS, FEATS - WINDOW)
+        quant("v", FEATS - WINDOW, FEATS)
+        step_quant(2)
+        for j in range(PACK):
+            squash(j)
+        turns(4)
+        widen(10, 2)
+        encode(A, 4, 5)
+        room(h[0], *HIGH, "tile4")
+        by_gpsimd(h[0], BANK, BANK + SHARE)
+        scales(3)
+        step_quant(3)
+        scores(4, 5)
+        room(h[1], *HIGH, "spare0")
+        stack(1, 512, 640)
+        turns(5)
+        widen(12, 2)
+        scores(6, 7)
+        in_window(lam[0], 0, QUARTER, "tile6")
+        scales(4)
+        weigh(1, 512, 640)
+        step_quant(4)
+        stack(1, 640, 768)
+        encode(A, 6, 7)
+        turns(6)
+        widen(14, 2)
+        scores(8, 9)
+        in_window(lam[0], QUARTER, RANKERS, "tile8")
+        scales(5)
+        weigh(1, 640, 768)
+        step_quant(5)
+        stack(1, 768, 896)
+        encode(A, 8, 9)
+        turns(7)
+        interleave(h[0], BANK + SHARE, FEATS)
+        scores(10, 11)
+        for s, slot in ((0, "tile2"), (1, "tile3"), (2, "tile5")):
+            room(h[s], *LOW, slot)
+        in_window(lam[1], 0, QUARTER, "tile10")
+        scales(6)
+        weigh(1, 768, 896)
+        step_quant(6)
+        stack(1, 896, 1024)
+        interleave(h[0], 0, QUARTER)
+        encode(A, 10, 11)
+        scores(12, 13)
+        in_window(lam[1], QUARTER, RANKERS, "tile12")
+        scales(7)
+        weigh(1, 896, 1024)
+        step_quant(7)
+        room(h[2], *HIGH, "spare1")
+        stack(2, 512, 768)
+        interleave(h[0], QUARTER, BANK)
+        scores(14, 15)
+        stack(2, 768, 1024)
+        interleave(h[1], 0, QUARTER)
+        for job in ((h[0], *HIGH), (h[1], *HIGH), (lam[1], 0, QUARTER), (lam[1], QUARTER, RANKERS), (lam[0], 0, QUARTER), (lam[0], QUARTER, RANKERS)):
+            quant(*job)
+        room(h[3], *HIGH, "tile7")
+        room(h[3], *LOW, "tile9")
+        in_window(lam[2], 0, QUARTER, "tile6")
+        in_window(lam[3], 0, WINDOW, "tile4")
+        weigh(2, *HIGH)
+        stack(3, *HIGH)
+        interleave(h[1], QUARTER, BANK)
+        interleave(h[2], *LOW)
+        weigh(3, *HIGH)
+        stack(3, QUARTER, BANK)
+        weigh(3, QUARTER, BANK)
+        for s in (0, 1):
+            for m in range(QTILES):
+                update(m, *HIGH, (s,))
+        encode_part(0, QUARTER, 12, 13, 14, 15)
+        interleave(h[3], 0, QUARTER)
+        for job in ((h[3], *HIGH), (lam[3], 0, WINDOW), (lam[2], 0, QUARTER), (h[2], *HIGH), (h[0], *LOW), (h[1], *LOW)):
+            quant(*job)
+        for s, first, slot in ((2, QUARTER, "unit1"), (2, WINDOW, "unit3"), (3, WINDOW, "unit2")):
+            room(lam[s], first, first + P, slot)
+        lam_product(nc.vector, 2, QUARTER, WINDOW, 2)
+        quant(h[2], *LOW)
+        quant(lam[2], QUARTER, WINDOW)
+        quant(h[3], *LOW)
+        lam_product(nc.vector, 2, WINDOW, RANKERS, 2)
+        lam_product(nc.vector, 3, WINDOW, RANKERS, 2)
+        quant(lam[2], WINDOW, RANKERS)
+        quant(lam[3], WINDOW, RANKERS)
+        for m in range(QTILES - 1):
+            update(m, *HIGH, (3,))
+        for m in range(2):
+            update(m, *HIGH, (2,))
+            store(m, *HIGH, on_scalar, f"res{m}")
+        for s in (0, 1):
+            for m in range(QTILES - 1):
+                update(m, *LOW, (s,))
+        update(2, *HIGH, (2,))
+        store(2, *HIGH, on_scalar, "res2")
+        for m in range(QTILES - 1):
+            update(m, *LOW, (2, 3))
+            store(m, *LOW, on_scalar, f"tile{13 + m}")
+        update(QTILES - 1, *HIGH, (2, 3))
+        store(QTILES - 1, *HIGH, on_vector, "tile11")
+        for i, piece in enumerate([(0, QUARTER), (QUARTER, QUARTER + P), (QUARTER + P, BANK)]):
+            update(QTILES - 1, *piece, range(GROUPS))
+            store(QTILES - 1, *piece, on_vector if i % 2 else on_scalar, f"last{i}")

@@ -148,7 +148,7 @@ def tile_lambdarank_head_gradient_s11_kernel(tc, d_bytes, d_scale, v, delta, ipw
             return h_raw[name[1]][:, :, first:stop]
 
         def interleave(name, first, stop, copy=on_scalar):
-            copy(out=grouped_columns(name, first, stop).rearrange("p (c i) t -> p c t i", i=8), in_=rows_of(name, first, stop).rearrange("p t (c i) -> p c t i", i=8))
+            copy(out=grouped_columns(name, first, stop).rearrange("p (c i) t -> p c t i", i=4), in_=rows_of(name, first, stop).rearrange("p t (c i) -> p c t i", i=4))
 
         def lam_product(engine, s, first, stop, run):
             engine.tensor_tensor(
@@ -467,12 +467,12 @@ def tile_lambdarank_head_gradient_s11_kernel(tc, d_bytes, d_scale, v, delta, ipw
             quant(*job)
         for s, first, slot in ((2, QUARTER, "unit1"), (2, WINDOW, "unit3"), (3, WINDOW, "unit2")):
             room(lam[s], first, first + P, slot)
-        lam_product(nc.vector, 2, QUARTER, WINDOW, 2)
+        lam_product(nc.vector, 2, QUARTER, WINDOW, 4)
         quant(h[2], *LOW)
         quant(lam[2], QUARTER, WINDOW)
         quant(h[3], *LOW)
-        lam_product(nc.vector, 2, WINDOW, RANKERS, 2)
-        lam_product(nc.vector, 3, WINDOW, RANKERS, 2)
+        lam_product(nc.vector, 2, WINDOW, RANKERS, 4)
+        lam_product(nc.vector, 3, WINDOW, RANKERS, 4)
         quant(lam[2], WINDOW, RANKERS)
         quant(lam[3], WINDOW, RANKERS)
         for m in range(QTILES - 1):

@@ -31,6 +31,7 @@ QTILES = RANKERS // P
 WORDS = PASSES * P
 WINDOW = 384
 SHARE = 320
+HALF_ROWS = P // 2
 QUARTER = FEATS // 4
 A, B = 0, 1
 
@@ -188,14 +189,16 @@ def tile_lambdarank_head_gradient_s11_kernel(tc, d_bytes, d_scale, v, delta, ipw
         def cast(copy, out, in_):
             copy(out=out.rearrange("p j (g u m e) -> p (j g) u m e", u=2, m=P, e=2), in_=in_.bitcast(FP8).rearrange("p j (g m u e) -> p (j g) u m e", m=P, u=2, e=2))
 
-        def cast_in_order(out, in_):
-            on_vector(out=out.rearrange("p (u m e) -> p m u e", u=2, e=2), in_=in_.bitcast(FP8).rearrange("p (m u e) -> p m u e", u=2, e=2))
+        def cast_half(g, half, copy):
+            rows = slice(HALF_ROWS * half, HALF_ROWS * (half + 1))
+            words = wide[0][:, GROUP * g : GROUP * (g + 1)].rearrange("p (u m e) -> p m u e", u=2, e=2)[:, rows]
+            copy(out=words, in_=raw[0][:, 0, GROUP * g : GROUP * (g + 1)].bitcast(FP8).rearrange("p (m u e) -> p m u e", u=2, e=2)[:, rows])
 
         def widen(j, tiles):
             cast(on_scalar, new_wide(j, tiles)[:], raw[j // PACK][:, j % PACK : j % PACK + tiles, :])
 
-        def turn(j, first=0, stop=PASSES):
-            bank = next_bank([P, 2, PASSES, P], late=2 if j > 1 else 0)
+        def turn(j, first=0, stop=PASSES, late=2):
+            bank = next_bank([P, 2, PASSES, P], late=late if j > 1 else 0)
             words = wide[j].bitcast(F32)
             for g in range(first, stop):
                 turned[j, g] = bank
@@ -287,12 +290,15 @@ def tile_lambdarank_head_gradient_s11_kernel(tc, d_bytes, d_scale, v, delta, ipw
 
         stacked = {}
 
-        def stack(s, first, stop, tiles=range(PACK)):
-            for col in range(first, stop, P):
-                if (s, col) not in stacked:
-                    stacked[s, col] = next_bank([P, PACK, P], late=0)
-                for t in tiles:
-                    times_d(PACK * s + t, stacked[s, col][:, t, :], e_columns(col, col + P))
+        def stack(s, first, stop):
+            for pair in range(first, stop, 2 * P):
+                columns = range(pair, min(pair + 2 * P, stop), P)
+                for col in columns:
+                    stacked[s, col] = next_bank([P, PACK, P])
+                for t in range(PACK):
+                    for g in range(PASSES):
+                        for col in columns:
+                            times_d(PACK * s + t, stacked[s, col][:, t, :], e_columns(col, col + P), (g,))
 
         def weigh(s, first, stop):
             for col in range(first, stop, P):
@@ -325,9 +331,9 @@ def tile_lambdarank_head_gradient_s11_kernel(tc, d_bytes, d_scale, v, delta, ipw
             ring.append([held[m, first][0], 0])
             nc.sync.dma_start(out=out[m * P : (m + 1) * P, first:stop], in_=res[:])
 
-        def turns(p):
-            turn(2 * p)
-            turn(2 * p + 1)
+        def turns(p, late=2):
+            turn(2 * p, late=late)
+            turn(2 * p + 1, late=late)
 
         def scales(p):
             scale(2 * p)
@@ -341,9 +347,10 @@ def tile_lambdarank_head_gradient_s11_kernel(tc, d_bytes, d_scale, v, delta, ipw
         lam = [("lam", s) for s in range(GROUPS)]
         LOW, HIGH = (0, BANK), (BANK, FEATS)
 
-        first_tile = new_wide(0, 1)
-        cast_in_order(first_tile[:, 0, :GROUP], raw[0][:, 0, :GROUP])
-        cast(on_scalar, first_tile[:, :, GROUP:], raw[0][:, 0:1, GROUP:])
+        new_wide(0, 1)
+        for g in range(PASSES):
+            for half, copy in enumerate((on_vector, on_scalar)):
+                cast_half(g, half, copy)
         widen(1, 1)
         widen(2, 1)
         warm_up(4)
@@ -445,11 +452,13 @@ def tile_lambdarank_head_gradient_s11_kernel(tc, d_bytes, d_scale, v, delta, ipw
         scores(14, 15)
         stack(2, 768, 1024)
         interleave(h[1], 0, QUARTER)
-        for job in ((h[0], *HIGH), (h[1], *HIGH), (lam[1], 0, QUARTER), (lam[1], QUARTER, RANKERS), (lam[0], 0, QUARTER), (lam[0], QUARTER, RANKERS)):
+        room(lam[2], P, QUARTER, "unit0")
+        lam_product(nc.vector, 2, P, QUARTER, 4)
+        for job in ((h[0], *HIGH), (lam[2], P, QUARTER), (h[1], *HIGH), (lam[1], 0, QUARTER), (lam[1], QUARTER, RANKERS), (lam[0], 0, QUARTER), (lam[0], QUARTER, RANKERS)):
             quant(*job)
         room(h[3], *HIGH, "tile7")
         room(h[3], *LOW, "tile9")
-        in_window(lam[2], 0, QUARTER, "tile6")
+        in_window(lam[2], 0, P, "tile6")
         in_window(lam[3], 0, WINDOW, "tile4")
         weigh(2, *HIGH)
         stack(3, *HIGH)
@@ -463,7 +472,7 @@ def tile_lambdarank_head_gradient_s11_kernel(tc, d_bytes, d_scale, v, delta, ipw
                 update(m, *HIGH, (s,))
         encode_part(0, QUARTER, 12, 13, 14, 15)
         interleave(h[3], 0, QUARTER)
-        for job in ((h[3], *HIGH), (lam[3], 0, WINDOW), (lam[2], 0, QUARTER), (h[2], *HIGH), (h[0], *LOW), (h[1], *LOW)):
+        for job in ((h[3], *HIGH), (lam[3], 0, WINDOW), (lam[2], 0, P), (h[2], *HIGH), (h[0], *LOW), (h[1], *LOW)):
             quant(*job)
         for s, first, slot in ((2, QUARTER, "unit1"), (2, WINDOW, "unit3"), (3, WINDOW, "unit2")):
             room(lam[s], first, first + P, slot)

from contextlib import ExitStack

import concourse.mybir as mybir
from concourse.masks import make_identity

F32 = mybir.dt.float32
BF16 = mybir.dt.bfloat16
I32 = mybir.dt.int32
U32 = mybir.dt.uint32
U8 = mybir.dt.uint8
FP8 = mybir.dt.float8_e4m3fn
E4M3X4 = mybir.dt.float8_e4m3fn_x4
E2M1X4 = mybir.dt.float4_e2m1fn_x4
MULT = mybir.AluOpType.mult
ADD = mybir.AluOpType.add
COPY = mybir.ActivationFunctionType.Copy
SIGMOID = mybir.ActivationFunctionType.Sigmoid

PAIRS, RAW, RANKERS, FEATS = 2048, 1024, 512, 1024
P = 128
PACK = 4
GROUP = P * PACK
GROUPS = PAIRS // GROUP
PASSES = RAW // GROUP
BANK = 512
BANKS = 8
HALVES = FEATS // BANK
TILES = PAIRS // P
STEPS = TILES // 2
QTILES = RANKERS // P
WORDS = PASSES * P
WINDOW = 384
SHARE = 320
HALF_ROWS = P // 2
QUARTER = FEATS // 4
A, B = 0, 1

FLOPS = 2 * PAIRS * RAW * RANKERS + 2 * PAIRS * RAW * FEATS + 2 * RANKERS * PAIRS * FEATS


def tile_lambdarank_head_gradient_s11_kernel(tc, d_bytes, d_scale, v, delta, ipw, e_words, e_scales, out):
    nc = tc.nc
    with ExitStack() as ctx:
        keep = ctx.enter_context(tc.tile_pool(name="keep", bufs=1))
        work = ctx.enter_context(tc.tile_pool(name="work", bufs=1))
        psum = ctx.enter_context(tc.psum_pool(name="psum", bufs=1))
        ring = [[bank, 0] for bank in range(BANKS)]

        def take_bank():
            place = 0
            while place < len(ring) and ring[place][1]:
                ring[place][1] -= 1
                place += 1
            return ring.pop(place % len(ring))[0]

        def next_bank(shape, late=0):
            bank = take_bank()
            ring.append([bank, late])
            return psum.tile(shape, F32, name=f"bank{bank}")

        ident = keep.tile([P, P], F32, name="ident")
        make_identity(nc, ident[:])

        ctx.enter_context(tc.manual_schedule())

        scale_kp = keep.tile([P, PASSES, PACK], F32, name="scale_kp")
        raw = [keep.tile([P, PACK, RAW], U8, name=f"raw{s}", align_bytes=64) for s in range(GROUPS)]
        dlt = [keep.tile([P, PACK, RANKERS], BF16, name=f"dlt{s}", align_bytes=64) for s in range(GROUPS)]
        v_raw = [keep.tile([P, PACK, RANKERS], BF16, name=f"v_raw{g}", align_bytes=64) for g in range(PASSES)]
        e_w = [keep.tile([P, PASSES, 2 * BANK], U8, name=f"e_w{half}", align_bytes=256) for half in range(HALVES)]
        e_s = keep.tile([P, PASSES, FEATS], U8, name="e_s", align_bytes=256)
        ipw_bf = keep.tile([P, GROUPS, PACK], BF16, name="ipw_bf")
        ipw_f = keep.tile([P, GROUPS, PACK], F32, name="ipw_f")

        d_view = d_bytes.rearrange("(s m t) k -> s m t k", m=P, t=PACK)
        dlt_view = delta.rearrange("(s m t) q -> s m t q", m=P, t=PACK)
        v_view = v.rearrange("(g p t) n -> g p t n", p=P, t=PACK)
        w_view = e_words.rearrange("g p n -> p g n")
        s_view = e_scales.rearrange("g r n -> r g n")

        table_in = keep.tile([P, 1], F32, name="table_in")
        table_out = keep.tile([P, 1], F32, name="table_out")
        warm = keep.tile([P, BANK], BF16, name="warm", align_bytes=64)
        nc.vector.memset(warm[:].bitcast(I32), 0)
        nc.vector.memset(table_in[:], 0.0)
        nc.vector.memset(e_s[:].bitcast(I32), 0)

        idle = next_bank([P, BANK])

        def warm_up(passes):
            for _ in range(passes):
                nc.tensor.matmul(out=idle[:], lhsT=warm[:, :P], rhs=warm[:], start=True, stop=True)

        def load_raw(s, first, stop):
            nc.sync.dma_start(out=raw[s][:, first:stop, :], in_=d_view[s][:, first:stop, :])

        def load_words(half):
            nc.sync.dma_start(out=e_w[half][:], in_=w_view[:, :, 2 * BANK * half : 2 * BANK * (half + 1)])

        def load_scales():
            for r in range(PACK):
                nc.sync.dma_start(out=e_s[r:P:32].bitcast(I32), in_=s_view[r:16:PACK].bitcast(I32))

        def load_v(g):
            nc.sync.dma_start(out=v_raw[g][:], in_=v_view[g])

        def load_delta(s):
            nc.sync.dma_start(out=dlt[s][:], in_=dlt_view[s])

        load_raw(0, 0, 1)
        nc.scalar.dma_start(out=scale_kp[:], in_=d_scale.rearrange("o (g p t) -> p (o g) t", p=P, t=PACK))
        nc.scalar.dma_start(out=ipw_bf[:], in_=ipw.rearrange("(s m t) -> m s t", m=P, t=PACK))
        nc.scalar.activation(out=table_out[:], in_=table_in[:], func=SIGMOID, scale=-1.0)
        load_raw(0, 1, 2)
        load_raw(0, 2, 4)
        load_raw(1, 0, 2)
        load_scales()
        load_words(B)
        load_v(0)
        load_words(A)
        load_raw(1, 2, 4)
        load_v(1)
        load_raw(2, 0, 4)
        load_delta(0)
        load_raw(3, 0, 4)
        for s in range(1, GROUPS):
            load_delta(s)

        on_vector, on_scalar = nc.vector.tensor_copy, nc.scalar.copy

        names = ["v"] + [(kind, s) for kind in ("h", "lam") for s in range(GROUPS)]
        width = {name: RANKERS if name[0] == "lam" else FEATS for name in names}
        codes = {name: keep.tile([P, width[name]], U32, name=f"codes{i}", align_bytes=256) for i, name in enumerate(names)}
        planes = {name: keep.tile([P, width[name]], U8, name=f"planes{i}", align_bytes=256) for i, name in enumerate(names)}
        h_raw = [keep.tile([P, PACK, FEATS if s == 0 else BANK], BF16, name=f"h_raw{s}", align_bytes=64) for s in range(GROUPS)]
        grouped = {}

        def room(name, first, stop, slot):
            grouped[name, first] = work.tile([P, stop - first, PACK], BF16, name=slot, align_bytes=64)

        def grouped_columns(name, first, stop):
            origin = max(start for (other, start) in grouped if other == name and start <= first)
            return grouped[name, origin][:, first - origin : stop - origin, :]

        def rows_of(name, first, stop):
            if name == "v":
                g = first // RANKERS
                return v_raw[g][:, :, first - g * RANKERS : stop - g * RANKERS]
            return h_raw[name[1]][:, :, first:stop]

        def interleave(name, first, stop, copy=on_scalar):
            copy(out=grouped_columns(name, first, stop).rearrange("p (c i) t -> p c t i", i=4), in_=rows_of(name, first, stop).rearrange("p t (c i) -> p c t i", i=4))

        def lam_product(engine, s, first, stop, run):
            engine.tensor_tensor(
                out=grouped_columns(("lam", s), first, stop).rearrange("p (c i) t -> p c t i", i=run),
                in0=sig[s][:, :, first:stop].rearrange("p t (c i) -> p c t i", i=run),
                in1=dlt[s][:, :, first:stop].rearrange("p t (c i) -> p c t i", i=run),
                op=MULT,
            )

        def in_window(name, first, stop, slot):
            room(name, first, stop, slot)
            by_gpsimd(name, first, stop)

        def by_gpsimd(name, first, stop):
            if name[0] == "lam":
                lam_product(nc.gpsimd, name[1], first, stop, 8)
            else:
                nc.gpsimd.tensor_scalar(out=grouped_columns(name, first, stop), in0=rows_of(name, first, stop).rearrange("p t n -> p n t"), scalar1=1.0, scalar2=0.0, op0=MULT, op1=ADD)

        def quantize(out, scales, in_):
            nc.vector.quantize_mx(out=out.bitcast(E4M3X4), scales=scales, in_=in_)

        def quant(name, first, stop):
            quantize(codes[name][:, first:stop], planes[name][:, first:stop], grouped_columns(name, first, stop).rearrange("p n t -> p (n t)"))

        d_codes = [keep.tile([P, 2 * WORDS], U32, name=f"d_codes{p}", align_bytes=256) for p in range(STEPS)]
        d_planes = [keep.tile([P, 2 * WORDS], U8, name=f"d_planes{p}", align_bytes=256) for p in range(STEPS)]
        wide, turned, d_grp = {}, {}, {}
        UNITS = 2 * PASSES

        def new_wide(j, tiles):
            both = work.tile([P, tiles, RAW], BF16, name="wide", bufs=3, align_bytes=64)
            for i in range(tiles):
                wide[j + i] = both[:, i, :]
            return both

        def cast(copy, out, in_):
            copy(out=out.rearrange("p j (g u m e) -> p (j g) u m e", u=2, m=P, e=2), in_=in_.bitcast(FP8).rearrange("p j (g m u e) -> p (j g) u m e", m=P, u=2, e=2))

        def cast_half(g, half, copy):
            rows = slice(HALF_ROWS * half, HALF_ROWS * (half + 1))
            words = wide[0][:, GROUP * g : GROUP * (g + 1)].rearrange("p (u m e) -> p m u e", u=2, e=2)[:, rows]
            copy(out=words, in_=raw[0][:, 0, GROUP * g : GROUP * (g + 1)].bitcast(FP8).rearrange("p (m u e) -> p m u e", u=2, e=2)[:, rows])

        def widen(j, tiles):
            cast(on_scalar, new_wide(j, tiles)[:], raw[j // PACK][:, j % PACK : j % PACK + tiles, :])

        def turn(j, first=0, stop=PASSES, late=2):
            bank = next_bank([P, 2, PASSES, P], late=late if j > 1 else 0)
            words = wide[j].bitcast(F32)
            for g in range(first, stop):
                turned[j, g] = bank
                for u in range(2):
                    nc.tensor.transpose(bank[:, u, g, :], words[:, P * (2 * g + u) : P * (2 * g + u + 1)], ident[:])

        def d_grouped(first, stop):
            if first < UNITS:
                if first not in d_grp:
                    d_grp[first] = work.tile([P, GROUP], BF16, name=f"unit{first}", align_bytes=64)
                return d_grp[first][:]
            origin = first - first % PASSES
            if origin not in d_grp:
                d_grp[origin] = work.tile([P, RAW], BF16, name=f"tile{origin // PASSES}", align_bytes=64)
            return d_grp[origin][:, GROUP * (first - origin) : GROUP * (stop - origin)]

        def scale(j, first=0, stop=PASSES):
            n = stop - first
            nc.vector.tensor_tensor(
                out=d_grouped(PASSES * j + first, PASSES * j + stop).rearrange("p (g r u e) -> p g r u e", g=n, u=2, e=2),
                in0=turned[j, first][:, :, first:stop, :].bitcast(BF16).rearrange("p u g (r e) -> p g r u e", e=2),
                in1=scale_kp[:, first:stop, :].rearrange("p g (o u e) -> p g o u e", o=1, e=2).to_broadcast([P, n, P, 2, 2]),
                op=MULT,
            )

        def d_quant(first, stop):
            p = first // UNITS
            cols = slice(P * (first - UNITS * p), P * (stop - UNITS * p))
            quantize(d_codes[p][:, cols], d_planes[p][:, cols], d_grouped(first, stop))

        def times_d(j, out, moving, passes=range(PASSES)):
            for g in passes:
                cols = slice(WORDS * (j % 2) + g * P, WORDS * (j % 2) + (g + 1) * P)
                rhs, rhs_scale = moving(g)
                nc.tensor.matmul_mx(
                    out=out, lhsT=d_codes[j // 2][:, cols].bitcast(E4M3X4), lhsT_scale=d_planes[j // 2][:, cols],
                    rhs=rhs, rhs_scale=rhs_scale, start=(g == 0), stop=(g == PASSES - 1),
                )

        def e_columns(first, stop):
            half, origin = first // BANK, first - first % BANK
            return lambda g: (e_w[half][:, g, 2 * (first - origin) : 2 * (stop - origin)].bitcast(E2M1X4), e_s[:, g, first:stop])

        sig, diff = {}, {}

        def score_pass(j, g):
            if g == 0:
                diff[j] = next_bank([P, RANKERS])
            cols = slice(g * RANKERS, (g + 1) * RANKERS)
            times_d(j, diff[j][:], lambda g: (codes["v"][:, cols].bitcast(E4M3X4), planes["v"][:, cols]), (g,))

        def squash(j):
            s, t = divmod(j, PACK)
            score_pass(j, PASSES - 1)
            if t == 0:
                sig[s] = work.tile([P, PACK, RANKERS], F32, name="sig", bufs=3, align_bytes=64)
            nc.scalar.activation(out=sig[s][:, t, :], in_=diff[j][:], func=SIGMOID, scale=-1.0)

        def scores(*tiles):
            for j in tiles:
                score_pass(j, 0)
                squash(j)

        encoded = {}

        def encode_product(j, half):
            encoded[j, half] = next_bank([P, BANK])
            times_d(j, encoded[j, half][:], e_columns(BANK * half, BANK * (half + 1)))

        def weigh_on_scalar(j, half):
            s, t = divmod(j, PACK)
            nc.scalar.activation(out=h_raw[s][:, t, BANK * half : BANK * (half + 1)], in_=encoded[j, half][:], func=COPY, scale=ipw_f[:, s, t : t + 1])

        def encode(half, *tiles):
            for j in tiles:
                encode_product(j, half)
                weigh_on_scalar(j, half)

        def encode_part(first, stop, *tiles):
            for j in tiles:
                s, t = divmod(j, PACK)
                part = next_bank([P, stop - first])
                times_d(j, part[:], e_columns(first, stop))
                nc.scalar.activation(out=h_raw[s][:, t, first:stop], in_=part[:], func=COPY, scale=ipw_f[:, s, t : t + 1])

        def weigh_rows(j, half):
            s, t = divmod(j, PACK)
            nc.vector.tensor_scalar(out=h_raw[s][:, t, BANK * half : BANK * (half + 1)], in0=encoded[j, half][:], scalar1=ipw_f[:, s, t : t + 1], scalar2=None, op0=MULT)

        stacked = {}

        def stack(s, first, stop):
            for pair in range(first, stop, 2 * P):
                columns = range(pair, min(pair + 2 * P, stop), P)
                for col in columns:
                    stacked[s, col] = next_bank([P, PACK, P])
                for t in range(PACK):
                    for g in range(PASSES):
                        for col in columns:
                            times_d(PACK * s + t, stacked[s, col][:, t, :], e_columns(col, col + P), (g,))

        def weigh(s, first, stop):
            for col in range(first, stop, P):
                nc.vector.tensor_tensor(
                    out=grouped_columns(("h", s), col, col + P).rearrange("p (c i) t -> p c t i", i=2),
                    in0=stacked[s, col][:].rearrange("p t (c i) -> p c t i", i=2),
                    in1=ipw_f[:, s, :].rearrange("p (c t i) -> p c t i", c=1, i=1).to_broadcast([P, P // 2, PACK, 2]),
                    op=MULT,
                )

        sums, held = {}, {}

        def update(m, first, stop, groups):
            rows = slice(m * P, (m + 1) * P)
            for s in groups:
                opening = (m, first) not in sums
                if opening:
                    held[m, first] = [take_bank(), GROUPS]
                    sums[m, first] = psum.tile([P, stop - first], F32, name=f"bank{held[m, first][0]}")
                held[m, first][1] -= 1
                nc.tensor.matmul_mx(
                    out=sums[m, first][:], lhsT=codes["lam", s][:, rows].bitcast(E4M3X4), lhsT_scale=planes["lam", s][:, rows],
                    rhs=codes["h", s][:, first:stop].bitcast(E4M3X4), rhs_scale=planes["h", s][:, first:stop],
                    start=opening, stop=(held[m, first][1] == 0),
                )

        def store(m, first, stop, copy, slot):
            res = work.tile([P, stop - first], F32, name=slot, align_bytes=64)
            copy(out=res[:], in_=sums[m, first][:])
            ring.append([held[m, first][0], 0])
            nc.sync.dma_start(out=out[m * P : (m + 1) * P, first:stop], in_=res[:])

        def turns(p, late=2):
            turn(2 * p, late=late)
            turn(2 * p + 1, late=late)

        def scales(p):
            scale(2 * p)
            scale(2 * p + 1)

        def step_quant(p):
            d_quant(UNITS * p, UNITS * p + PASSES)
            d_quant(UNITS * p + PASSES, UNITS * (p + 1))

        h = [("h", s) for s in range(GROUPS)]
        lam = [("lam", s) for s in range(GROUPS)]
        LOW, HIGH = (0, BANK), (BANK, FEATS)

        new_wide(0, 1)
        for g in range(PASSES):
            for half, copy in enumerate((on_vector, on_scalar)):
                cast_half(g, half, copy)
        widen(1, 1)
        widen(2, 1)
        warm_up(4)
        for g in range(PASSES):
            turn(0, g, g + 1)
        warm_up(1)
        widen(3, 1)
        turn(1)
        warm_up(1)
        turns(1)
        warm_up(1)
        widen(4, 2)
        nc.scalar.copy(out=ipw_f[:], in_=ipw_bf[:])
        scale(0, 0, 1)
        for unit in range(1, UNITS):
            scale(unit // PASSES, unit % PASSES, unit % PASSES + 1)
            d_quant(unit - 1, unit)
        d_quant(UNITS - 1, UNITS)
        encode(B, 0)
        encode_product(1, B)
        turns(2)
        room("v", QUARTER, RANKERS, "spare0")
        interleave("v", QUARTER, RANKERS)
        weigh_on_scalar(1, B)
        widen(6, 2)
        encode(A, 0, 1)
        in_window("v", 0, QUARTER, "unit2")
        scales(1)
        d_quant(4, 6)
        quant("v", QUARTER, RANKERS)
        quant("v", 0, QUARTER)
        d_quant(6, 8)
        room("v", RANKERS, FEATS - WINDOW, "unit0")
        interleave("v", RANKERS, FEATS - WINDOW)
        encode(B, 2)
        encode(A, 2)
        encode_product(3, B)
        turns(3)
        widen(8, 2)
        encode(A, 3)
        for j in range(PACK):
            score_pass(j, 0)
        in_window("v", FEATS - WINDOW, FEATS, "unit2")
        scales(2)
        weigh_rows(3, B)
        quant("v", RANKERS, FEATS - WINDOW)
        quant("v", FEATS - WINDOW, FEATS)
        step_quant(2)
        for j in range(PACK):
            squash(j)
        turns(4)
        widen(10, 2)
        encode(A, 4, 5)
        room(h[0], *HIGH, "tile4")
        by_gpsimd(h[0], BANK, BANK + SHARE)
        scales(3)
        step_quant(3)
        scores(4, 5)
        room(h[1], *HIGH, "spare0")
        stack(1, 512, 640)
        turns(5)
        widen(12, 2)
        scores(6, 7)
        in_window(lam[0], 0, QUARTER, "tile6")
        scales(4)
        weigh(1, 512, 640)
        step_quant(4)
        stack(1, 640, 768)
        encode(A, 6, 7)
        turns(6)
        widen(14, 2)
        scores(8, 9)
        in_window(lam[0], QUARTER, RANKERS, "tile8")
        scales(5)
        weigh(1, 640, 768)
        step_quant(5)
        stack(1, 768, 896)
        encode(A, 8, 9)
        turns(7)
        interleave(h[0], BANK + SHARE, FEATS)
        scores(10, 11)
        for s, slot in ((0, "tile2"), (1, "tile3"), (2, "tile5")):
            room(h[s], *LOW, slot)
        in_window(lam[1], 0, QUARTER, "tile10")
        scales(6)
        weigh(1, 768, 896)
        step_quant(6)
        stack(1, 896, 1024)
        interleave(h[0], 0, QUARTER)
        encode(A, 10, 11)
        scores(12, 13)
        in_window(lam[1], QUARTER, RANKERS, "tile12")
        scales(7)
        weigh(1, 896, 1024)
        step_quant(7)
        room(h[2], *HIGH, "spare1")
        stack(2, 512, 768)
        interleave(h[0], QUARTER, BANK)
        scores(14, 15)
        stack(2, 768, 1024)
        interleave(h[1], 0, QUARTER)
        room(lam[2], P, QUARTER, "unit0")
        lam_product(nc.vector, 2, P, QUARTER, 4)
        for job in ((h[0], *HIGH), (lam[2], P, QUARTER), (h[1], *HIGH), (lam[1], 0, QUARTER), (lam[1], QUARTER, RANKERS), (lam[0], 0, QUARTER), (lam[0], QUARTER, RANKERS)):
            quant(*job)
        room(h[3], *HIGH, "tile7")
        room(h[3], *LOW, "tile9")
        in_window(lam[2], 0, P, "tile6")
        in_window(lam[3], 0, WINDOW, "tile4")
        weigh(2, *HIGH)
        stack(3, *HIGH)
        interleave(h[1], QUARTER, BANK)
        interleave(h[2], *LOW)
        weigh(3, *HIGH)
        stack(3, QUARTER, BANK)
        weigh(3, QUARTER, BANK)
        for s in (0, 1):
            for m in range(QTILES):
                update(m, *HIGH, (s,))
        encode_part(0, QUARTER, 12, 13, 14, 15)
        interleave(h[3], 0, QUARTER)
        for job in ((h[3], *HIGH), (lam[3], 0, WINDOW), (lam[2], 0, P), (h[2], *HIGH), (h[0], *LOW), (h[1], *LOW)):
            quant(*job)
        for s, first, slot in ((2, QUARTER, "unit1"), (2, WINDOW, "unit3"), (3, WINDOW, "unit2")):
            room(lam[s], first, first + P, slot)
        lam_product(nc.vector, 2, QUARTER, WINDOW, 4)
        quant(h[2], *LOW)
        quant(lam[2], QUARTER, WINDOW)
        quant(h[3], *LOW)
        lam_product(nc.vector, 2, WINDOW, RANKERS, 4)
        lam_product(nc.vector, 3, WINDOW, RANKERS, 4)
        quant(lam[2], WINDOW, RANKERS)
        quant(lam[3], WINDOW, RANKERS)
        for m in range(QTILES - 1):
            update(m, *HIGH, (3,))
        for m in range(2):
            update(m, *HIGH, (2,))
            store(m, *HIGH, on_scalar, f"res{m}")
        for s in (0, 1):
            for m in range(QTILES - 1):
                update(m, *LOW, (s,))
        update(2, *HIGH, (2,))
        store(2, *HIGH, on_scalar, "res2")
        for m in range(QTILES - 1):
            update(m, *LOW, (2, 3))
            store(m, *LOW, on_scalar, f"tile{13 + m}")
        update(QTILES - 1, *HIGH, (2, 3))
        store(QTILES - 1, *HIGH, on_vector, "tile11")
        for i, piece in enumerate([(0, QUARTER), (QUARTER, QUARTER + P), (QUARTER + P, BANK)]):
            update(QTILES - 1, *piece, range(GROUPS))
            store(QTILES - 1, *piece, on_vector if i % 2 else on_scalar, f"last{i}")
